import numpy as np
import ml_dtypes


def mxq(x, axis, fmt="e4m3"):
    dtype, down = {"e4m3": (ml_dtypes.float8_e4m3fn, 7), "e5m2": (ml_dtypes.float8_e5m2, 14)}[fmt]
    v = np.moveaxis(np.asarray(x, np.float32).astype(ml_dtypes.bfloat16).astype(np.float64), axis, -1)
    blocks = v.reshape(v.shape[:-1] + (-1, 32))
    amax = np.abs(blocks).max(-1, keepdims=True)
    byte = np.maximum(np.where(amax > 0, np.frexp(amax)[1] - 1 + 127, 0) - down, 1)
    scale = np.exp2(byte - 127.0)
    codes = (blocks / scale).astype(np.float32).astype(dtype).astype(np.float64)
    return np.moveaxis((codes * scale).reshape(v.shape), -1, axis)


WIDE = False


def mx_kscale(k):
    if not WIDE:
        return np.ones(k)
    levels = np.array([10, -10, 5, -5, 0])
    if k % 512:
        return np.exp2(np.random.permutation(np.resize(levels, k // 32))).repeat(32)
    a = np.empty((k // 512, 16))
    for p in range(k // 512):
        a[p, :8] = np.random.permutation(np.resize(levels, 8))
        for g in range(8):
            far = levels[np.abs(levels - a[p, g]) >= 10]
            a[p, g + 8] = far[np.random.randint(len(far))]
    return np.exp2(a.ravel()).repeat(32)


def f64(x):
    return np.asarray(x).astype(np.float64)


def striped(idx):
    return np.tile(idx.reshape(-1, 16).T, (8, 1)).astype(np.uint16)


def unstriped(offs):
    return offs[:16].T.reshape(-1).astype(np.int64)


E2M1 = np.array([0.0, 0.5, 1.0, 1.5, 2.0, 3.0, 4.0, 6.0, -0.0, -0.5, -1.0, -1.5, -2.0, -3.0, -4.0, -6.0])


def pack_weight(w, fmt):
    k, n = w.shape
    w = f64(np.asarray(w, np.float32).astype(ml_dtypes.bfloat16)).reshape(k // 32, 32, n)
    amax = np.abs(w).max(1)
    if fmt == "e4m3":
        byte = np.frexp(amax)[1] - 1 + 127 - 7
    else:
        mant, ex = np.frexp(amax / 6.0)
        byte = np.where(mant > 0.5, ex, ex - 1) + 127
    byte = np.clip(np.where(amax > 0, byte, 1), 1, 254)
    scaled = (w * np.exp2(127.0 - byte)[:, None, :]).reshape(k, n).astype(np.float32)
    by_word = np.ascontiguousarray(scaled.reshape(k // 512, 128, 4, n).transpose(0, 1, 3, 2))
    if fmt == "e4m3":
        words = by_word.astype(ml_dtypes.float8_e4m3fn).view(np.uint8)
    else:
        c = by_word.astype(ml_dtypes.float4_e2m1fn).view(np.uint8) & 0xF
        words = (c[..., 0::2] | (c[..., 1::2] << 4)).reshape(k // 512, 128, 2 * n)
    return np.ascontiguousarray(words), np.ascontiguousarray(byte.astype(np.uint8).reshape(k // 512, 16, n))


def unpack_weight(words, scales, fmt):
    g, _, n = scales.shape
    words = np.ascontiguousarray(words).reshape(g, 128, n, -1)
    if fmt == "e4m3":
        vals = words.view(ml_dtypes.float8_e4m3fn).astype(np.float64)
    else:
        nib = np.empty((g, 128, n, 4), np.uint8)
        nib[..., 0::2] = words & 0xF
        nib[..., 1::2] = words >> 4
        vals = E2M1[nib]
    vals = vals * np.repeat(np.exp2(scales.astype(np.float64) - 127.0), 8, axis=1)[..., None]
    return vals.transpose(0, 1, 3, 2).reshape(g * 512, n)


def d_relu(v):
    return (v > 0).astype(np.float64)


K, T, E1, C1, E2, C2, H = 256, 512, 2, 256, 2, 256, 512
N = 1024


def by_expert(wq, xq, E, C):
    return np.concatenate([wq[e].T @ xq[:, e * C:(e + 1) * C] for e in range(E)], axis=1)


def setup_inputs():
    n = np.random.standard_normal
    v = mx_kscale(N)
    u = mx_kscale(H)
    slots1, slots2 = np.random.permutation(T), np.random.permutation(T)
    dy = pack_weight(n((N, T)) * v[:, None], "e4m3")
    w2t = [pack_weight(m, "e2m1") for m in n((E2, N, H)) / np.sqrt(N) / v[None, :, None] * u]
    return {
        "dy_words": dy[0],
        "dy_scales": dy[1],
        "w2t_words": np.stack([m[0] for m in w2t]),
        "w2t_scales": np.stack([m[1] for m in w2t]),
        "w1t": (n((E1, H, K)) / np.sqrt(H) / u[None, :, None]).astype(np.float32),
        "a": (n((H, T))).astype(np.float32),
        "gate1": (np.tile(np.random.uniform(0.2, 1.0, T), (128, 1))).astype(np.float32),
        "gate2": (np.tile(np.random.uniform(0.2, 1.0, T), (128, 1))).astype(np.float32),
        "offs": striped(slots1),
        "offs2": striped(slots2),
    }


def reference(dy_words, dy_scales, w2t_words, w2t_scales, w1t, a, gate1, gate2, offs, offs2):
    w2t = np.stack([unpack_weight(w2t_words[e], w2t_scales[e], "e2m1") for e in range(E2)])
    w1tq = mxq(f64(w1t), 1, "e4m3")
    idx, idx2 = unstriped(offs), unstriped(offs2)
    gq = unpack_weight(dy_words, dy_scales, "e4m3")[:, idx2]
    dc = np.zeros((H, T))
    dc[:, idx2] = f64(gate2[:1]) * by_expert(w2t, gq, E2, C2)
    da = f64(gate1[:1]) * dc[:, idx] * d_relu(f64(a))
    out = np.zeros((K, T))
    out[:, idx] = by_expert(w1tq, mxq(da, 0, "e4m3"), E1, C1)
    return out

@@ -1,0 +1,193 @@
+from contextlib import ExitStack
+
+import concourse.mybir as mybir
+from concourse.masks import make_identity
+
+K, T, H, N = 256, 512, 512, 1024
+E, C = 2, 256
+FLOPS = 2 * T * (N * H + H * K)
+
+F32 = mybir.dt.float32
+BF16 = mybir.dt.bfloat16
+I32 = mybir.dt.int32
+U32 = mybir.dt.uint32
+U16 = mybir.dt.uint16
+U8 = mybir.dt.uint8
+FP8X4 = mybir.dt.float8_e4m3fn_x4
+FP4X4 = mybir.dt.float4_e2m1fn_x4
+ALU = mybir.AluOpType
+ACT = mybir.ActivationFunctionType
+
+P = 128
+PACK = 4
+PASSES = N // (P * PACK)
+LANES = 16
+
+
+def tile_moe_seb_relu_kernel(tc, dy_words, dy_scales, w2t_words, w2t_scales, w1t, a, gate1, gate2, offs, offs2, out):
+    nc = tc.nc
+
+    def entries(tile, lo, hi):
+        return tile[:, lo // LANES : hi // LANES]
+
+    with ExitStack() as ctx:
+        keep = ctx.enter_context(tc.tile_pool(name="keep", bufs=1))
+        ring = ctx.enter_context(tc.tile_pool(name="ring", bufs=2))
+        mm_psum = ctx.enter_context(tc.psum_pool(name="mm_psum", bufs=3))
+        tr_psum = ctx.enter_context(tc.psum_pool(name="tr_psum", bufs=3))
+        out_psum = ctx.enter_context(tc.psum_pool(name="out_psum", bufs=2))
+
+        list2 = keep.tile([P, T // LANES], U16, name="list2")
+        list1 = keep.tile([P, T // LANES], U16, name="list1")
+        dy_w = keep.tile([P, PASSES, T], I32, name="dy_w", align_bytes=64)
+        dy_s = keep.tile([P, PASSES, T], U8, name="dy_s", align_bytes=64)
+        w2_w = keep.tile([P, E, PASSES, 2 * H], U8, name="w2_w", align_bytes=64)
+        w2_s = keep.tile([P, E * PASSES, H], U8, name="w2_s", align_bytes=64)
+        q_col = keep.tile([P, T // P], F32, name="q_col")
+        ident = keep.tile([P, P], F32, name="ident")
+        a_sb = keep.tile([P, PACK, T], F32, name="a_sb")
+        g1 = keep.tile([P, T], F32, name="g1")
+        w1_raw = keep.tile([P, E, PACK, K], F32, name="w1_raw")
+
+        nc.vector.memset(dy_s[:].bitcast(I32), 0)
+        nc.vector.memset(w2_s[:].bitcast(I32), 0)
+
+        nc.sync.dma_start(list2[:], offs2)
+        nc.sync.dma_start(dy_w[:], dy_words.rearrange("s p t d -> p s (t d)").bitcast(I32))
+        for quad in range(4):
+            nc.sync.dma_start(
+                dy_s[32 * quad : 32 * quad + 4, :, :].bitcast(I32),
+                dy_scales[:, 4 * quad : 4 * quad + 4, :].rearrange("s b t -> b s t").bitcast(I32),
+            )
+        nc.sync.dma_start(w2_w[:, 0, :, :].bitcast(I32), w2t_words[0].rearrange("s p n -> p s n").bitcast(I32))
+        for quad in range(4):
+            nc.sync.dma_start(
+                w2_s[32 * quad : 32 * quad + 4, :, :].bitcast(I32),
+                w2t_scales[:, :, 4 * quad : 4 * quad + 4, :].rearrange("f s b i -> b (f s) i").bitcast(I32),
+            )
+        with nc.allow_non_contiguous_dma(reason="one gate value a partition"):
+            nc.gpsimd.dma_start(q_col[:], gate2[0, :].rearrange("(c p) -> p c", p=P))
+        make_identity(nc, ident[:])
+        nc.sync.dma_start(w2_w[:, 1, :, :].bitcast(I32), w2t_words[1].rearrange("s p n -> p s n").bitcast(I32))
+        nc.sync.dma_start(g1[:], gate1)
+        a_rows = a.rearrange("(p t) j -> p t j", t=PACK)
+        nc.sync.dma_start(a_sb[:, 0:2, :], a_rows[:, 0:2, :])
+        nc.sync.dma_start(a_sb[:, 2:4, :], a_rows[:, 2:4, :])
+        for e in range(E):
+            nc.sync.dma_start(w1_raw[:, e, :, :], w1t[e].rearrange("(p t) k -> p t k", t=PACK))
+        nc.sync.dma_start(list1[:], offs)
+
+        slot_w = [keep.tile([P, T], U32, name="slot_w%d" % s, align_bytes=64) for s in range(PASSES)]
+        slot_s = [keep.tile([P, T], U8, name="slot_s%d" % s, align_bytes=64) for s in range(PASSES)]
+        dc = [keep.tile([P, T], F32, name="dc%d" % t) for t in range(PACK)]
+        dc_slots = keep.tile([P, E, PACK, C], F32, name="dc_slots")
+
+        def gather_dy(lo, hi):
+            for s in range(PASSES):
+                nc.vector.tensor_copy(slot_w[s][:, lo:hi], dy_w[:, s, :].bitcast(U32).indirect(entries(list2, lo, hi)))
+            for s in range(PASSES):
+                nc.vector.tensor_copy(slot_s[s][:, lo:hi], dy_s[:, s, :].indirect(entries(list2, lo, hi)))
+
+        def second_layer(c):
+            f, half = divmod(c, C // P)
+            cols = slice(c * P, (c + 1) * P)
+            acc = mm_psum.tile([P, H], F32, name="acc")
+            for s in range(PASSES):
+                nc.tensor.matmul_mx(
+                    out=acc[:],
+                    lhsT=slot_w[s][:, cols].bitcast(FP8X4),
+                    lhsT_scale=slot_s[s][:, cols],
+                    rhs=w2_w[:, f, s, :].bitcast(FP4X4),
+                    rhs_scale=w2_s[:, PASSES * f + s, :],
+                    start=(s == 0),
+                    stop=(s == PASSES - 1),
+                )
+            gated = ring.tile([P, PACK, P], F32, name="gated")
+            nc.scalar.activation(gated[:], acc[:].rearrange("p (m t) -> p t m", t=PACK), ACT.Copy, scale=q_col[:, c : c + 1])
+            turned = tr_psum.tile([P, PACK, P], F32, name="turned")
+            for t in range(PACK):
+                nc.tensor.transpose(turned[:, t, :], gated[:, t, :], ident[:])
+            nc.scalar.copy(dc_slots[:, f, :, half * P : (half + 1) * P], turned[:])
+
+        def scatter_dc(lo, hi):
+            f = lo // C
+            for t in range(PACK):
+                nc.vector.tensor_copy(dc[t][:].indirect(entries(list2, lo, hi)), dc_slots[:, f, t, lo - f * C : hi - f * C])
+
+        gather_dy(0, 128)
+        second_layer(0)
+        gather_dy(128, 256)
+        second_layer(1)
+        gather_dy(256, 512)
+        second_layer(2)
+        second_layer(3)
+        scatter_dc(0, 128)
+        scatter_dc(128, 256)
+        scatter_dc(256, 512)
+
+        slope = keep.tile([P, PACK, T], F32, name="slope")
+        for t in range(PACK):
+            nc.vector.scalar_tensor_tensor(slope[:, t, :], a_sb[:, t, :], 0.0, g1[:], ALU.is_gt, ALU.mult)
+
+        w1_bf = keep.tile([P, E, K, PACK], BF16, name="w1_bf", align_bytes=64)
+        w1_w = keep.tile([P, E, K], U32, name="w1_w", align_bytes=64)
+        w1_s = keep.tile([P, E, K], U8, name="w1_s", align_bytes=64)
+        for e in range(E):
+            nc.scalar.copy(w1_bf[:, e, :, :], w1_raw[:, e, :, :].rearrange("p t k -> p k t"))
+
+        def quantize_w1(e):
+            nc.vector.quantize_mx(out=w1_w[:, e, :].bitcast(FP8X4), scales=w1_s[:, e, :], in_=w1_bf[:, e, :, :].rearrange("p k t -> p (k t)"))
+
+        da = keep.tile([P, E, PACK, C], F32, name="da")
+        da_bf = keep.tile([P, E, C, PACK], BF16, name="da_bf", align_bytes=64)
+        da_w = keep.tile([P, E, C], U32, name="da_w", align_bytes=64)
+        da_s = keep.tile([P, E, C], U8, name="da_s", align_bytes=64)
+        dx_slots = keep.tile([P, E, K // P, C], F32, name="dx_slots")
+        dx = [keep.tile([P, T], F32, name="dx%d" % kt) for kt in range(K // P)]
+
+        def gather_dc(e, t):
+            nc.vector.tensor_tensor(da[:, e, t, :], dc[t][:].indirect(entries(list1, e * C, (e + 1) * C)), slope[:, t, e * C : (e + 1) * C], ALU.mult)
+
+        def round_da(e):
+            nc.scalar.copy(da_bf[:, e, :, :], da[:, e, :, :].rearrange("p t j -> p j t"))
+
+        def quantize_da(e):
+            nc.vector.quantize_mx(out=da_w[:, e, :].bitcast(FP8X4), scales=da_s[:, e, :], in_=da_bf[:, e, :, :].rearrange("p j t -> p (j t)"))
+
+        def first_layer(e, kt):
+            cols = slice(kt * P, (kt + 1) * P)
+            acc1 = out_psum.tile([P, C], F32, name="acc1")
+            nc.tensor.matmul_mx(
+                out=acc1[:],
+                lhsT=w1_w[:, e, cols].bitcast(FP8X4),
+                lhsT_scale=w1_s[:, e, cols],
+                rhs=da_w[:, e, :].bitcast(FP8X4),
+                rhs_scale=da_s[:, e, :],
+                start=True,
+                stop=True,
+            )
+            nc.scalar.copy(dx_slots[:, e, kt, :], acc1[:])
+
+        def scatter_dx(e, kt):
+            nc.vector.tensor_copy(dx[kt][:].indirect(entries(list1, e * C, (e + 1) * C)), dx_slots[:, e, kt, :])
+
+        quantize_w1(0)
+        for t in range(PACK):
+            gather_dc(0, t)
+        round_da(0)
+        for t in range(PACK - 1):
+            gather_dc(1, t)
+        quantize_da(0)
+        gather_dc(1, PACK - 1)
+        quantize_w1(1)
+        first_layer(0, 0)
+        round_da(1)
+        first_layer(0, 1)
+        scatter_dx(0, 0)
+        quantize_da(1)
+        first_layer(1, 0)
+        first_layer(1, 1)
+        scatter_dx(0, 1)
+        for kt in range(K // P):
+            scatter_dx(1, kt)
+            nc.sync.dma_start(out[kt * P : (kt + 1) * P, :], dx[kt][:])

@@ -32,9 +32,11 @@ def tile_moe_seb_relu_kernel(tc, dy_words, dy_scales, w2t_words, w2t_scales, w1t
 
     with ExitStack() as ctx:
         keep = ctx.enter_context(tc.tile_pool(name="keep", bufs=1))
-        ring = ctx.enter_context(tc.tile_pool(name="ring", bufs=2))
-        mm_psum = ctx.enter_context(tc.psum_pool(name="mm_psum", bufs=3))
+        ring = ctx.enter_context(tc.tile_pool(name="ring", bufs=3))
+        once = ctx.enter_context(tc.tile_pool(name="once", bufs=1))
+        mm_psum = ctx.enter_context(tc.psum_pool(name="mm_psum", bufs=1))
         tr_psum = ctx.enter_context(tc.psum_pool(name="tr_psum", bufs=3))
+        late_psum = ctx.enter_context(tc.psum_pool(name="late_psum", bufs=1))
         out_psum = ctx.enter_context(tc.psum_pool(name="out_psum", bufs=2))
 
         list2 = keep.tile([P, T // LANES], U16, name="list2")
@@ -49,25 +51,30 @@ def tile_moe_seb_relu_kernel(tc, dy_words, dy_scales, w2t_words, w2t_scales, w1t
         g1 = keep.tile([P, T], F32, name="g1")
         w1_raw = keep.tile([P, E, PACK, K], F32, name="w1_raw")
 
-        nc.vector.memset(dy_s[:].bitcast(I32), 0)
+        nc.gpsimd.memset(dy_s[:].bitcast(I32), 0)
         nc.vector.memset(w2_s[:].bitcast(I32), 0)
 
         nc.sync.dma_start(list2[:], offs2)
-        nc.sync.dma_start(dy_w[:], dy_words.rearrange("s p t d -> p s (t d)").bitcast(I32))
+        dy_rows = dy_words.rearrange("s p t d -> p s (t d)").bitcast(I32)
+        nc.sync.dma_start(dy_w[:, 0, :], dy_rows[:, 0, :])
         for quad in range(4):
             nc.sync.dma_start(
                 dy_s[32 * quad : 32 * quad + 4, :, :].bitcast(I32),
                 dy_scales[:, 4 * quad : 4 * quad + 4, :].rearrange("s b t -> b s t").bitcast(I32),
             )
+        nc.sync.dma_start(dy_w[:, 1, :], dy_rows[:, 1, :])
         nc.sync.dma_start(w2_w[:, 0, :, :].bitcast(I32), w2t_words[0].rearrange("s p n -> p s n").bitcast(I32))
         for quad in range(4):
             nc.sync.dma_start(
                 w2_s[32 * quad : 32 * quad + 4, :, :].bitcast(I32),
                 w2t_scales[:, :, 4 * quad : 4 * quad + 4, :].rearrange("f s b i -> b (f s) i").bitcast(I32),
             )
-        with nc.allow_non_contiguous_dma(reason="one gate value a partition"):
-            nc.gpsimd.dma_start(q_col[:], gate2[0, :].rearrange("(c p) -> p c", p=P))
+        q_rows = keep.tile([P, P], F32, name="q_rows")
+        nc.gpsimd.dma_start(q_rows[:], gate2[0 : P * P // T, :].rearrange("r (c m) -> (r c) m", m=P))
         make_identity(nc, ident[:])
+        q_turned = tr_psum.tile([P, P], F32, name="q_turned", tag="turned")
+        nc.tensor.transpose(q_turned[:], q_rows[:], ident[:])
+        nc.scalar.activation(q_col[:], q_turned[:, 0 : T // P], ACT.Copy)
         nc.sync.dma_start(w2_w[:, 1, :, :].bitcast(I32), w2t_words[1].rearrange("s p n -> p s n").bitcast(I32))
         nc.sync.dma_start(g1[:], gate1)
         a_rows = a.rearrange("(p t) j -> p t j", t=PACK)
@@ -79,19 +86,22 @@ def tile_moe_seb_relu_kernel(tc, dy_words, dy_scales, w2t_words, w2t_scales, w1t
 
         slot_w = [keep.tile([P, T], U32, name="slot_w%d" % s, align_bytes=64) for s in range(PASSES)]
         slot_s = [keep.tile([P, T], U8, name="slot_s%d" % s, align_bytes=64) for s in range(PASSES)]
-        dc = [keep.tile([P, T], F32, name="dc%d" % t) for t in range(PACK)]
+        dc = [keep.tile([P, T], F32, name="dc%d" % t, tag="dc%d" % t, align_bytes=64) for t in range(PACK)]
         dc_slots = keep.tile([P, E, PACK, C], F32, name="dc_slots")
 
-        def gather_dy(lo, hi):
-            for s in range(PASSES):
-                nc.vector.tensor_copy(slot_w[s][:, lo:hi], dy_w[:, s, :].bitcast(U32).indirect(entries(list2, lo, hi)))
-            for s in range(PASSES):
-                nc.vector.tensor_copy(slot_s[s][:, lo:hi], dy_s[:, s, :].indirect(entries(list2, lo, hi)))
+        def gather_words(s, lo, hi):
+            nc.vector.tensor_copy(slot_w[s][:, lo:hi], dy_w[:, s, :].bitcast(U32).indirect(entries(list2, lo, hi)))
 
-        def second_layer(c):
+        def gather_scales(s, lo, hi):
+            nc.vector.tensor_copy(slot_s[s][:, lo:hi], dy_s[:, s, :].indirect(entries(list2, lo, hi)))
+
+        def second_layer(c, plane_runs):
             f, half = divmod(c, C // P)
             cols = slice(c * P, (c + 1) * P)
-            acc = mm_psum.tile([P, H], F32, name="acc")
+            if c == 3:
+                acc = late_psum.tile([P, H], F32, name="acc", tag="late")
+            else:
+                acc = mm_psum.tile([P, H], F32, name="acc")
             for s in range(PASSES):
                 nc.tensor.matmul_mx(
                     out=acc[:],
@@ -102,57 +112,85 @@ def tile_moe_seb_relu_kernel(tc, dy_words, dy_scales, w2t_words, w2t_scales, w1t
                     start=(s == 0),
                     stop=(s == PASSES - 1),
                 )
-            gated = ring.tile([P, PACK, P], F32, name="gated")
-            nc.scalar.activation(gated[:], acc[:].rearrange("p (m t) -> p t m", t=PACK), ACT.Copy, scale=q_col[:, c : c + 1])
-            turned = tr_psum.tile([P, PACK, P], F32, name="turned")
-            for t in range(PACK):
-                nc.tensor.transpose(turned[:, t, :], gated[:, t, :], ident[:])
-            nc.scalar.copy(dc_slots[:, f, :, half * P : (half + 1) * P], turned[:])
+            pool = once if c == 3 else ring
+            gated = pool.tile([P, PACK, P], F32, name="gated", tag="stage", align_bytes=64)
+            by_plane = acc[:].rearrange("p (m t) -> p t m", t=PACK)
+            for t0, t1 in plane_runs:
+                nc.scalar.activation(gated[:, t0:t1, :], by_plane[:, t0:t1, :], ACT.Copy, scale=q_col[:, c : c + 1])
+            for t0, t1 in plane_runs:
+                if c == 1 and t1 == PACK:
+                    turned = late_psum.tile([P, t1 - t0, P], F32, name="turned", tag="late")
+                else:
+                    turned = tr_psum.tile([P, t1 - t0, P], F32, name="turned", tag="turned")
+                for t in range(t0, t1):
+                    nc.tensor.transpose(turned[:, t - t0, :], gated[:, t, :], ident[:])
+                nc.scalar.copy(dc_slots[:, f, t0:t1, half * P : (half + 1) * P], turned[:])
 
         def scatter_dc(lo, hi):
             f = lo // C
             for t in range(PACK):
                 nc.vector.tensor_copy(dc[t][:].indirect(entries(list2, lo, hi)), dc_slots[:, f, t, lo - f * C : hi - f * C])
 
-        gather_dy(0, 128)
-        second_layer(0)
-        gather_dy(128, 256)
-        second_layer(1)
-        gather_dy(256, 512)
-        second_layer(2)
-        second_layer(3)
+        gather_words(0, 0, 256)
+        gather_scales(0, 0, 128)
+        gather_scales(1, 0, 128)
+        gather_words(1, 0, 128)
+        second_layer(0, [(0, 1), (1, PACK)])
+        gather_words(1, 128, 256)
+        gather_scales(0, 128, 512)
+        gather_scales(1, 128, 512)
+        second_layer(1, [(0, 1), (1, PACK)])
+        gather_words(0, 256, 512)
+        gather_words(1, 256, 512)
+        second_layer(2, [(0, PACK)])
+        second_layer(3, [(0, PACK)])
         scatter_dc(0, 128)
         scatter_dc(128, 256)
-        scatter_dc(256, 512)
+        scatter_dc(256, 384)
+        scatter_dc(384, 512)
 
         slope = keep.tile([P, PACK, T], F32, name="slope")
-        for t in range(PACK):
-            nc.vector.scalar_tensor_tensor(slope[:, t, :], a_sb[:, t, :], 0.0, g1[:], ALU.is_gt, ALU.mult)
+        mask = keep.tile([P, PACK, T], F32, name="mask")
+        for e in range(E):
+            slots = slice(e * C, (e + 1) * C)
+            if e == 0:
+                nc.gpsimd.tensor_scalar(mask[:, :, slots], a_sb[:, :, slots], 0.0, 0.0, ALU.is_gt, ALU.add)
+            else:
+                positive = once.tile([P, PACK, C], F32, name="positive", tag="stage", align_bytes=64)
+                nc.scalar.activation(positive[:], a_sb[:, :, slots], ACT.Relu)
+                nc.scalar.activation(mask[:, :, slots], positive[:], ACT.Sign)
+            nc.gpsimd.tensor_tensor(slope[:, :, slots], mask[:, :, slots], g1[:, slots].unsqueeze(1).to_broadcast([P, PACK, C]), ALU.mult)
 
-        w1_bf = keep.tile([P, E, K, PACK], BF16, name="w1_bf", align_bytes=64)
-        w1_w = keep.tile([P, E, K], U32, name="w1_w", align_bytes=64)
+        w1_bf = once.tile([P, E, K, PACK], BF16, name="w1_bf", tag="stage", align_bytes=64)
         w1_s = keep.tile([P, E, K], U8, name="w1_s", align_bytes=64)
         for e in range(E):
             nc.scalar.copy(w1_bf[:, e, :, :], w1_raw[:, e, :, :].rearrange("p t k -> p k t"))
 
-        def quantize_w1(e):
-            nc.vector.quantize_mx(out=w1_w[:, e, :].bitcast(FP8X4), scales=w1_s[:, e, :], in_=w1_bf[:, e, :, :].rearrange("p k t -> p (k t)"))
 
-        da = keep.tile([P, E, PACK, C], F32, name="da")
-        da_bf = keep.tile([P, E, C, PACK], BF16, name="da_bf", align_bytes=64)
-        da_w = keep.tile([P, E, C], U32, name="da_w", align_bytes=64)
+        da = keep.tile([P, E, PACK, C], F32, name="da", align_bytes=64)
+        da_bf = [
+            da[:, 1, 2:PACK, :].rearrange("p t j -> p (t j)").bitcast(BF16),
+            None,
+        ]
+        da_w = [
+            keep.tile([P, C], U32, name="da_w0", tag="handed", align_bytes=64),
+            keep.tile([P, C], U32, name="da_w1", align_bytes=64),
+        ]
         da_s = keep.tile([P, E, C], U8, name="da_s", align_bytes=64)
         dx_slots = keep.tile([P, E, K // P, C], F32, name="dx_slots")
-        dx = [keep.tile([P, T], F32, name="dx%d" % kt) for kt in range(K // P)]
+        dx = [keep.tile([P, T], F32, name="dx0"), None]
 
         def gather_dc(e, t):
             nc.vector.tensor_tensor(da[:, e, t, :], dc[t][:].indirect(entries(list1, e * C, (e + 1) * C)), slope[:, t, e * C : (e + 1) * C], ALU.mult)
 
         def round_da(e):
-            nc.scalar.copy(da_bf[:, e, :, :], da[:, e, :, :].rearrange("p t j -> p j t"))
+            if e == 1:
+                da_bf1 = keep.tile([P, C * PACK], BF16, name="da_bf1", tag="handed", align_bytes=64)
+                da_bf[1] = da_bf1[:]
+            nc.scalar.copy(da_bf[e].rearrange("p (j t) -> p j t", t=PACK), da[:, e, :, :].rearrange("p t j -> p j t"))
 
         def quantize_da(e):
-            nc.vector.quantize_mx(out=da_w[:, e, :].bitcast(FP8X4), scales=da_s[:, e, :], in_=da_bf[:, e, :, :].rearrange("p j t -> p (j t)"))
+            nc.vector.quantize_mx(out=da_w[e][:].bitcast(FP8X4), scales=da_s[:, e, :], in_=da_bf[e])
 
         def first_layer(e, kt):
             cols = slice(kt * P, (kt + 1) * P)
@@ -161,7 +199,7 @@ def tile_moe_seb_relu_kernel(tc, dy_words, dy_scales, w2t_words, w2t_scales, w1t
                 out=acc1[:],
                 lhsT=w1_w[:, e, cols].bitcast(FP8X4),
                 lhsT_scale=w1_s[:, e, cols],
-                rhs=da_w[:, e, :].bitcast(FP8X4),
+                rhs=da_w[e][:].bitcast(FP8X4),
                 rhs_scale=da_s[:, e, :],
                 start=True,
                 stop=True,
@@ -171,22 +209,28 @@ def tile_moe_seb_relu_kernel(tc, dy_words, dy_scales, w2t_words, w2t_scales, w1t
         def scatter_dx(e, kt):
             nc.vector.tensor_copy(dx[kt][:].indirect(entries(list1, e * C, (e + 1) * C)), dx_slots[:, e, kt, :])
 
-        quantize_w1(0)
         for t in range(PACK):
             gather_dc(0, t)
         round_da(0)
-        for t in range(PACK - 1):
-            gather_dc(1, t)
+        gather_dc(1, 0)
+        gather_dc(1, 1)
+        w1_w = keep.tile([P, E, K], U32, name="w1_w", tag="dc0", align_bytes=64)
+        nc.vector.quantize_mx(
+            out=w1_w[:].rearrange("p e k -> p (e k)").bitcast(FP8X4),
+            scales=w1_s[:].rearrange("p e k -> p (e k)"),
+            in_=w1_bf[:].rearrange("p e k t -> p (e k t)"),
+        )
         quantize_da(0)
-        gather_dc(1, PACK - 1)
-        quantize_w1(1)
+        gather_dc(1, 2)
+        gather_dc(1, 3)
         first_layer(0, 0)
-        round_da(1)
         first_layer(0, 1)
+        round_da(1)
         scatter_dx(0, 0)
         quantize_da(1)
         first_layer(1, 0)
         first_layer(1, 1)
+        dx[1] = keep.tile([P, T], F32, name="dx1", tag="handed", align_bytes=64)
         scatter_dx(0, 1)
         for kt in range(K // P):
             scatter_dx(1, kt)

@@ -35,8 +35,7 @@ def tile_moe_seb_relu_kernel(tc, dy_words, dy_scales, w2t_words, w2t_scales, w1t
         ring = ctx.enter_context(tc.tile_pool(name="ring", bufs=3))
         once = ctx.enter_context(tc.tile_pool(name="once", bufs=1))
         mm_psum = ctx.enter_context(tc.psum_pool(name="mm_psum", bufs=1))
-        tr_psum = ctx.enter_context(tc.psum_pool(name="tr_psum", bufs=3))
-        late_psum = ctx.enter_context(tc.psum_pool(name="late_psum", bufs=1))
+        tr_psum = ctx.enter_context(tc.psum_pool(name="tr_psum", bufs=4))
         out_psum = ctx.enter_context(tc.psum_pool(name="out_psum", bufs=2))
 
         list2 = keep.tile([P, T // LANES], U16, name="list2")
@@ -49,14 +48,14 @@ def tile_moe_seb_relu_kernel(tc, dy_words, dy_scales, w2t_words, w2t_scales, w1t
         ident = keep.tile([P, P], F32, name="ident")
         a_sb = keep.tile([P, PACK, T], F32, name="a_sb")
         g1 = keep.tile([P, T], F32, name="g1")
-        w1_raw = keep.tile([P, E, PACK, K], F32, name="w1_raw")
+        w1_raw = keep.tile([P, E, PACK, K], F32, name="w1_raw", tag="rows", align_bytes=64)
 
         nc.gpsimd.memset(dy_s[:].bitcast(I32), 0)
         nc.vector.memset(w2_s[:].bitcast(I32), 0)
 
-        nc.sync.dma_start(list2[:], offs2)
         dy_rows = dy_words.rearrange("s p t d -> p s (t d)").bitcast(I32)
         nc.sync.dma_start(dy_w[:, 0, :], dy_rows[:, 0, :])
+        nc.sync.dma_start(list2[:], offs2)
         for quad in range(4):
             nc.sync.dma_start(
                 dy_s[32 * quad : 32 * quad + 4, :, :].bitcast(I32),
@@ -98,10 +97,7 @@ def tile_moe_seb_relu_kernel(tc, dy_words, dy_scales, w2t_words, w2t_scales, w1t
         def second_layer(c, plane_runs):
             f, half = divmod(c, C // P)
             cols = slice(c * P, (c + 1) * P)
-            if c == 3:
-                acc = late_psum.tile([P, H], F32, name="acc", tag="late")
-            else:
-                acc = mm_psum.tile([P, H], F32, name="acc")
+            acc = mm_psum.tile([P, H], F32, name="acc")
             for s in range(PASSES):
                 nc.tensor.matmul_mx(
                     out=acc[:],
@@ -118,10 +114,7 @@ def tile_moe_seb_relu_kernel(tc, dy_words, dy_scales, w2t_words, w2t_scales, w1t
             for t0, t1 in plane_runs:
                 nc.scalar.activation(gated[:, t0:t1, :], by_plane[:, t0:t1, :], ACT.Copy, scale=q_col[:, c : c + 1])
             for t0, t1 in plane_runs:
-                if c == 1 and t1 == PACK:
-                    turned = late_psum.tile([P, t1 - t0, P], F32, name="turned", tag="late")
-                else:
-                    turned = tr_psum.tile([P, t1 - t0, P], F32, name="turned", tag="turned")
+                turned = tr_psum.tile([P, t1 - t0, P], F32, name="turned", tag="turned")
                 for t in range(t0, t1):
                     nc.tensor.transpose(turned[:, t - t0, :], gated[:, t, :], ident[:])
                 nc.scalar.copy(dc_slots[:, f, t0:t1, half * P : (half + 1) * P], turned[:])
@@ -131,18 +124,17 @@ def tile_moe_seb_relu_kernel(tc, dy_words, dy_scales, w2t_words, w2t_scales, w1t
             for t in range(PACK):
                 nc.vector.tensor_copy(dc[t][:].indirect(entries(list2, lo, hi)), dc_slots[:, f, t, lo - f * C : hi - f * C])
 
-        gather_words(0, 0, 256)
+        gather_words(0, 0, 128)
+        gather_words(0, 128, 512)
+        gather_words(1, 0, 128)
         gather_scales(0, 0, 128)
         gather_scales(1, 0, 128)
-        gather_words(1, 0, 128)
         second_layer(0, [(0, 1), (1, PACK)])
-        gather_words(1, 128, 256)
+        gather_words(1, 128, 512)
         gather_scales(0, 128, 512)
         gather_scales(1, 128, 512)
         second_layer(1, [(0, 1), (1, PACK)])
-        gather_words(0, 256, 512)
-        gather_words(1, 256, 512)
-        second_layer(2, [(0, PACK)])
+        second_layer(2, [(0, 1), (1, PACK)])
         second_layer(3, [(0, PACK)])
         scatter_dc(0, 128)
         scatter_dc(128, 256)
@@ -167,9 +159,12 @@ def tile_moe_seb_relu_kernel(tc, dy_words, dy_scales, w2t_words, w2t_scales, w1t
             nc.scalar.copy(w1_bf[:, e, :, :], w1_raw[:, e, :, :].rearrange("p t k -> p k t"))
 
 
-        da = keep.tile([P, E, PACK, C], F32, name="da", align_bytes=64)
+        da = [
+            keep.tile([P, PACK, C], F32, name="da0", align_bytes=64),
+            keep.tile([P, PACK, C], F32, name="da1", tag="rows", align_bytes=64),
+        ]
         da_bf = [
-            da[:, 1, 2:PACK, :].rearrange("p t j -> p (t j)").bitcast(BF16),
+            da[1][:, 2:PACK, :].rearrange("p t j -> p (t j)").bitcast(BF16),
             None,
         ]
         da_w = [
@@ -181,13 +176,13 @@ def tile_moe_seb_relu_kernel(tc, dy_words, dy_scales, w2t_words, w2t_scales, w1t
         dx = [keep.tile([P, T], F32, name="dx0"), None]
 
         def gather_dc(e, t):
-            nc.vector.tensor_tensor(da[:, e, t, :], dc[t][:].indirect(entries(list1, e * C, (e + 1) * C)), slope[:, t, e * C : (e + 1) * C], ALU.mult)
+            nc.vector.tensor_tensor(da[e][:, t, :], dc[t][:].indirect(entries(list1, e * C, (e + 1) * C)), slope[:, t, e * C : (e + 1) * C], ALU.mult)
 
         def round_da(e):
             if e == 1:
                 da_bf1 = keep.tile([P, C * PACK], BF16, name="da_bf1", tag="handed", align_bytes=64)
                 da_bf[1] = da_bf1[:]
-            nc.scalar.copy(da_bf[e].rearrange("p (j t) -> p j t", t=PACK), da[:, e, :, :].rearrange("p t j -> p j t"))
+            nc.scalar.copy(da_bf[e].rearrange("p (j t) -> p j t", t=PACK), da[e][:].rearrange("p t j -> p j t"))
 
         def quantize_da(e):
             nc.vector.quantize_mx(out=da_w[e][:].bitcast(FP8X4), scales=da_s[:, e, :], in_=da_bf[e])

@@ -68,12 +68,11 @@ def tile_moe_seb_relu_kernel(tc, dy_words, dy_scales, w2t_words, w2t_scales, w1t
                 w2_s[32 * quad : 32 * quad + 4, :, :].bitcast(I32),
                 w2t_scales[:, :, 4 * quad : 4 * quad + 4, :].rearrange("f s b i -> b (f s) i").bitcast(I32),
             )
-        q_rows = keep.tile([P, P], F32, name="q_rows")
-        nc.gpsimd.dma_start(q_rows[:], gate2[0 : P * P // T, :].rearrange("r (c m) -> (r c) m", m=P))
-        make_identity(nc, ident[:])
-        q_turned = tr_psum.tile([P, P], F32, name="q_turned", tag="turned")
-        nc.tensor.transpose(q_turned[:], q_rows[:], ident[:])
-        nc.scalar.activation(q_col[:], q_turned[:, 0 : T // P], ACT.Copy)
+        with nc.allow_non_contiguous_dma(reason="one value of gate2 a partition"):
+            nc.sync.dma_start(q_col[:], gate2[0, :].rearrange("(c p) -> p c", p=P))
+        ident_made = keep.tile([P, P], F32, name="ident_made")
+        make_identity(nc, ident_made[:])
+        nc.scalar.activation(ident[:], ident_made[:], ACT.Copy)
         nc.sync.dma_start(w2_w[:, 1, :, :].bitcast(I32), w2t_words[1].rearrange("s p n -> p s n").bitcast(I32))
         nc.sync.dma_start(g1[:], gate1)
         a_rows = a.rearrange("(p t) j -> p t j", t=PACK)
@@ -145,12 +144,12 @@ def tile_moe_seb_relu_kernel(tc, dy_words, dy_scales, w2t_words, w2t_scales, w1t
         mask = keep.tile([P, PACK, T], F32, name="mask")
         for e in range(E):
             slots = slice(e * C, (e + 1) * C)
-            if e == 0:
-                nc.gpsimd.tensor_scalar(mask[:, :, slots], a_sb[:, :, slots], 0.0, 0.0, ALU.is_gt, ALU.add)
-            else:
-                positive = once.tile([P, PACK, C], F32, name="positive", tag="stage", align_bytes=64)
-                nc.scalar.activation(positive[:], a_sb[:, :, slots], ACT.Relu)
-                nc.scalar.activation(mask[:, :, slots], positive[:], ACT.Sign)
+            split = PACK if e == 0 else 2
+            nc.gpsimd.tensor_scalar(mask[:, :split, slots], a_sb[:, :split, slots], 0.0, 0.0, ALU.is_gt, ALU.add)
+            if split < PACK:
+                positive = once.tile([P, PACK - split, C], F32, name="positive", tag="stage", align_bytes=64)
+                nc.scalar.activation(positive[:], a_sb[:, split:, slots], ACT.Relu)
+                nc.scalar.activation(mask[:, split:, slots], positive[:], ACT.Sign)
             nc.gpsimd.tensor_tensor(slope[:, :, slots], mask[:, :, slots], g1[:, slots].unsqueeze(1).to_broadcast([P, PACK, C]), ALU.mult)
 
         w1_bf = once.tile([P, E, K, PACK], BF16, name="w1_bf", tag="stage", align_bytes=64)

@@ -22,17 +22,29 @@ P = 128
 PACK = 4
 PASSES = N // (P * PACK)
 LANES = 16
+QUADS, QUAD, QUAD_ROWS = 4, 32, 4
+GROUPS = T // P
+
+PLANE_RUNS = [
+    [(0, 1), (1, 2), (2, PACK)],
+    [(0, 1), (1, PACK)],
+    [(0, 1), (1, PACK)],
+    [(0, PACK)],
+]
+GPSIMD_MASK_PLANES = [PACK, 2]
 
 
-def tile_moe_seb_relu_kernel(tc, dy_words, dy_scales, w2t_words, w2t_scales, w1t, a, gate1, gate2, offs, offs2, out):
+def tile_moe_seb_relu_kernel(
+    tc, dy_words, dy_scales, w2t_words, w2t_scales, w1t, a, gate1, gate2, offs, offs2, out
+):
     nc = tc.nc
 
-    def entries(tile, lo, hi):
-        return tile[:, lo // LANES : hi // LANES]
+    def entries(list_tile, lo, hi):
+        return list_tile[:, lo // LANES : hi // LANES]
 
     with ExitStack() as ctx:
         keep = ctx.enter_context(tc.tile_pool(name="keep", bufs=1))
-        ring = ctx.enter_context(tc.tile_pool(name="ring", bufs=3))
+        ring = ctx.enter_context(tc.tile_pool(name="ring", bufs=GROUPS - 1))
         once = ctx.enter_context(tc.tile_pool(name="once", bufs=1))
         mm_psum = ctx.enter_context(tc.psum_pool(name="mm_psum", bufs=1))
         tr_psum = ctx.enter_context(tc.psum_pool(name="tr_psum", bufs=4))
@@ -44,7 +56,7 @@ def tile_moe_seb_relu_kernel(tc, dy_words, dy_scales, w2t_words, w2t_scales, w1t
         dy_s = keep.tile([P, PASSES, T], U8, name="dy_s", align_bytes=64)
         w2_w = keep.tile([P, E, PASSES, 2 * H], U8, name="w2_w", align_bytes=64)
         w2_s = keep.tile([P, E * PASSES, H], U8, name="w2_s", align_bytes=64)
-        q_col = keep.tile([P, T // P], F32, name="q_col")
+        q_col = keep.tile([P, GROUPS], F32, name="q_col")
         ident = keep.tile([P, P], F32, name="ident")
         a_sb = keep.tile([P, PACK, T], F32, name="a_sb")
         g1 = keep.tile([P, T], F32, name="g1")
@@ -56,17 +68,17 @@ def tile_moe_seb_relu_kernel(tc, dy_words, dy_scales, w2t_words, w2t_scales, w1t
         dy_rows = dy_words.rearrange("s p t d -> p s (t d)").bitcast(I32)
         nc.sync.dma_start(dy_w[:, 0, :], dy_rows[:, 0, :])
         nc.sync.dma_start(list2[:], offs2)
-        for quad in range(4):
+        for quad in range(QUADS):
             nc.sync.dma_start(
-                dy_s[32 * quad : 32 * quad + 4, :, :].bitcast(I32),
-                dy_scales[:, 4 * quad : 4 * quad + 4, :].rearrange("s b t -> b s t").bitcast(I32),
+                dy_s[QUAD * quad : QUAD * quad + QUAD_ROWS, :, :].bitcast(I32),
+                dy_scales[:, QUAD_ROWS * quad : QUAD_ROWS * (quad + 1), :].rearrange("s b t -> b s t").bitcast(I32),
             )
         nc.sync.dma_start(dy_w[:, 1, :], dy_rows[:, 1, :])
         nc.sync.dma_start(w2_w[:, 0, :, :].bitcast(I32), w2t_words[0].rearrange("s p n -> p s n").bitcast(I32))
-        for quad in range(4):
+        for quad in range(QUADS):
             nc.sync.dma_start(
-                w2_s[32 * quad : 32 * quad + 4, :, :].bitcast(I32),
-                w2t_scales[:, :, 4 * quad : 4 * quad + 4, :].rearrange("f s b i -> b (f s) i").bitcast(I32),
+                w2_s[QUAD * quad : QUAD * quad + QUAD_ROWS, :, :].bitcast(I32),
+                w2t_scales[:, :, QUAD_ROWS * quad : QUAD_ROWS * (quad + 1), :].rearrange("f s b i -> b (f s) i").bitcast(I32),
             )
         with nc.allow_non_contiguous_dma(reason="one value of gate2 a partition"):
             nc.sync.dma_start(q_col[:], gate2[0, :].rearrange("(c p) -> p c", p=P))
@@ -76,8 +88,8 @@ def tile_moe_seb_relu_kernel(tc, dy_words, dy_scales, w2t_words, w2t_scales, w1t
         nc.sync.dma_start(w2_w[:, 1, :, :].bitcast(I32), w2t_words[1].rearrange("s p n -> p s n").bitcast(I32))
         nc.sync.dma_start(g1[:], gate1)
         a_rows = a.rearrange("(p t) j -> p t j", t=PACK)
-        nc.sync.dma_start(a_sb[:, 0:2, :], a_rows[:, 0:2, :])
-        nc.sync.dma_start(a_sb[:, 2:4, :], a_rows[:, 2:4, :])
+        for t0 in range(0, PACK, PACK // 2):
+            nc.sync.dma_start(a_sb[:, t0 : t0 + PACK // 2, :], a_rows[:, t0 : t0 + PACK // 2, :])
         for e in range(E):
             nc.sync.dma_start(w1_raw[:, e, :, :], w1t[e].rearrange("(p t) k -> p t k", t=PACK))
         nc.sync.dma_start(list1[:], offs)
@@ -93,7 +105,7 @@ def tile_moe_seb_relu_kernel(tc, dy_words, dy_scales, w2t_words, w2t_scales, w1t
         def gather_scales(s, lo, hi):
             nc.vector.tensor_copy(slot_s[s][:, lo:hi], dy_s[:, s, :].indirect(entries(list2, lo, hi)))
 
-        def second_layer(c, plane_runs):
+        def second_layer(c):
             f, half = divmod(c, C // P)
             cols = slice(c * P, (c + 1) * P)
             acc = mm_psum.tile([P, H], F32, name="acc")
@@ -107,125 +119,118 @@ def tile_moe_seb_relu_kernel(tc, dy_words, dy_scales, w2t_words, w2t_scales, w1t
                     start=(s == 0),
                     stop=(s == PASSES - 1),
                 )
-            pool = once if c == 3 else ring
+            pool = once if c == GROUPS - 1 else ring
             gated = pool.tile([P, PACK, P], F32, name="gated", tag="stage", align_bytes=64)
             by_plane = acc[:].rearrange("p (m t) -> p t m", t=PACK)
-            for t0, t1 in plane_runs:
+            for t0, t1 in PLANE_RUNS[c]:
                 nc.scalar.activation(gated[:, t0:t1, :], by_plane[:, t0:t1, :], ACT.Copy, scale=q_col[:, c : c + 1])
-            for t0, t1 in plane_runs:
+            for t0, t1 in PLANE_RUNS[c]:
                 turned = tr_psum.tile([P, t1 - t0, P], F32, name="turned", tag="turned")
                 for t in range(t0, t1):
                     nc.tensor.transpose(turned[:, t - t0, :], gated[:, t, :], ident[:])
                 nc.scalar.copy(dc_slots[:, f, t0:t1, half * P : (half + 1) * P], turned[:])
 
-        def scatter_dc(lo, hi):
-            f = lo // C
+        def scatter_dc(c):
+            f, half = divmod(c, C // P)
             for t in range(PACK):
-                nc.vector.tensor_copy(dc[t][:].indirect(entries(list2, lo, hi)), dc_slots[:, f, t, lo - f * C : hi - f * C])
+                nc.vector.tensor_copy(
+                    dc[t][:].indirect(entries(list2, c * P, (c + 1) * P)), dc_slots[:, f, t, half * P : (half + 1) * P]
+                )
 
-        gather_words(0, 0, 128)
-        gather_words(0, 128, 512)
-        gather_words(1, 0, 128)
-        gather_scales(0, 0, 128)
-        gather_scales(1, 0, 128)
-        second_layer(0, [(0, 1), (1, PACK)])
-        gather_words(1, 128, 512)
-        gather_scales(0, 128, 512)
-        gather_scales(1, 128, 512)
-        second_layer(1, [(0, 1), (1, PACK)])
-        second_layer(2, [(0, 1), (1, PACK)])
-        second_layer(3, [(0, PACK)])
-        scatter_dc(0, 128)
-        scatter_dc(128, 256)
-        scatter_dc(256, 384)
-        scatter_dc(384, 512)
+        gather_words(0, 0, P)
+        gather_words(0, P, T)
+        gather_words(1, 0, P)
+        gather_scales(0, 0, P)
+        gather_scales(1, 0, P)
+        second_layer(0)
+        gather_words(1, P, T)
+        gather_scales(0, P, T)
+        gather_scales(1, P, T)
+        for c in range(1, GROUPS):
+            second_layer(c)
+        for c in range(GROUPS):
+            scatter_dc(c)
 
         slope = keep.tile([P, PACK, T], F32, name="slope")
         mask = keep.tile([P, PACK, T], F32, name="mask")
         for e in range(E):
             slots = slice(e * C, (e + 1) * C)
-            split = PACK if e == 0 else 2
+            split = GPSIMD_MASK_PLANES[e]
             nc.gpsimd.tensor_scalar(mask[:, :split, slots], a_sb[:, :split, slots], 0.0, 0.0, ALU.is_gt, ALU.add)
             if split < PACK:
                 positive = once.tile([P, PACK - split, C], F32, name="positive", tag="stage", align_bytes=64)
                 nc.scalar.activation(positive[:], a_sb[:, split:, slots], ACT.Relu)
                 nc.scalar.activation(mask[:, split:, slots], positive[:], ACT.Sign)
-            nc.gpsimd.tensor_tensor(slope[:, :, slots], mask[:, :, slots], g1[:, slots].unsqueeze(1).to_broadcast([P, PACK, C]), ALU.mult)
+            nc.gpsimd.tensor_tensor(
+                slope[:, :, slots], mask[:, :, slots], g1[:, slots].unsqueeze(1).to_broadcast([P, PACK, C]), ALU.mult
+            )
 
         w1_bf = once.tile([P, E, K, PACK], BF16, name="w1_bf", tag="stage", align_bytes=64)
         w1_s = keep.tile([P, E, K], U8, name="w1_s", align_bytes=64)
         for e in range(E):
             nc.scalar.copy(w1_bf[:, e, :, :], w1_raw[:, e, :, :].rearrange("p t k -> p k t"))
 
-
-        da = [
-            keep.tile([P, PACK, C], F32, name="da0", align_bytes=64),
-            keep.tile([P, PACK, C], F32, name="da1", tag="rows", align_bytes=64),
-        ]
-        da_bf = [
-            da[1][:, 2:PACK, :].rearrange("p t j -> p (t j)").bitcast(BF16),
-            None,
-        ]
-        da_w = [
-            keep.tile([P, C], U32, name="da_w0", tag="handed", align_bytes=64),
-            keep.tile([P, C], U32, name="da_w1", align_bytes=64),
-        ]
+        shift = PACK // 2
+        da = keep.tile([P, PACK + shift, C], F32, name="da", tag="da", align_bytes=64)
         da_s = keep.tile([P, E, C], U8, name="da_s", align_bytes=64)
         dx_slots = keep.tile([P, E, K // P, C], F32, name="dx_slots")
-        dx = [keep.tile([P, T], F32, name="dx0"), None]
 
         def gather_dc(e, t):
-            nc.vector.tensor_tensor(da[e][:, t, :], dc[t][:].indirect(entries(list1, e * C, (e + 1) * C)), slope[:, t, e * C : (e + 1) * C], ALU.mult)
-
-        def round_da(e):
-            if e == 1:
-                da_bf1 = keep.tile([P, C * PACK], BF16, name="da_bf1", tag="handed", align_bytes=64)
-                da_bf[1] = da_bf1[:]
-            nc.scalar.copy(da_bf[e].rearrange("p (j t) -> p j t", t=PACK), da[e][:].rearrange("p t j -> p j t"))
-
-        def quantize_da(e):
-            nc.vector.quantize_mx(out=da_w[e][:].bitcast(FP8X4), scales=da_s[:, e, :], in_=da_bf[e])
-
-        def first_layer(e, kt):
-            cols = slice(kt * P, (kt + 1) * P)
-            acc1 = out_psum.tile([P, C], F32, name="acc1")
-            nc.tensor.matmul_mx(
-                out=acc1[:],
-                lhsT=w1_w[:, e, cols].bitcast(FP8X4),
-                lhsT_scale=w1_s[:, e, cols],
-                rhs=da_w[e][:].bitcast(FP8X4),
-                rhs_scale=da_s[:, e, :],
-                start=True,
-                stop=True,
+            slots = slice(e * C, (e + 1) * C)
+            nc.vector.tensor_tensor(
+                da[:, shift * e + t, :], dc[t][:].indirect(entries(list1, e * C, (e + 1) * C)), slope[:, t, slots], ALU.mult
             )
-            nc.scalar.copy(dx_slots[:, e, kt, :], acc1[:])
 
-        def scatter_dx(e, kt):
-            nc.vector.tensor_copy(dx[kt][:].indirect(entries(list1, e * C, (e + 1) * C)), dx_slots[:, e, kt, :])
+        def round_da(e, da_bf):
+            nc.scalar.copy(da_bf[:], da[:, shift * e : shift * e + PACK, :].rearrange("p t j -> p j t"))
+
+        def quantize_da(e, da_bf, da_w):
+            nc.vector.quantize_mx(out=da_w[:].bitcast(FP8X4), scales=da_s[:, e, :], in_=da_bf[:].rearrange("p j t -> p (j t)"))
+
+        def first_layer(e, w1_w, da_w):
+            for kt in range(K // P):
+                cols = slice(kt * P, (kt + 1) * P)
+                acc1 = out_psum.tile([P, C], F32, name="acc1")
+                nc.tensor.matmul_mx(
+                    out=acc1[:],
+                    lhsT=w1_w[:, e, cols].bitcast(FP8X4),
+                    lhsT_scale=w1_s[:, e, cols],
+                    rhs=da_w[:].bitcast(FP8X4),
+                    rhs_scale=da_s[:, e, :],
+                    start=True,
+                    stop=True,
+                )
+                nc.scalar.copy(dx_slots[:, e, kt, :], acc1[:])
+
+        def scatter_dx(e, kt, window):
+            nc.vector.tensor_copy(window[:].indirect(entries(list1, e * C, (e + 1) * C)), dx_slots[:, e, kt, :])
 
         for t in range(PACK):
             gather_dc(0, t)
-        round_da(0)
-        gather_dc(1, 0)
-        gather_dc(1, 1)
-        w1_w = keep.tile([P, E, K], U32, name="w1_w", tag="dc0", align_bytes=64)
+        da_bf0 = keep.tile([P, C, PACK], BF16, name="da_bf0", tag="rows", align_bytes=64)
+        round_da(0, da_bf0)
+        for t in range(shift, PACK):
+            gather_dc(1, t)
+        w1_w = keep.tile([P, E, K], U32, name="w1_w", tag="dc%d" % shift, align_bytes=64)
         nc.vector.quantize_mx(
             out=w1_w[:].rearrange("p e k -> p (e k)").bitcast(FP8X4),
             scales=w1_s[:].rearrange("p e k -> p (e k)"),
             in_=w1_bf[:].rearrange("p e k t -> p (e k t)"),
         )
-        quantize_da(0)
-        gather_dc(1, 2)
-        gather_dc(1, 3)
-        first_layer(0, 0)
-        first_layer(0, 1)
-        round_da(1)
-        scatter_dx(0, 0)
-        quantize_da(1)
-        first_layer(1, 0)
-        first_layer(1, 1)
-        dx[1] = keep.tile([P, T], F32, name="dx1", tag="handed", align_bytes=64)
-        scatter_dx(0, 1)
-        for kt in range(K // P):
-            scatter_dx(1, kt)
-            nc.sync.dma_start(out[kt * P : (kt + 1) * P, :], dx[kt][:])
+        da_w0 = keep.tile([P, C], U32, name="da_w0", tag="handed", align_bytes=64)
+        quantize_da(0, da_bf0, da_w0)
+        for t in range(shift):
+            gather_dc(1, t)
+        first_layer(0, w1_w, da_w0)
+        da_bf1 = keep.tile([P, C, PACK], BF16, name="da_bf1", tag="handed", align_bytes=64)
+        round_da(1, da_bf1)
+        dx0 = keep.tile([P, T], F32, name="dx0")
+        scatter_dx(0, 0, dx0)
+        da_w1 = keep.tile([P, C], U32, name="da_w1", align_bytes=64)
+        quantize_da(1, da_bf1, da_w1)
+        first_layer(1, w1_w, da_w1)
+        dx1 = keep.tile([P, T], F32, name="dx1", tag="da", align_bytes=64)
+        scatter_dx(0, 1, dx1)
+        for kt, window in enumerate([dx0, dx1]):
+            scatter_dx(1, kt, window)
+            nc.sync.dma_start(out[kt * P : (kt + 1) * P, :], window[:])

@@ -95,7 +95,12 @@ def tile_moe_seb_relu_kernel(
         nc.sync.dma_start(list1[:], offs)
 
         slot_w = [keep.tile([P, T], U32, name="slot_w%d" % s, align_bytes=64) for s in range(PASSES)]
-        slot_s = [keep.tile([P, T], U8, name="slot_s%d" % s, align_bytes=64) for s in range(PASSES)]
+        first_s = [keep.tile([P, P], U8, name="first_s%d" % s, tag="slot_s%d" % s, align_bytes=64) for s in range(PASSES)]
+        rest_s = [keep.tile([P, T - P], U8, name="rest_s%d" % s, tag="slot_s%d" % s, align_bytes=64) for s in range(PASSES)]
+
+        def slot_scales(s, lo, hi):
+            return first_s[s][:, lo:hi] if hi <= P else rest_s[s][:, lo - P : hi - P]
+
         dc = [keep.tile([P, T], F32, name="dc%d" % t, tag="dc%d" % t, align_bytes=64) for t in range(PACK)]
         dc_slots = keep.tile([P, E, PACK, C], F32, name="dc_slots")
 
@@ -103,7 +108,7 @@ def tile_moe_seb_relu_kernel(
             nc.vector.tensor_copy(slot_w[s][:, lo:hi], dy_w[:, s, :].bitcast(U32).indirect(entries(list2, lo, hi)))
 
         def gather_scales(s, lo, hi):
-            nc.vector.tensor_copy(slot_s[s][:, lo:hi], dy_s[:, s, :].indirect(entries(list2, lo, hi)))
+            nc.vector.tensor_copy(slot_scales(s, lo, hi), dy_s[:, s, :].indirect(entries(list2, lo, hi)))
 
         def second_layer(c):
             f, half = divmod(c, C // P)
@@ -113,7 +118,7 @@ def tile_moe_seb_relu_kernel(
                 nc.tensor.matmul_mx(
                     out=acc[:],
                     lhsT=slot_w[s][:, cols].bitcast(FP8X4),
-                    lhsT_scale=slot_s[s][:, cols],
+                    lhsT_scale=slot_scales(s, c * P, (c + 1) * P),
                     rhs=w2_w[:, f, s, :].bitcast(FP4X4),
                     rhs_scale=w2_s[:, PASSES * f + s, :],
                     start=(s == 0),

@@ -28,10 +28,9 @@ GROUPS = T // P
 PLANE_RUNS = [
     [(0, 1), (1, 2), (2, PACK)],
     [(0, 1), (1, PACK)],
-    [(0, 1), (1, PACK)],
+    [(0, PACK)],
     [(0, PACK)],
 ]
-GPSIMD_MASK_PLANES = [PACK, 2]
 
 
 def tile_moe_seb_relu_kernel(
@@ -44,10 +43,9 @@ def tile_moe_seb_relu_kernel(
 
     with ExitStack() as ctx:
         keep = ctx.enter_context(tc.tile_pool(name="keep", bufs=1))
-        ring = ctx.enter_context(tc.tile_pool(name="ring", bufs=GROUPS - 1))
         once = ctx.enter_context(tc.tile_pool(name="once", bufs=1))
         mm_psum = ctx.enter_context(tc.psum_pool(name="mm_psum", bufs=1))
-        tr_psum = ctx.enter_context(tc.psum_pool(name="tr_psum", bufs=4))
+        tr_psum = ctx.enter_context(tc.psum_pool(name="tr_psum", bufs=3))
         out_psum = ctx.enter_context(tc.psum_pool(name="out_psum", bufs=2))
 
         list2 = keep.tile([P, T // LANES], U16, name="list2")
@@ -57,6 +55,7 @@ def tile_moe_seb_relu_kernel(
         w2_w = keep.tile([P, E, PASSES, 2 * H], U8, name="w2_w", align_bytes=64)
         w2_s = keep.tile([P, E * PASSES, H], U8, name="w2_s", align_bytes=64)
         q_col = keep.tile([P, GROUPS], F32, name="q_col")
+        q_rows = keep.tile([P, P], F32, name="q_rows")
         ident = keep.tile([P, P], F32, name="ident")
         a_sb = keep.tile([P, PACK, T], F32, name="a_sb")
         g1 = keep.tile([P, T], F32, name="g1")
@@ -64,6 +63,8 @@ def tile_moe_seb_relu_kernel(
 
         nc.gpsimd.memset(dy_s[:].bitcast(I32), 0)
         nc.vector.memset(w2_s[:].bitcast(I32), 0)
+        nc.gpsimd.memset(q_rows[:], 0.0)
+        nc.gpsimd.dma_start(q_rows[:GROUPS, :], gate2[0, :].rearrange("(c p) -> c p", p=P))
 
         dy_rows = dy_words.rearrange("s p t d -> p s (t d)").bitcast(I32)
         nc.sync.dma_start(dy_w[:, 0, :], dy_rows[:, 0, :])
@@ -80,8 +81,6 @@ def tile_moe_seb_relu_kernel(
                 w2_s[QUAD * quad : QUAD * quad + QUAD_ROWS, :, :].bitcast(I32),
                 w2t_scales[:, :, QUAD_ROWS * quad : QUAD_ROWS * (quad + 1), :].rearrange("f s b i -> b (f s) i").bitcast(I32),
             )
-        with nc.allow_non_contiguous_dma(reason="one value of gate2 a partition"):
-            nc.sync.dma_start(q_col[:], gate2[0, :].rearrange("(c p) -> p c", p=P))
         ident_made = keep.tile([P, P], F32, name="ident_made")
         make_identity(nc, ident_made[:])
         nc.scalar.activation(ident[:], ident_made[:], ACT.Copy)
@@ -93,6 +92,10 @@ def tile_moe_seb_relu_kernel(
         for e in range(E):
             nc.sync.dma_start(w1_raw[:, e, :, :], w1t[e].rearrange("(p t) k -> p t k", t=PACK))
         nc.sync.dma_start(list1[:], offs)
+
+        q_turned = mm_psum.tile([P, P], F32, name="q_turned", tag="acc")
+        nc.tensor.transpose(q_turned[:], q_rows[:], ident[:])
+        nc.scalar.copy(q_col[:], q_turned[:, :GROUPS])
 
         slot_w = [keep.tile([P, T], U32, name="slot_w%d" % s, align_bytes=64) for s in range(PASSES)]
         first_s = [keep.tile([P, P], U8, name="first_s%d" % s, tag="slot_s%d" % s, align_bytes=64) for s in range(PASSES)]
@@ -113,7 +116,7 @@ def tile_moe_seb_relu_kernel(
         def second_layer(c):
             f, half = divmod(c, C // P)
             cols = slice(c * P, (c + 1) * P)
-            acc = mm_psum.tile([P, H], F32, name="acc")
+            acc = mm_psum.tile([P, H], F32, name="acc", tag="second" if c == 2 else "acc")
             for s in range(PASSES):
                 nc.tensor.matmul_mx(
                     out=acc[:],
@@ -124,13 +127,15 @@ def tile_moe_seb_relu_kernel(
                     start=(s == 0),
                     stop=(s == PASSES - 1),
                 )
-            pool = once if c == GROUPS - 1 else ring
-            gated = pool.tile([P, PACK, P], F32, name="gated", tag="stage", align_bytes=64)
+            gated = once.tile([P, PACK, P], F32, name="gated", tag="stage%d" % c, align_bytes=64)
             by_plane = acc[:].rearrange("p (m t) -> p t m", t=PACK)
             for t0, t1 in PLANE_RUNS[c]:
                 nc.scalar.activation(gated[:, t0:t1, :], by_plane[:, t0:t1, :], ACT.Copy, scale=q_col[:, c : c + 1])
             for t0, t1 in PLANE_RUNS[c]:
-                turned = tr_psum.tile([P, t1 - t0, P], F32, name="turned", tag="turned")
+                if c == 0 and t1 == PACK:
+                    turned = mm_psum.tile([P, t1 - t0, P], F32, name="turned", tag="second")
+                else:
+                    turned = tr_psum.tile([P, t1 - t0, P], F32, name="turned", tag="turned")
                 for t in range(t0, t1):
                     nc.tensor.transpose(turned[:, t - t0, :], gated[:, t, :], ident[:])
                 nc.scalar.copy(dc_slots[:, f, t0:t1, half * P : (half + 1) * P], turned[:])
@@ -157,20 +162,19 @@ def tile_moe_seb_relu_kernel(
             scatter_dc(c)
 
         slope = keep.tile([P, PACK, T], F32, name="slope")
-        mask = keep.tile([P, PACK, T], F32, name="mask")
+        clipped = keep.tile([P, PACK, T], F32, name="clipped", tag="clipped", align_bytes=64)
         for e in range(E):
             slots = slice(e * C, (e + 1) * C)
-            split = GPSIMD_MASK_PLANES[e]
-            nc.gpsimd.tensor_scalar(mask[:, :split, slots], a_sb[:, :split, slots], 0.0, 0.0, ALU.is_gt, ALU.add)
-            if split < PACK:
-                positive = once.tile([P, PACK - split, C], F32, name="positive", tag="stage", align_bytes=64)
-                nc.scalar.activation(positive[:], a_sb[:, split:, slots], ACT.Relu)
-                nc.scalar.activation(mask[:, split:, slots], positive[:], ACT.Sign)
+            nc.gpsimd.tensor_scalar(clipped[:, :, slots], a_sb[:, :, slots], 1.0, 0.0, ALU.min, ALU.max)
+        for e in range(E):
+            slots = slice(e * C, (e + 1) * C)
+            mask = once.tile([P, PACK, C], F32, name="mask", tag="stage%d" % (1 + e), align_bytes=64)
+            nc.scalar.activation(mask[:], clipped[:, :, slots], ACT.Sign)
             nc.gpsimd.tensor_tensor(
-                slope[:, :, slots], mask[:, :, slots], g1[:, slots].unsqueeze(1).to_broadcast([P, PACK, C]), ALU.mult
+                slope[:, :, slots], mask[:], g1[:, slots].unsqueeze(1).to_broadcast([P, PACK, C]), ALU.mult
             )
 
-        w1_bf = once.tile([P, E, K, PACK], BF16, name="w1_bf", tag="stage", align_bytes=64)
+        w1_bf = once.tile([P, E, K, PACK], BF16, name="w1_bf", tag="stage3", align_bytes=64)
         w1_s = keep.tile([P, E, K], U8, name="w1_s", align_bytes=64)
         for e in range(E):
             nc.scalar.copy(w1_bf[:, e, :, :], w1_raw[:, e, :, :].rearrange("p t k -> p k t"))

@@ -43,6 +43,7 @@ def tile_moe_seb_relu_kernel(
 
     with ExitStack() as ctx:
         keep = ctx.enter_context(tc.tile_pool(name="keep", bufs=1))
+        late = ctx.enter_context(tc.tile_pool(name="late", bufs=1))
         once = ctx.enter_context(tc.tile_pool(name="once", bufs=1))
         mm_psum = ctx.enter_context(tc.psum_pool(name="mm_psum", bufs=1))
         tr_psum = ctx.enter_context(tc.psum_pool(name="tr_psum", bufs=3))
@@ -52,19 +53,23 @@ def tile_moe_seb_relu_kernel(
         list1 = keep.tile([P, T // LANES], U16, name="list1")
         dy_w = keep.tile([P, PASSES, T], I32, name="dy_w", align_bytes=64)
         dy_s = keep.tile([P, PASSES, T], U8, name="dy_s", align_bytes=64)
-        w2_w = keep.tile([P, E, PASSES, 2 * H], U8, name="w2_w", align_bytes=64)
+        plane_bytes = 4 * T
+        q_rows = late.tile([P, (2 * PACK + 2) * T], F32, name="q_rows", offset=0, align_bytes=64)
+        w2_w = [
+            keep.tile([P, PASSES, 2 * H], U8, name="w2_w0", align_bytes=64),
+            late.tile([P, PASSES, 2 * H], U8, name="w2_w1", offset=0, align_bytes=64),
+        ]
         w2_s = keep.tile([P, E * PASSES, H], U8, name="w2_s", align_bytes=64)
         q_col = keep.tile([P, GROUPS], F32, name="q_col")
-        q_rows = keep.tile([P, P], F32, name="q_rows")
         ident = keep.tile([P, P], F32, name="ident")
-        a_sb = keep.tile([P, PACK, T], F32, name="a_sb")
-        g1 = keep.tile([P, T], F32, name="g1")
-        w1_raw = keep.tile([P, E, PACK, K], F32, name="w1_raw", tag="rows", align_bytes=64)
+        a_sb = late.tile([P, PACK, T], F32, name="a_sb", offset=2 * plane_bytes, align_bytes=64)
+        g1 = late.tile([P, T], F32, name="g1", offset=plane_bytes, align_bytes=64)
+        w1_raw = late.tile([P, E, PACK, K], F32, name="w1_raw", offset=(2 + PACK) * plane_bytes, align_bytes=64)
 
         nc.gpsimd.memset(dy_s[:].bitcast(I32), 0)
         nc.vector.memset(w2_s[:].bitcast(I32), 0)
-        nc.gpsimd.memset(q_rows[:], 0.0)
-        nc.gpsimd.dma_start(q_rows[:GROUPS, :], gate2[0, :].rearrange("(c p) -> c p", p=P))
+        nc.gpsimd.memset(q_rows[:, :P], 0.0)
+        nc.gpsimd.dma_start(q_rows[:GROUPS, :P], gate2[0, :].rearrange("(c p) -> c p", p=P))
 
         dy_rows = dy_words.rearrange("s p t d -> p s (t d)").bitcast(I32)
         nc.sync.dma_start(dy_w[:, 0, :], dy_rows[:, 0, :])
@@ -75,16 +80,17 @@ def tile_moe_seb_relu_kernel(
                 dy_scales[:, QUAD_ROWS * quad : QUAD_ROWS * (quad + 1), :].rearrange("s b t -> b s t").bitcast(I32),
             )
         nc.sync.dma_start(dy_w[:, 1, :], dy_rows[:, 1, :])
-        nc.sync.dma_start(w2_w[:, 0, :, :].bitcast(I32), w2t_words[0].rearrange("s p n -> p s n").bitcast(I32))
-        for quad in range(QUADS):
-            nc.sync.dma_start(
-                w2_s[QUAD * quad : QUAD * quad + QUAD_ROWS, :, :].bitcast(I32),
-                w2t_scales[:, :, QUAD_ROWS * quad : QUAD_ROWS * (quad + 1), :].rearrange("f s b i -> b (f s) i").bitcast(I32),
-            )
+        nc.sync.dma_start(w2_w[0][:].bitcast(I32), w2t_words[0].rearrange("s p n -> p s n").bitcast(I32))
+        for f in range(E):
+            for quad in range(QUADS):
+                nc.sync.dma_start(
+                    w2_s[QUAD * quad : QUAD * quad + QUAD_ROWS, PASSES * f : PASSES * (f + 1), :].bitcast(I32),
+                    w2t_scales[f, :, QUAD_ROWS * quad : QUAD_ROWS * (quad + 1), :].rearrange("s b i -> b s i").bitcast(I32),
+                )
         ident_made = keep.tile([P, P], F32, name="ident_made")
         make_identity(nc, ident_made[:])
         nc.scalar.activation(ident[:], ident_made[:], ACT.Copy)
-        nc.sync.dma_start(w2_w[:, 1, :, :].bitcast(I32), w2t_words[1].rearrange("s p n -> p s n").bitcast(I32))
+        nc.sync.dma_start(w2_w[1][:].bitcast(I32), w2t_words[1].rearrange("s p n -> p s n").bitcast(I32))
         nc.sync.dma_start(g1[:], gate1)
         a_rows = a.rearrange("(p t) j -> p t j", t=PACK)
         for t0 in range(0, PACK, PACK // 2):
@@ -94,7 +100,7 @@ def tile_moe_seb_relu_kernel(
         nc.sync.dma_start(list1[:], offs)
 
         q_turned = mm_psum.tile([P, P], F32, name="q_turned", tag="acc")
-        nc.tensor.transpose(q_turned[:], q_rows[:], ident[:])
+        nc.tensor.transpose(q_turned[:], q_rows[:, :P], ident[:])
         nc.scalar.copy(q_col[:], q_turned[:, :GROUPS])
 
         slot_w = [keep.tile([P, T], U32, name="slot_w%d" % s, align_bytes=64) for s in range(PASSES)]
@@ -122,7 +128,7 @@ def tile_moe_seb_relu_kernel(
                     out=acc[:],
                     lhsT=slot_w[s][:, cols].bitcast(FP8X4),
                     lhsT_scale=slot_scales(s, c * P, (c + 1) * P),
-                    rhs=w2_w[:, f, s, :].bitcast(FP4X4),
+                    rhs=w2_w[f][:, s, :].bitcast(FP4X4),
                     rhs_scale=w2_s[:, PASSES * f + s, :],
                     start=(s == 0),
                     stop=(s == PASSES - 1),
@@ -140,12 +146,9 @@ def tile_moe_seb_relu_kernel(
                     nc.tensor.transpose(turned[:, t - t0, :], gated[:, t, :], ident[:])
                 nc.scalar.copy(dc_slots[:, f, t0:t1, half * P : (half + 1) * P], turned[:])
 
-        def scatter_dc(c):
-            f, half = divmod(c, C // P)
+        def scatter_dc(f, lo, hi):
             for t in range(PACK):
-                nc.vector.tensor_copy(
-                    dc[t][:].indirect(entries(list2, c * P, (c + 1) * P)), dc_slots[:, f, t, half * P : (half + 1) * P]
-                )
+                nc.vector.tensor_copy(dc[t][:].indirect(entries(list2, f * C + lo, f * C + hi)), dc_slots[:, f, t, lo:hi])
 
         gather_words(0, 0, P)
         gather_words(0, P, T)
@@ -158,10 +161,12 @@ def tile_moe_seb_relu_kernel(
         gather_scales(1, P, T)
         for c in range(1, GROUPS):
             second_layer(c)
-        for c in range(GROUPS):
-            scatter_dc(c)
+        scatter_dc(0, 0, P)
+        scatter_dc(0, P, C)
+        scatter_dc(1, 0, P)
+        scatter_dc(1, P, C)
 
-        slope = keep.tile([P, PACK, T], F32, name="slope")
+        slope = [keep.tile([P, PACK, C], F32, name="slope%d" % e, tag="slope%d" % e, align_bytes=64) for e in range(E)]
         clipped = keep.tile([P, PACK, T], F32, name="clipped", tag="clipped", align_bytes=64)
         for e in range(E):
             slots = slice(e * C, (e + 1) * C)
@@ -171,27 +176,28 @@ def tile_moe_seb_relu_kernel(
             mask = once.tile([P, PACK, C], F32, name="mask", tag="stage%d" % (1 + e), align_bytes=64)
             nc.scalar.activation(mask[:], clipped[:, :, slots], ACT.Sign)
             nc.gpsimd.tensor_tensor(
-                slope[:, :, slots], mask[:], g1[:, slots].unsqueeze(1).to_broadcast([P, PACK, C]), ALU.mult
+                slope[e][:], mask[:], g1[:, slots].unsqueeze(1).to_broadcast([P, PACK, C]), ALU.mult
+            )
+
+        def interleave(columns, planes):
+            nc.scalar.copy(
+                columns.rearrange("p (c i) t -> p c t i", i=PACK), planes.rearrange("p t (c i) -> p c t i", i=PACK)
             )
 
         w1_bf = once.tile([P, E, K, PACK], BF16, name="w1_bf", tag="stage3", align_bytes=64)
         w1_s = keep.tile([P, E, K], U8, name="w1_s", align_bytes=64)
         for e in range(E):
-            nc.scalar.copy(w1_bf[:, e, :, :], w1_raw[:, e, :, :].rearrange("p t k -> p k t"))
+            interleave(w1_bf[:, e, :, :], w1_raw[:, e, :, :])
 
-        shift = PACK // 2
-        da = keep.tile([P, PACK + shift, C], F32, name="da", tag="da", align_bytes=64)
+        da_all = keep.tile([P, PACK + 1, C], F32, name="da_all", tag="da", align_bytes=64)
+        da = [da_all[:, e : e + PACK, :] for e in range(E)]
         da_s = keep.tile([P, E, C], U8, name="da_s", align_bytes=64)
         dx_slots = keep.tile([P, E, K // P, C], F32, name="dx_slots")
 
-        def gather_dc(e, t):
-            slots = slice(e * C, (e + 1) * C)
+        def gather_dc(e, t, lo, hi):
             nc.vector.tensor_tensor(
-                da[:, shift * e + t, :], dc[t][:].indirect(entries(list1, e * C, (e + 1) * C)), slope[:, t, slots], ALU.mult
+                da[e][:, t, lo:hi], dc[t][:].indirect(entries(list1, e * C + lo, e * C + hi)), slope[e][:, t, lo:hi], ALU.mult
             )
-
-        def round_da(e, da_bf):
-            nc.scalar.copy(da_bf[:], da[:, shift * e : shift * e + PACK, :].rearrange("p t j -> p j t"))
 
         def quantize_da(e, da_bf, da_w):
             nc.vector.quantize_mx(out=da_w[:].bitcast(FP8X4), scales=da_s[:, e, :], in_=da_bf[:].rearrange("p j t -> p (j t)"))
@@ -215,12 +221,12 @@ def tile_moe_seb_relu_kernel(
             nc.vector.tensor_copy(window[:].indirect(entries(list1, e * C, (e + 1) * C)), dx_slots[:, e, kt, :])
 
         for t in range(PACK):
-            gather_dc(0, t)
-        da_bf0 = keep.tile([P, C, PACK], BF16, name="da_bf0", tag="rows", align_bytes=64)
-        round_da(0, da_bf0)
-        for t in range(shift, PACK):
-            gather_dc(1, t)
-        w1_w = keep.tile([P, E, K], U32, name="w1_w", tag="dc%d" % shift, align_bytes=64)
+            gather_dc(0, t, 0, C)
+        da_bf0 = late.tile([P, C, PACK], BF16, name="da_bf0", offset=(2 + PACK) * plane_bytes, align_bytes=64)
+        for t in range(0, PACK, 2):
+            interleave(da_bf0[:, :, t : t + 2], da[0][:, t : t + 2, :])
+        gather_dc(1, PACK - 1, 0, C)
+        w1_w = keep.tile([P, E, K], U32, name="w1_w", tag="slope0", align_bytes=64)
         nc.vector.quantize_mx(
             out=w1_w[:].rearrange("p e k -> p (e k)").bitcast(FP8X4),
             scales=w1_s[:].rearrange("p e k -> p (e k)"),
@@ -228,11 +234,11 @@ def tile_moe_seb_relu_kernel(
         )
         da_w0 = keep.tile([P, C], U32, name="da_w0", tag="handed", align_bytes=64)
         quantize_da(0, da_bf0, da_w0)
-        for t in range(shift):
-            gather_dc(1, t)
+        for t in reversed(range(PACK - 1)):
+            gather_dc(1, t, 0, C)
         first_layer(0, w1_w, da_w0)
         da_bf1 = keep.tile([P, C, PACK], BF16, name="da_bf1", tag="handed", align_bytes=64)
-        round_da(1, da_bf1)
+        interleave(da_bf1[:], da[1])
         dx0 = keep.tile([P, T], F32, name="dx0")
         scatter_dx(0, 0, dx0)
         da_w1 = keep.tile([P, C], U32, name="da_w1", align_bytes=64)

@@ -43,33 +43,32 @@ def tile_moe_seb_relu_kernel(
 
     with ExitStack() as ctx:
         keep = ctx.enter_context(tc.tile_pool(name="keep", bufs=1))
-        late = ctx.enter_context(tc.tile_pool(name="late", bufs=1))
         once = ctx.enter_context(tc.tile_pool(name="once", bufs=1))
         mm_psum = ctx.enter_context(tc.psum_pool(name="mm_psum", bufs=1))
         tr_psum = ctx.enter_context(tc.psum_pool(name="tr_psum", bufs=3))
-        out_psum = ctx.enter_context(tc.psum_pool(name="out_psum", bufs=2))
+        out_psum = ctx.enter_context(tc.psum_pool(name="out_psum", bufs=3))
 
         list2 = keep.tile([P, T // LANES], U16, name="list2")
         list1 = keep.tile([P, T // LANES], U16, name="list1")
         dy_w = keep.tile([P, PASSES, T], I32, name="dy_w", align_bytes=64)
         dy_s = keep.tile([P, PASSES, T], U8, name="dy_s", align_bytes=64)
-        plane_bytes = 4 * T
-        q_rows = late.tile([P, (2 * PACK + 2) * T], F32, name="q_rows", offset=0, align_bytes=64)
-        w2_w = [
-            keep.tile([P, PASSES, 2 * H], U8, name="w2_w0", align_bytes=64),
-            late.tile([P, PASSES, 2 * H], U8, name="w2_w1", offset=0, align_bytes=64),
-        ]
+        w2_w = [keep.tile([P, PASSES, 2 * H], U8, name="w2_w%d" % f, align_bytes=64) for f in range(E)]
         w2_s = keep.tile([P, E * PASSES, H], U8, name="w2_s", align_bytes=64)
-        q_col = keep.tile([P, GROUPS], F32, name="q_col")
+        q_col = [keep.tile([P, 1], F32, name="q_col%d" % c) for c in range(GROUPS)]
         ident = keep.tile([P, P], F32, name="ident")
-        a_sb = late.tile([P, PACK, T], F32, name="a_sb", offset=2 * plane_bytes, align_bytes=64)
-        g1 = late.tile([P, T], F32, name="g1", offset=plane_bytes, align_bytes=64)
-        w1_raw = late.tile([P, E, PACK, K], F32, name="w1_raw", offset=(2 + PACK) * plane_bytes, align_bytes=64)
+        a_sb = keep.tile([P, PACK, T], F32, name="a_sb")
+        g1 = keep.tile([P, T], F32, name="g1")
+        w1_raw = keep.tile([P, E, PACK, K], F32, name="w1_raw", tag="rows", align_bytes=64)
 
         nc.gpsimd.memset(dy_s[:].bitcast(I32), 0)
-        nc.vector.memset(w2_s[:].bitcast(I32), 0)
-        nc.gpsimd.memset(q_rows[:, :P], 0.0)
-        nc.gpsimd.dma_start(q_rows[:GROUPS, :P], gate2[0, :].rearrange("(c p) -> c p", p=P))
+        w2_s_words = w2_s[:].rearrange("p a i -> p (a i)").bitcast(I32)
+        odd = E * PASSES * H // 8 + 1
+        nc.vector.memset(w2_s_words[:, :odd], 0)
+        nc.vector.memset(w2_s_words[:, odd:], 0)
+
+        def load_gates(f):
+            for c in range(f * C // P, (f + 1) * C // P):
+                nc.sync.dma_start(q_col[c][:], gate2[0, c * P : (c + 1) * P].rearrange("(p o) -> p o", o=1))
 
         dy_rows = dy_words.rearrange("s p t d -> p s (t d)").bitcast(I32)
         nc.sync.dma_start(dy_w[:, 0, :], dy_rows[:, 0, :])
@@ -87,21 +86,20 @@ def tile_moe_seb_relu_kernel(
                     w2_s[QUAD * quad : QUAD * quad + QUAD_ROWS, PASSES * f : PASSES * (f + 1), :].bitcast(I32),
                     w2t_scales[f, :, QUAD_ROWS * quad : QUAD_ROWS * (quad + 1), :].rearrange("s b i -> b s i").bitcast(I32),
                 )
+            if f == 0:
+                load_gates(0)
         ident_made = keep.tile([P, P], F32, name="ident_made")
         make_identity(nc, ident_made[:])
         nc.scalar.activation(ident[:], ident_made[:], ACT.Copy)
         nc.sync.dma_start(w2_w[1][:].bitcast(I32), w2t_words[1].rearrange("s p n -> p s n").bitcast(I32))
-        nc.sync.dma_start(g1[:], gate1)
         a_rows = a.rearrange("(p t) j -> p t j", t=PACK)
         for t0 in range(0, PACK, PACK // 2):
             nc.sync.dma_start(a_sb[:, t0 : t0 + PACK // 2, :], a_rows[:, t0 : t0 + PACK // 2, :])
+        load_gates(1)
+        nc.sync.dma_start(g1[:], gate1)
         for e in range(E):
             nc.sync.dma_start(w1_raw[:, e, :, :], w1t[e].rearrange("(p t) k -> p t k", t=PACK))
         nc.sync.dma_start(list1[:], offs)
-
-        q_turned = mm_psum.tile([P, P], F32, name="q_turned", tag="acc")
-        nc.tensor.transpose(q_turned[:], q_rows[:, :P], ident[:])
-        nc.scalar.copy(q_col[:], q_turned[:, :GROUPS])
 
         slot_w = [keep.tile([P, T], U32, name="slot_w%d" % s, align_bytes=64) for s in range(PASSES)]
         first_s = [keep.tile([P, P], U8, name="first_s%d" % s, tag="slot_s%d" % s, align_bytes=64) for s in range(PASSES)]
@@ -136,7 +134,7 @@ def tile_moe_seb_relu_kernel(
             gated = once.tile([P, PACK, P], F32, name="gated", tag="stage%d" % c, align_bytes=64)
             by_plane = acc[:].rearrange("p (m t) -> p t m", t=PACK)
             for t0, t1 in PLANE_RUNS[c]:
-                nc.scalar.activation(gated[:, t0:t1, :], by_plane[:, t0:t1, :], ACT.Copy, scale=q_col[:, c : c + 1])
+                nc.scalar.activation(gated[:, t0:t1, :], by_plane[:, t0:t1, :], ACT.Copy, scale=q_col[c][:])
             for t0, t1 in PLANE_RUNS[c]:
                 if c == 0 and t1 == PACK:
                     turned = mm_psum.tile([P, t1 - t0, P], F32, name="turned", tag="second")
@@ -189,8 +187,9 @@ def tile_moe_seb_relu_kernel(
         for e in range(E):
             interleave(w1_bf[:, e, :, :], w1_raw[:, e, :, :])
 
-        da_all = keep.tile([P, PACK + 1, C], F32, name="da_all", tag="da", align_bytes=64)
-        da = [da_all[:, e : e + PACK, :] for e in range(E)]
+        shift = C + C // 2
+        da_all = keep.tile([P, PACK * C + shift], F32, name="da_all", tag="da", align_bytes=64)
+        da = [da_all[:, shift * e : shift * e + PACK * C].rearrange("p (t j) -> p t j", t=PACK) for e in range(E)]
         da_s = keep.tile([P, E, C], U8, name="da_s", align_bytes=64)
         dx_slots = keep.tile([P, E, K // P, C], F32, name="dx_slots")
 
@@ -202,27 +201,26 @@ def tile_moe_seb_relu_kernel(
         def quantize_da(e, da_bf, da_w):
             nc.vector.quantize_mx(out=da_w[:].bitcast(FP8X4), scales=da_s[:, e, :], in_=da_bf[:].rearrange("p j t -> p (j t)"))
 
-        def first_layer(e, w1_w, da_w):
-            for kt in range(K // P):
-                cols = slice(kt * P, (kt + 1) * P)
-                acc1 = out_psum.tile([P, C], F32, name="acc1")
-                nc.tensor.matmul_mx(
-                    out=acc1[:],
-                    lhsT=w1_w[:, e, cols].bitcast(FP8X4),
-                    lhsT_scale=w1_s[:, e, cols],
-                    rhs=da_w[:].bitcast(FP8X4),
-                    rhs_scale=da_s[:, e, :],
-                    start=True,
-                    stop=True,
-                )
-                nc.scalar.copy(dx_slots[:, e, kt, :], acc1[:])
+        def first_layer(e, kt, lo, hi, w1_w, da_w):
+            cols = slice(kt * P, (kt + 1) * P)
+            acc1 = out_psum.tile([P, hi - lo], F32, name="acc1")
+            nc.tensor.matmul_mx(
+                out=acc1[:],
+                lhsT=w1_w[:, e, cols].bitcast(FP8X4),
+                lhsT_scale=w1_s[:, e, cols],
+                rhs=da_w[:, lo:hi].bitcast(FP8X4),
+                rhs_scale=da_s[:, e, lo:hi],
+                start=True,
+                stop=True,
+            )
+            return acc1
 
-        def scatter_dx(e, kt, window):
-            nc.vector.tensor_copy(window[:].indirect(entries(list1, e * C, (e + 1) * C)), dx_slots[:, e, kt, :])
+        def scatter_dx(e, kt, lo, hi, window):
+            nc.vector.tensor_copy(window[:].indirect(entries(list1, e * C + lo, e * C + hi)), dx_slots[:, e, kt, lo:hi])
 
         for t in range(PACK):
             gather_dc(0, t, 0, C)
-        da_bf0 = late.tile([P, C, PACK], BF16, name="da_bf0", offset=(2 + PACK) * plane_bytes, align_bytes=64)
+        da_bf0 = keep.tile([P, C, PACK], BF16, name="da_bf0", tag="rows", align_bytes=64)
         for t in range(0, PACK, 2):
             interleave(da_bf0[:, :, t : t + 2], da[0][:, t : t + 2, :])
         gather_dc(1, PACK - 1, 0, C)
@@ -234,18 +232,25 @@ def tile_moe_seb_relu_kernel(
         )
         da_w0 = keep.tile([P, C], U32, name="da_w0", tag="handed", align_bytes=64)
         quantize_da(0, da_bf0, da_w0)
-        for t in reversed(range(PACK - 1)):
+        for t in (2, 0, 1):
             gather_dc(1, t, 0, C)
-        first_layer(0, w1_w, da_w0)
+        nc.scalar.copy(dx_slots[:, 0, 0, :], first_layer(0, 0, 0, C, w1_w, da_w0)[:])
+        second_bank = first_layer(0, 1, 0, C, w1_w, da_w0)
         da_bf1 = keep.tile([P, C, PACK], BF16, name="da_bf1", tag="handed", align_bytes=64)
-        interleave(da_bf1[:], da[1])
+        for t in (2, 0):
+            interleave(da_bf1[:, :, t : t + 2], da[1][:, t : t + 2, :])
+        nc.scalar.copy(dx_slots[:, 0, 1, :], second_bank[:])
         dx0 = keep.tile([P, T], F32, name="dx0")
-        scatter_dx(0, 0, dx0)
+        scatter_dx(0, 0, 0, C, dx0)
         da_w1 = keep.tile([P, C], U32, name="da_w1", align_bytes=64)
         quantize_da(1, da_bf1, da_w1)
-        first_layer(1, w1_w, da_w1)
+        for lo in range(0, C, P):
+            for kt in range(K // P):
+                nc.scalar.copy(dx_slots[:, 1, kt, lo : lo + P], first_layer(1, kt, lo, lo + P, w1_w, da_w1)[:])
         dx1 = keep.tile([P, T], F32, name="dx1", tag="da", align_bytes=64)
-        scatter_dx(0, 1, dx1)
+        scatter_dx(0, 1, 0, C, dx1)
+        for lo in range(0, C, P):
+            for kt, window in enumerate([dx0, dx1]):
+                scatter_dx(1, kt, lo, lo + P, window)
         for kt, window in enumerate([dx0, dx1]):
-            scatter_dx(1, kt, window)
             nc.sync.dma_start(out[kt * P : (kt + 1) * P, :], window[:])

@@ -171,7 +171,7 @@ def tile_moe_seb_relu_kernel(
             nc.gpsimd.tensor_scalar(clipped[:, :, slots], a_sb[:, :, slots], 1.0, 0.0, ALU.min, ALU.max)
         for e in range(E):
             slots = slice(e * C, (e + 1) * C)
-            mask = once.tile([P, PACK, C], F32, name="mask", tag="stage%d" % (1 + e), align_bytes=64)
+            mask = once.tile([P, PACK, C], F32, name="mask", tag="stage%d" % (2 + e), align_bytes=64)
             nc.scalar.activation(mask[:], clipped[:, :, slots], ACT.Sign)
             nc.gpsimd.tensor_tensor(
                 slope[e][:], mask[:], g1[:, slots].unsqueeze(1).to_broadcast([P, PACK, C]), ALU.mult
@@ -182,7 +182,7 @@ def tile_moe_seb_relu_kernel(
                 columns.rearrange("p (c i) t -> p c t i", i=PACK), planes.rearrange("p t (c i) -> p c t i", i=PACK)
             )
 
-        w1_bf = once.tile([P, E, K, PACK], BF16, name="w1_bf", tag="stage3", align_bytes=64)
+        w1_bf = keep.tile([P, E, K, PACK], BF16, name="w1_bf", tag="clipped", align_bytes=64)
         w1_s = keep.tile([P, E, K], U8, name="w1_s", align_bytes=64)
         for e in range(E):
             interleave(w1_bf[:, e, :, :], w1_raw[:, e, :, :])

@@ -23,6 +23,7 @@ PACK = 4
 PASSES = N // (P * PACK)
 LANES = 16
 QUADS, QUAD, QUAD_ROWS = 4, 32, 4
+QUAD_ORDER = (0, 2, 1, 3)
 GROUPS = T // P
 
 PLANE_RUNS = [
@@ -73,7 +74,7 @@ def tile_moe_seb_relu_kernel(
         dy_rows = dy_words.rearrange("s p t d -> p s (t d)").bitcast(I32)
         nc.sync.dma_start(dy_w[:, 0, :], dy_rows[:, 0, :])
         nc.sync.dma_start(list2[:], offs2)
-        for quad in range(QUADS):
+        for quad in QUAD_ORDER:
             nc.sync.dma_start(
                 dy_s[QUAD * quad : QUAD * quad + QUAD_ROWS, :, :].bitcast(I32),
                 dy_scales[:, QUAD_ROWS * quad : QUAD_ROWS * (quad + 1), :].rearrange("s b t -> b s t").bitcast(I32),
@@ -81,7 +82,7 @@ def tile_moe_seb_relu_kernel(
         nc.sync.dma_start(dy_w[:, 1, :], dy_rows[:, 1, :])
         nc.sync.dma_start(w2_w[0][:].bitcast(I32), w2t_words[0].rearrange("s p n -> p s n").bitcast(I32))
         for f in range(E):
-            for quad in range(QUADS):
+            for quad in QUAD_ORDER:
                 nc.sync.dma_start(
                     w2_s[QUAD * quad : QUAD * quad + QUAD_ROWS, PASSES * f : PASSES * (f + 1), :].bitcast(I32),
                     w2t_scales[f, :, QUAD_ROWS * quad : QUAD_ROWS * (quad + 1), :].rearrange("s b i -> b s i").bitcast(I32),
@@ -223,7 +224,8 @@ def tile_moe_seb_relu_kernel(
         da_bf0 = keep.tile([P, C, PACK], BF16, name="da_bf0", tag="rows", align_bytes=64)
         for t in range(0, PACK, 2):
             interleave(da_bf0[:, :, t : t + 2], da[0][:, t : t + 2, :])
-        gather_dc(1, PACK - 1, 0, C)
+        gather_dc(1, 3, 0, C)
+        gather_dc(1, 2, P, C)
         w1_w = keep.tile([P, E, K], U32, name="w1_w", tag="slope0", align_bytes=64)
         nc.vector.quantize_mx(
             out=w1_w[:].rearrange("p e k -> p (e k)").bitcast(FP8X4),
@@ -232,7 +234,8 @@ def tile_moe_seb_relu_kernel(
         )
         da_w0 = keep.tile([P, C], U32, name="da_w0", tag="handed", align_bytes=64)
         quantize_da(0, da_bf0, da_w0)
-        for t in (2, 0, 1):
+        gather_dc(1, 2, 0, P)
+        for t in range(2):
             gather_dc(1, t, 0, C)
         nc.scalar.copy(dx_slots[:, 0, 0, :], first_layer(0, 0, 0, C, w1_w, da_w0)[:])
         second_bank = first_layer(0, 1, 0, C, w1_w, da_w0)

@@ -25,6 +25,9 @@ LANES = 16
 QUADS, QUAD, QUAD_ROWS = 4, 32, 4
 QUAD_ORDER = (0, 2, 1, 3)
 GROUPS = T // P
+GROUPS_PER_EXPERT = C // P
+SECOND_BANK_GROUP = 2
+PAIR = PACK // 2
 
 PLANE_RUNS = [
     [(0, 1), (1, 2), (2, PACK)],
@@ -44,7 +47,7 @@ def tile_moe_seb_relu_kernel(
 
     with ExitStack() as ctx:
         keep = ctx.enter_context(tc.tile_pool(name="keep", bufs=1))
-        once = ctx.enter_context(tc.tile_pool(name="once", bufs=1))
+        stage = ctx.enter_context(tc.tile_pool(name="stage", bufs=1))
         mm_psum = ctx.enter_context(tc.psum_pool(name="mm_psum", bufs=1))
         tr_psum = ctx.enter_context(tc.psum_pool(name="tr_psum", bufs=3))
         out_psum = ctx.enter_context(tc.psum_pool(name="out_psum", bufs=3))
@@ -63,12 +66,12 @@ def tile_moe_seb_relu_kernel(
 
         nc.gpsimd.memset(dy_s[:].bitcast(I32), 0)
         w2_s_words = w2_s[:].rearrange("p a i -> p (a i)").bitcast(I32)
-        odd = E * PASSES * H // 8 + 1
+        odd = w2_s_words.shape[1] // 2 + 1
         nc.vector.memset(w2_s_words[:, :odd], 0)
         nc.vector.memset(w2_s_words[:, odd:], 0)
 
         def load_gates(f):
-            for c in range(f * C // P, (f + 1) * C // P):
+            for c in range(f * GROUPS_PER_EXPERT, (f + 1) * GROUPS_PER_EXPERT):
                 nc.sync.dma_start(q_col[c][:], gate2[0, c * P : (c + 1) * P].rearrange("(p o) -> p o", o=1))
 
         dy_rows = dy_words.rearrange("s p t d -> p s (t d)").bitcast(I32)
@@ -94,8 +97,8 @@ def tile_moe_seb_relu_kernel(
         nc.scalar.activation(ident[:], ident_made[:], ACT.Copy)
         nc.sync.dma_start(w2_w[1][:].bitcast(I32), w2t_words[1].rearrange("s p n -> p s n").bitcast(I32))
         a_rows = a.rearrange("(p t) j -> p t j", t=PACK)
-        for t0 in range(0, PACK, PACK // 2):
-            nc.sync.dma_start(a_sb[:, t0 : t0 + PACK // 2, :], a_rows[:, t0 : t0 + PACK // 2, :])
+        for t0 in range(0, PACK, PAIR):
+            nc.sync.dma_start(a_sb[:, t0 : t0 + PAIR, :], a_rows[:, t0 : t0 + PAIR, :])
         load_gates(1)
         nc.sync.dma_start(g1[:], gate1)
         for e in range(E):
@@ -109,7 +112,7 @@ def tile_moe_seb_relu_kernel(
         def slot_scales(s, lo, hi):
             return first_s[s][:, lo:hi] if hi <= P else rest_s[s][:, lo - P : hi - P]
 
-        dc = [keep.tile([P, T], F32, name="dc%d" % t, tag="dc%d" % t, align_bytes=64) for t in range(PACK)]
+        dc = [keep.tile([P, T], F32, name="dc%d" % t, align_bytes=64) for t in range(PACK)]
         dc_slots = keep.tile([P, E, PACK, C], F32, name="dc_slots")
 
         def gather_words(s, lo, hi):
@@ -119,9 +122,9 @@ def tile_moe_seb_relu_kernel(
             nc.vector.tensor_copy(slot_scales(s, lo, hi), dy_s[:, s, :].indirect(entries(list2, lo, hi)))
 
         def second_layer(c):
-            f, half = divmod(c, C // P)
+            f, half = divmod(c, GROUPS_PER_EXPERT)
             cols = slice(c * P, (c + 1) * P)
-            acc = mm_psum.tile([P, H], F32, name="acc", tag="second" if c == 2 else "acc")
+            acc = mm_psum.tile([P, H], F32, name="acc", tag="second" if c == SECOND_BANK_GROUP else "acc")
             for s in range(PASSES):
                 nc.tensor.matmul_mx(
                     out=acc[:],
@@ -132,7 +135,7 @@ def tile_moe_seb_relu_kernel(
                     start=(s == 0),
                     stop=(s == PASSES - 1),
                 )
-            gated = once.tile([P, PACK, P], F32, name="gated", tag="stage%d" % c, align_bytes=64)
+            gated = stage.tile([P, PACK, P], F32, name="gated", tag="stage%d" % c, align_bytes=64)
             by_plane = acc[:].rearrange("p (m t) -> p t m", t=PACK)
             for t0, t1 in PLANE_RUNS[c]:
                 nc.scalar.activation(gated[:, t0:t1, :], by_plane[:, t0:t1, :], ACT.Copy, scale=q_col[c][:])
@@ -160,10 +163,9 @@ def tile_moe_seb_relu_kernel(
         gather_scales(1, P, T)
         for c in range(1, GROUPS):
             second_layer(c)
-        scatter_dc(0, 0, P)
-        scatter_dc(0, P, C)
-        scatter_dc(1, 0, P)
-        scatter_dc(1, P, C)
+        for f in range(E):
+            for lo in range(0, C, P):
+                scatter_dc(f, lo, lo + P)
 
         slope = [keep.tile([P, PACK, C], F32, name="slope%d" % e, tag="slope%d" % e, align_bytes=64) for e in range(E)]
         clipped = keep.tile([P, PACK, T], F32, name="clipped", tag="clipped", align_bytes=64)
@@ -172,7 +174,7 @@ def tile_moe_seb_relu_kernel(
             nc.gpsimd.tensor_scalar(clipped[:, :, slots], a_sb[:, :, slots], 1.0, 0.0, ALU.min, ALU.max)
         for e in range(E):
             slots = slice(e * C, (e + 1) * C)
-            mask = once.tile([P, PACK, C], F32, name="mask", tag="stage%d" % (2 + e), align_bytes=64)
+            mask = stage.tile([P, PACK, C], F32, name="mask", tag="stage%d" % (GROUPS - E + e), align_bytes=64)
             nc.scalar.activation(mask[:], clipped[:, :, slots], ACT.Sign)
             nc.gpsimd.tensor_tensor(
                 slope[e][:], mask[:], g1[:, slots].unsqueeze(1).to_broadcast([P, PACK, C]), ALU.mult
@@ -188,15 +190,19 @@ def tile_moe_seb_relu_kernel(
         for e in range(E):
             interleave(w1_bf[:, e, :, :], w1_raw[:, e, :, :])
 
-        shift = C + C // 2
-        da_all = keep.tile([P, PACK * C + shift], F32, name="da_all", tag="da", align_bytes=64)
-        da = [da_all[:, shift * e : shift * e + PACK * C].rearrange("p (t j) -> p t j", t=PACK) for e in range(E)]
+        da_all = keep.tile([P, PACK + PAIR, C], F32, name="da_all", tag="da", align_bytes=64)
+        da = [da_all[:, PAIR * e : PAIR * e + PACK, :] for e in range(E)]
         da_s = keep.tile([P, E, C], U8, name="da_s", align_bytes=64)
         dx_slots = keep.tile([P, E, K // P, C], F32, name="dx_slots")
 
-        def gather_dc(e, t, lo, hi):
+        def gather_dc(e, t):
             nc.vector.tensor_tensor(
-                da[e][:, t, lo:hi], dc[t][:].indirect(entries(list1, e * C + lo, e * C + hi)), slope[e][:, t, lo:hi], ALU.mult
+                da[e][:, t, :], dc[t][:].indirect(entries(list1, e * C, (e + 1) * C)), slope[e][:, t, :], ALU.mult
+            )
+
+        def quantize_w1(e, w1_w):
+            nc.vector.quantize_mx(
+                out=w1_w[:].bitcast(FP8X4), scales=w1_s[:, e, :], in_=w1_bf[:, e, :, :].rearrange("p k t -> p (k t)")
             )
 
         def quantize_da(e, da_bf, da_w):
@@ -207,7 +213,7 @@ def tile_moe_seb_relu_kernel(
             acc1 = out_psum.tile([P, hi - lo], F32, name="acc1")
             nc.tensor.matmul_mx(
                 out=acc1[:],
-                lhsT=w1_w[:, e, cols].bitcast(FP8X4),
+                lhsT=w1_w[:, cols].bitcast(FP8X4),
                 lhsT_scale=w1_s[:, e, cols],
                 rhs=da_w[:, lo:hi].bitcast(FP8X4),
                 rhs_scale=da_s[:, e, lo:hi],
@@ -220,28 +226,24 @@ def tile_moe_seb_relu_kernel(
             nc.vector.tensor_copy(window[:].indirect(entries(list1, e * C + lo, e * C + hi)), dx_slots[:, e, kt, lo:hi])
 
         for t in range(PACK):
-            gather_dc(0, t, 0, C)
+            gather_dc(0, t)
         da_bf0 = keep.tile([P, C, PACK], BF16, name="da_bf0", tag="rows", align_bytes=64)
-        for t in range(0, PACK, 2):
-            interleave(da_bf0[:, :, t : t + 2], da[0][:, t : t + 2, :])
-        gather_dc(1, 3, 0, C)
-        gather_dc(1, 2, P, C)
-        w1_w = keep.tile([P, E, K], U32, name="w1_w", tag="slope0", align_bytes=64)
-        nc.vector.quantize_mx(
-            out=w1_w[:].rearrange("p e k -> p (e k)").bitcast(FP8X4),
-            scales=w1_s[:].rearrange("p e k -> p (e k)"),
-            in_=w1_bf[:].rearrange("p e k t -> p (e k t)"),
-        )
+        for t0 in range(0, PACK, PAIR):
+            interleave(da_bf0[:, :, t0 : t0 + PAIR], da[0][:, t0 : t0 + PAIR, :])
+        for t in range(PAIR, PACK):
+            gather_dc(1, t)
+        w1_w0 = keep.tile([P, K], U32, name="w1_w0", tag="slope0", align_bytes=64)
+        quantize_w1(0, w1_w0)
         da_w0 = keep.tile([P, C], U32, name="da_w0", tag="handed", align_bytes=64)
         quantize_da(0, da_bf0, da_w0)
-        gather_dc(1, 2, 0, P)
-        for t in range(2):
-            gather_dc(1, t, 0, C)
-        nc.scalar.copy(dx_slots[:, 0, 0, :], first_layer(0, 0, 0, C, w1_w, da_w0)[:])
-        second_bank = first_layer(0, 1, 0, C, w1_w, da_w0)
+        for t in range(PAIR):
+            gather_dc(1, t)
+        w1_w1 = keep.tile([P, K], U32, name="w1_w1", tag="rows", align_bytes=64)
+        quantize_w1(1, w1_w1)
+        nc.scalar.copy(dx_slots[:, 0, 0, :], first_layer(0, 0, 0, C, w1_w0, da_w0)[:])
+        second_bank = first_layer(0, 1, 0, C, w1_w0, da_w0)
         da_bf1 = keep.tile([P, C, PACK], BF16, name="da_bf1", tag="handed", align_bytes=64)
-        for t in (2, 0):
-            interleave(da_bf1[:, :, t : t + 2], da[1][:, t : t + 2, :])
+        interleave(da_bf1[:], da[1])
         nc.scalar.copy(dx_slots[:, 0, 1, :], second_bank[:])
         dx0 = keep.tile([P, T], F32, name="dx0")
         scatter_dx(0, 0, 0, C, dx0)
@@ -249,7 +251,7 @@ def tile_moe_seb_relu_kernel(
         quantize_da(1, da_bf1, da_w1)
         for lo in range(0, C, P):
             for kt in range(K // P):
-                nc.scalar.copy(dx_slots[:, 1, kt, lo : lo + P], first_layer(1, kt, lo, lo + P, w1_w, da_w1)[:])
+                nc.scalar.copy(dx_slots[:, 1, kt, lo : lo + P], first_layer(1, kt, lo, lo + P, w1_w1, da_w1)[:])
         dx1 = keep.tile([P, T], F32, name="dx1", tag="da", align_bytes=64)
         scatter_dx(0, 1, 0, C, dx1)
         for lo in range(0, C, P):

@@ -1,7 +1,6 @@
 from contextlib import ExitStack
 
 import concourse.mybir as mybir
-from concourse.masks import make_identity
 
 K, T, H, N = 256, 512, 512, 1024
 E, C = 2, 256
@@ -24,17 +23,11 @@ PASSES = N // (P * PACK)
 LANES = 16
 QUADS, QUAD, QUAD_ROWS = 4, 32, 4
 QUAD_ORDER = (0, 2, 1, 3)
+BLOCKS, RUN = H // 32, 8
 GROUPS = T // P
 GROUPS_PER_EXPERT = C // P
-SECOND_BANK_GROUP = 2
-PAIR = PACK // 2
-
-PLANE_RUNS = [
-    [(0, 1), (1, 2), (2, PACK)],
-    [(0, 1), (1, PACK)],
-    [(0, PACK)],
-    [(0, PACK)],
-]
+VECTOR_PLANE = PACK - 1
+EARLY_PLANES, LAST_PLANE = (3, 0, 1), 2
 
 
 def tile_moe_seb_relu_kernel(
@@ -47,32 +40,25 @@ def tile_moe_seb_relu_kernel(
 
     with ExitStack() as ctx:
         keep = ctx.enter_context(tc.tile_pool(name="keep", bufs=1))
-        stage = ctx.enter_context(tc.tile_pool(name="stage", bufs=1))
-        mm_psum = ctx.enter_context(tc.psum_pool(name="mm_psum", bufs=1))
-        tr_psum = ctx.enter_context(tc.psum_pool(name="tr_psum", bufs=3))
-        out_psum = ctx.enter_context(tc.psum_pool(name="out_psum", bufs=3))
+        psum = ctx.enter_context(tc.psum_pool(name="psum", bufs=8))
 
         list2 = keep.tile([P, T // LANES], U16, name="list2")
         list1 = keep.tile([P, T // LANES], U16, name="list1")
         dy_w = keep.tile([P, PASSES, T], I32, name="dy_w", align_bytes=64)
         dy_s = keep.tile([P, PASSES, T], U8, name="dy_s", align_bytes=64)
-        w2_w = [keep.tile([P, PASSES, 2 * H], U8, name="w2_w%d" % f, align_bytes=64) for f in range(E)]
-        w2_s = keep.tile([P, E * PASSES, H], U8, name="w2_s", align_bytes=64)
-        q_col = [keep.tile([P, 1], F32, name="q_col%d" % c) for c in range(GROUPS)]
-        ident = keep.tile([P, P], F32, name="ident")
+        w2_w_raw = [keep.tile([P, PASSES, 2 * H], U8, name="w2_w_raw%d" % f, align_bytes=64) for f in range(E)]
+        w2_s_raw = keep.tile([P, E * PASSES, H], U8, name="w2_s_raw", align_bytes=64)
+        q = [keep.tile([P, C], F32, name="q%d" % f, tag="q%d" % f, align_bytes=64) for f in range(E)]
+        q_first = keep.tile([P, C], F32, name="q_first", tag="first", align_bytes=64)
         a_sb = keep.tile([P, PACK, T], F32, name="a_sb")
         g1 = keep.tile([P, T], F32, name="g1")
-        w1_raw = keep.tile([P, E, PACK, K], F32, name="w1_raw", tag="rows", align_bytes=64)
+        w1_raw = [keep.tile([P, PACK, K], F32, name="w1_raw%d" % e) for e in range(E)]
 
         nc.gpsimd.memset(dy_s[:].bitcast(I32), 0)
-        w2_s_words = w2_s[:].rearrange("p a i -> p (a i)").bitcast(I32)
+        w2_s_words = w2_s_raw[:].rearrange("p a i -> p (a i)").bitcast(I32)
         odd = w2_s_words.shape[1] // 2 + 1
         nc.vector.memset(w2_s_words[:, :odd], 0)
         nc.vector.memset(w2_s_words[:, odd:], 0)
-
-        def load_gates(f):
-            for c in range(f * GROUPS_PER_EXPERT, (f + 1) * GROUPS_PER_EXPERT):
-                nc.sync.dma_start(q_col[c][:], gate2[0, c * P : (c + 1) * P].rearrange("(p o) -> p o", o=1))
 
         dy_rows = dy_words.rearrange("s p t d -> p s (t d)").bitcast(I32)
         nc.sync.dma_start(dy_w[:, 0, :], dy_rows[:, 0, :])
@@ -83,179 +69,178 @@ def tile_moe_seb_relu_kernel(
                 dy_scales[:, QUAD_ROWS * quad : QUAD_ROWS * (quad + 1), :].rearrange("s b t -> b s t").bitcast(I32),
             )
         nc.sync.dma_start(dy_w[:, 1, :], dy_rows[:, 1, :])
-        nc.sync.dma_start(w2_w[0][:].bitcast(I32), w2t_words[0].rearrange("s p n -> p s n").bitcast(I32))
-        for f in range(E):
-            for quad in QUAD_ORDER:
-                nc.sync.dma_start(
-                    w2_s[QUAD * quad : QUAD * quad + QUAD_ROWS, PASSES * f : PASSES * (f + 1), :].bitcast(I32),
-                    w2t_scales[f, :, QUAD_ROWS * quad : QUAD_ROWS * (quad + 1), :].rearrange("s b i -> b s i").bitcast(I32),
-                )
-            if f == 0:
-                load_gates(0)
-        ident_made = keep.tile([P, P], F32, name="ident_made")
-        make_identity(nc, ident_made[:])
-        nc.scalar.activation(ident[:], ident_made[:], ACT.Copy)
-        nc.sync.dma_start(w2_w[1][:].bitcast(I32), w2t_words[1].rearrange("s p n -> p s n").bitcast(I32))
-        a_rows = a.rearrange("(p t) j -> p t j", t=PACK)
-        for t0 in range(0, PACK, PAIR):
-            nc.sync.dma_start(a_sb[:, t0 : t0 + PAIR, :], a_rows[:, t0 : t0 + PAIR, :])
-        load_gates(1)
+        w2_rows = w2t_words.rearrange("f s p n -> f p s n").bitcast(I32)
+        nc.sync.dma_start(w2_w_raw[0][:].bitcast(I32), w2_rows[0])
+        for quad in QUAD_ORDER:
+            nc.sync.dma_start(
+                w2_s_raw[QUAD * quad : QUAD * quad + QUAD_ROWS, :, :].bitcast(I32),
+                w2t_scales[:, :, QUAD_ROWS * quad : QUAD_ROWS * (quad + 1), :].rearrange("f s b i -> b (f s) i").bitcast(I32),
+            )
+        nc.sync.dma_start(w2_w_raw[1][:].bitcast(I32), w2_rows[1])
+        nc.sync.dma_start(q_first[:], gate2[:, :C])
+        nc.sync.dma_start(q[0][:], gate2[:, :C])
+        nc.sync.dma_start(q[1][:], gate2[:, C:])
+
+        def load_planes(planes, rows):
+            by_plane = rows.rearrange("(b t u) c -> t b u c", t=PACK, u=RUN)
+            for t in range(PACK):
+                nc.sync.dma_start(planes[:, t, :], by_plane[t])
+
+        load_planes(w1_raw[0], w1t[0])
+        load_planes(a_sb, a)
         nc.sync.dma_start(g1[:], gate1)
-        for e in range(E):
-            nc.sync.dma_start(w1_raw[:, e, :, :], w1t[e].rearrange("(p t) k -> p t k", t=PACK))
         nc.sync.dma_start(list1[:], offs)
+        load_planes(w1_raw[1], w1t[1])
+
+        w2_w = [keep.tile([P, PASSES, PACK, 2 * P], U8, name="w2_w%d" % f, align_bytes=64) for f in range(E)]
+        w2_s = [keep.tile([P, PASSES, PACK, P], U8, name="w2_s%d" % f, align_bytes=64) for f in range(E)]
+
+        def sort_by_plane(planes, raw):
+            nc.scalar.copy(
+                planes.bitcast(U32).rearrange("p s t (b w) -> p s t b w", b=BLOCKS),
+                raw.bitcast(U32).rearrange("p s (b t w) -> p s t b w", b=BLOCKS, t=PACK),
+            )
+
+        for f in range(E):
+            passes = slice(PASSES * f, PASSES * (f + 1))
+            sort_by_plane(w2_w[f][:], w2_w_raw[f][:])
+            sort_by_plane(w2_s[f][:], w2_s_raw[:, passes, :])
 
         slot_w = [keep.tile([P, T], U32, name="slot_w%d" % s, align_bytes=64) for s in range(PASSES)]
-        first_s = [keep.tile([P, P], U8, name="first_s%d" % s, tag="slot_s%d" % s, align_bytes=64) for s in range(PASSES)]
-        rest_s = [keep.tile([P, T - P], U8, name="rest_s%d" % s, tag="slot_s%d" % s, align_bytes=64) for s in range(PASSES)]
-
-        def slot_scales(s, lo, hi):
-            return first_s[s][:, lo:hi] if hi <= P else rest_s[s][:, lo - P : hi - P]
-
+        slot_s = [
+            keep.tile([P, PASSES, C], U8, name="slot_s0", align_bytes=64),
+            keep.tile([P, PASSES, C], U8, name="slot_s1", tag="first", align_bytes=64),
+        ]
         dc = [keep.tile([P, T], F32, name="dc%d" % t, align_bytes=64) for t in range(PACK)]
-        dc_slots = keep.tile([P, E, PACK, C], F32, name="dc_slots")
+        dc_slots = [
+            [keep.tile([P, C], F32, name="dc_slots%d%d" % (f, t), tag="dc_slots%d%d" % (f, t), align_bytes=64) for t in range(PACK)]
+            for f in range(E)
+        ]
 
-        def gather_words(s, lo, hi):
+        def gather_words(f, s):
+            lo, hi = f * C, (f + 1) * C
             nc.vector.tensor_copy(slot_w[s][:, lo:hi], dy_w[:, s, :].bitcast(U32).indirect(entries(list2, lo, hi)))
 
-        def gather_scales(s, lo, hi):
-            nc.vector.tensor_copy(slot_scales(s, lo, hi), dy_s[:, s, :].indirect(entries(list2, lo, hi)))
+        def gather_scales(f, s):
+            nc.vector.tensor_copy(slot_s[f][:, s, :], dy_s[:, s, :].indirect(entries(list2, f * C, (f + 1) * C)))
 
-        def second_layer(c):
-            f, half = divmod(c, GROUPS_PER_EXPERT)
-            cols = slice(c * P, (c + 1) * P)
-            acc = mm_psum.tile([P, H], F32, name="acc", tag="second" if c == SECOND_BANK_GROUP else "acc")
+        def second_layer(f, t):
+            acc = psum.tile([P, C], F32, name="acc", tag="bank")
             for s in range(PASSES):
                 nc.tensor.matmul_mx(
                     out=acc[:],
-                    lhsT=slot_w[s][:, cols].bitcast(FP8X4),
-                    lhsT_scale=slot_scales(s, c * P, (c + 1) * P),
-                    rhs=w2_w[f][:, s, :].bitcast(FP4X4),
-                    rhs_scale=w2_s[:, PASSES * f + s, :],
+                    lhsT=w2_w[f][:, s, t, :].bitcast(FP4X4),
+                    lhsT_scale=w2_s[f][:, s, t, :],
+                    rhs=slot_w[s][:, f * C : (f + 1) * C].bitcast(FP8X4),
+                    rhs_scale=slot_s[f][:, s, :],
                     start=(s == 0),
                     stop=(s == PASSES - 1),
                 )
-            gated = stage.tile([P, PACK, P], F32, name="gated", tag="stage%d" % c, align_bytes=64)
-            by_plane = acc[:].rearrange("p (m t) -> p t m", t=PACK)
-            for t0, t1 in PLANE_RUNS[c]:
-                nc.scalar.activation(gated[:, t0:t1, :], by_plane[:, t0:t1, :], ACT.Copy, scale=q_col[c][:])
-            for t0, t1 in PLANE_RUNS[c]:
-                if c == 0 and t1 == PACK:
-                    turned = mm_psum.tile([P, t1 - t0, P], F32, name="turned", tag="second")
-                else:
-                    turned = tr_psum.tile([P, t1 - t0, P], F32, name="turned", tag="turned")
-                for t in range(t0, t1):
-                    nc.tensor.transpose(turned[:, t - t0, :], gated[:, t, :], ident[:])
-                nc.scalar.copy(dc_slots[:, f, t0:t1, half * P : (half + 1) * P], turned[:])
+            nc.vector.tensor_tensor(dc_slots[f][t][:], acc[:], (q_first if f == 0 and t == 0 else q[f])[:], ALU.mult)
 
-        def scatter_dc(f, lo, hi):
-            for t in range(PACK):
-                nc.vector.tensor_copy(dc[t][:].indirect(entries(list2, f * C + lo, f * C + hi)), dc_slots[:, f, t, lo:hi])
+        def scatter(on_vector, window, offsets, values):
+            if on_vector:
+                nc.vector.tensor_copy(window[:].indirect(offsets), values)
+            else:
+                nc.scalar.activation(window[:].indirect(offsets), values, ACT.Copy)
 
-        gather_words(0, 0, P)
-        gather_words(0, P, T)
-        gather_words(1, 0, P)
-        gather_scales(0, 0, P)
-        gather_scales(1, 0, P)
-        second_layer(0)
-        gather_words(1, P, T)
-        gather_scales(0, P, T)
-        gather_scales(1, P, T)
-        for c in range(1, GROUPS):
-            second_layer(c)
-        for f in range(E):
-            for lo in range(0, C, P):
-                scatter_dc(f, lo, lo + P)
-
-        slope = [keep.tile([P, PACK, C], F32, name="slope%d" % e, tag="slope%d" % e, align_bytes=64) for e in range(E)]
-        clipped = keep.tile([P, PACK, T], F32, name="clipped", tag="clipped", align_bytes=64)
-        for e in range(E):
-            slots = slice(e * C, (e + 1) * C)
-            nc.gpsimd.tensor_scalar(clipped[:, :, slots], a_sb[:, :, slots], 1.0, 0.0, ALU.min, ALU.max)
-        for e in range(E):
-            slots = slice(e * C, (e + 1) * C)
-            mask = stage.tile([P, PACK, C], F32, name="mask", tag="stage%d" % (GROUPS - E + e), align_bytes=64)
-            nc.scalar.activation(mask[:], clipped[:, :, slots], ACT.Sign)
-            nc.gpsimd.tensor_tensor(
-                slope[e][:], mask[:], g1[:, slots].unsqueeze(1).to_broadcast([P, PACK, C]), ALU.mult
-            )
-
-        def interleave(columns, planes):
-            nc.scalar.copy(
-                columns.rearrange("p (c i) t -> p c t i", i=PACK), planes.rearrange("p t (c i) -> p c t i", i=PACK)
-            )
-
-        w1_bf = keep.tile([P, E, K, PACK], BF16, name="w1_bf", tag="clipped", align_bytes=64)
-        w1_s = keep.tile([P, E, K], U8, name="w1_s", align_bytes=64)
-        for e in range(E):
-            interleave(w1_bf[:, e, :, :], w1_raw[:, e, :, :])
-
-        da_all = keep.tile([P, PACK + PAIR, C], F32, name="da_all", tag="da", align_bytes=64)
-        da = [da_all[:, PAIR * e : PAIR * e + PACK, :] for e in range(E)]
-        da_s = keep.tile([P, E, C], U8, name="da_s", align_bytes=64)
-        dx_slots = keep.tile([P, E, K // P, C], F32, name="dx_slots")
-
-        def gather_dc(e, t):
-            nc.vector.tensor_tensor(
-                da[e][:, t, :], dc[t][:].indirect(entries(list1, e * C, (e + 1) * C)), slope[e][:, t, :], ALU.mult
-            )
-
-        def quantize_w1(e, w1_w):
-            nc.vector.quantize_mx(
-                out=w1_w[:].bitcast(FP8X4), scales=w1_s[:, e, :], in_=w1_bf[:, e, :, :].rearrange("p k t -> p (k t)")
-            )
-
-        def quantize_da(e, da_bf, da_w):
-            nc.vector.quantize_mx(out=da_w[:].bitcast(FP8X4), scales=da_s[:, e, :], in_=da_bf[:].rearrange("p j t -> p (j t)"))
-
-        def first_layer(e, kt, lo, hi, w1_w, da_w):
-            cols = slice(kt * P, (kt + 1) * P)
-            acc1 = out_psum.tile([P, hi - lo], F32, name="acc1")
-            nc.tensor.matmul_mx(
-                out=acc1[:],
-                lhsT=w1_w[:, cols].bitcast(FP8X4),
-                lhsT_scale=w1_s[:, e, cols],
-                rhs=da_w[:, lo:hi].bitcast(FP8X4),
-                rhs_scale=da_s[:, e, lo:hi],
-                start=True,
-                stop=True,
-            )
-            return acc1
-
-        def scatter_dx(e, kt, lo, hi, window):
-            nc.vector.tensor_copy(window[:].indirect(entries(list1, e * C + lo, e * C + hi)), dx_slots[:, e, kt, lo:hi])
-
+        for s in range(PASSES):
+            gather_words(0, s)
+        for s in range(PASSES):
+            gather_scales(0, s)
+        for s in range(PASSES):
+            gather_words(1, s)
+        second_layer(0, 0)
+        for s in range(PASSES):
+            gather_scales(1, s)
+        for t in range(1, PACK):
+            second_layer(0, t)
         for t in range(PACK):
-            gather_dc(0, t)
-        da_bf0 = keep.tile([P, C, PACK], BF16, name="da_bf0", tag="rows", align_bytes=64)
-        for t0 in range(0, PACK, PAIR):
-            interleave(da_bf0[:, :, t0 : t0 + PAIR], da[0][:, t0 : t0 + PAIR, :])
-        for t in range(PAIR, PACK):
-            gather_dc(1, t)
-        w1_w0 = keep.tile([P, K], U32, name="w1_w0", tag="slope0", align_bytes=64)
-        quantize_w1(0, w1_w0)
-        da_w0 = keep.tile([P, C], U32, name="da_w0", tag="handed", align_bytes=64)
-        quantize_da(0, da_bf0, da_w0)
-        for t in range(PAIR):
-            gather_dc(1, t)
-        w1_w1 = keep.tile([P, K], U32, name="w1_w1", tag="rows", align_bytes=64)
-        quantize_w1(1, w1_w1)
-        nc.scalar.copy(dx_slots[:, 0, 0, :], first_layer(0, 0, 0, C, w1_w0, da_w0)[:])
-        second_bank = first_layer(0, 1, 0, C, w1_w0, da_w0)
-        da_bf1 = keep.tile([P, C, PACK], BF16, name="da_bf1", tag="handed", align_bytes=64)
-        interleave(da_bf1[:], da[1])
-        nc.scalar.copy(dx_slots[:, 0, 1, :], second_bank[:])
-        dx0 = keep.tile([P, T], F32, name="dx0")
-        scatter_dx(0, 0, 0, C, dx0)
-        da_w1 = keep.tile([P, C], U32, name="da_w1", align_bytes=64)
-        quantize_da(1, da_bf1, da_w1)
-        for lo in range(0, C, P):
+            second_layer(1, t)
+        for f in range(E):
+            for t in range(PACK):
+                scatter(t == VECTOR_PLANE, dc[t], entries(list2, f * C, (f + 1) * C), dc_slots[f][t][:])
+
+        slope = [keep.tile([P, PACK, C], F32, name="slope%d" % e, tag="slope") for e in range(E)]
+        da = [keep.tile([P, PACK, C], F32, name="da%d" % e) for e in range(E)]
+        w1_bf = [
+            keep.tile([P, K, PACK], BF16, name="w1_bf0", align_bytes=64),
+            keep.tile([P, K, PACK], BF16, name="w1_bf1", tag="dc_slots1%d" % LAST_PLANE, align_bytes=64),
+        ]
+        w1_w = [keep.tile([P, K], U32, name="w1_w%d" % e, align_bytes=64) for e in range(E)]
+        w1_s = [keep.tile([P, K], U8, name="w1_s%d" % e, align_bytes=64) for e in range(E)]
+        dx_slots = keep.tile([P, GROUPS, K // P, P], F32, name="dx_slots")
+        dx = [keep.tile([P, T], F32, name="dx%d" % kt) for kt in range(K // P)]
+
+        def make_slope(e):
+            slots = slice(e * C, (e + 1) * C)
+            nc.vector.scalar_tensor_tensor(
+                slope[e][:], a_sb[:, :, slots], 0.0, g1[:, slots].unsqueeze(1).to_broadcast([P, PACK, C]), ALU.is_gt, ALU.mult
+            )
+
+        def interleave(copy, columns, planes):
+            copy(columns.rearrange("p (c i) t -> p c t i", i=PACK), planes.rearrange("p t (c i) -> p c t i", i=PACK))
+
+        def round_on_gpsimd(rounded, values):
+            nc.gpsimd.tensor_scalar(rounded, values, 1.0, 0.0, ALU.mult, ALU.add)
+
+        def quantize(words, scales, columns):
+            nc.vector.quantize_mx(out=words.bitcast(FP8X4), scales=scales, in_=columns.rearrange("p c t -> p (c t)"))
+
+        def gather_dc(e, t, lo, hi):
+            nc.vector.tensor_tensor(
+                da[e][:, t, lo:hi], dc[t][:].indirect(entries(list1, e * C + lo, e * C + hi)), slope[e][:, t, lo:hi], ALU.mult
+            )
+
+        def first_layer(c):
+            e, half = divmod(c, GROUPS_PER_EXPERT)
+            lo = half * P
+            gather_dc(e, LAST_PLANE, lo, lo + P)
+            da_bf = keep.tile([P, P, PACK], BF16, name="da_bf%d" % c, align_bytes=64)
+            da_w = keep.tile([P, P], U32, name="da_w%d" % c, align_bytes=64)
+            da_s = keep.tile([P, P], U8, name="da_s%d" % c, align_bytes=64)
+            interleave(nc.vector.tensor_copy, da_bf[:], da[e][:, :, lo : lo + P])
+            quantize(da_w[:], da_s[:], da_bf[:])
+            last = c == GROUPS - 1
+            if last:
+                banks = [psum.tile([P, P], F32, name="acc1", tag="bank")[:] for kt in range(K // P)]
+            else:
+                both = psum.tile([P, K // P, P], F32, name="acc1", tag="bank")
+                banks = [both[:, kt, :] for kt in range(K // P)]
             for kt in range(K // P):
-                nc.scalar.copy(dx_slots[:, 1, kt, lo : lo + P], first_layer(1, kt, lo, lo + P, w1_w1, da_w1)[:])
-        dx1 = keep.tile([P, T], F32, name="dx1", tag="da", align_bytes=64)
-        scatter_dx(0, 1, 0, C, dx1)
-        for lo in range(0, C, P):
-            for kt, window in enumerate([dx0, dx1]):
-                scatter_dx(1, kt, lo, lo + P, window)
-        for kt, window in enumerate([dx0, dx1]):
-            nc.sync.dma_start(out[kt * P : (kt + 1) * P, :], window[:])
+                cols = slice(kt * P, (kt + 1) * P)
+                nc.tensor.matmul_mx(
+                    out=banks[kt],
+                    lhsT=w1_w[e][:, cols].bitcast(FP8X4),
+                    lhsT_scale=w1_s[e][:, cols],
+                    rhs=da_w[:].bitcast(FP8X4),
+                    rhs_scale=da_s[:],
+                    start=True,
+                    stop=True,
+                )
+            if last:
+                for kt in (1, 0):
+                    nc.vector.tensor_copy(dx_slots[:, c, kt, :], banks[kt])
+            else:
+                nc.scalar.copy(dx_slots[:, c, :, :], both[:])
+
+        def scatter_dx(c, kt):
+            scatter(c == GROUPS - 1, dx[kt], entries(list1, c * P, (c + 1) * P), dx_slots[:, c, kt, :])
+
+        round_on_gpsimd(w1_bf[0][:], w1_raw[0][:].rearrange("p t k -> p k t"))
+        interleave(nc.scalar.copy, w1_bf[1][:], w1_raw[1][:])
+        for e in range(E):
+            make_slope(e)
+            for t in EARLY_PLANES:
+                gather_dc(e, t, 0, C)
+            quantize(w1_w[e][:], w1_s[e][:], w1_bf[e][:])
+            for half in range(GROUPS_PER_EXPERT):
+                first_layer(e * GROUPS_PER_EXPERT + half)
+                if e == 0:
+                    for kt in range(K // P):
+                        scatter_dx(half, kt)
+        for kt in range(K // P):
+            scatter_dx(GROUPS - 2, kt)
+            scatter_dx(GROUPS - 1, 1 - kt)
+        for kt in range(K // P):
+            nc.sync.dma_start(out[kt * P : (kt + 1) * P, :], dx[kt][:])

@@ -26,8 +26,9 @@ QUAD_ORDER = (0, 2, 1, 3)
 BLOCKS, RUN = H // 32, 8
 GROUPS = T // P
 GROUPS_PER_EXPERT = C // P
-VECTOR_PLANE = PACK - 1
-EARLY_PLANES, LAST_PLANE = (3, 0, 1), 2
+VECTOR_SLOTS = 320
+SCALAR_ROUNDS = (1, 2)
+EARLY_PLANES, LAST_PLANE = (0, 1, 2), 3
 
 
 def tile_moe_seb_relu_kernel(
@@ -49,7 +50,7 @@ def tile_moe_seb_relu_kernel(
         w2_w_raw = [keep.tile([P, PASSES, 2 * H], U8, name="w2_w_raw%d" % f, align_bytes=64) for f in range(E)]
         w2_s_raw = keep.tile([P, E * PASSES, H], U8, name="w2_s_raw", align_bytes=64)
         q = [keep.tile([P, C], F32, name="q%d" % f, tag="q%d" % f, align_bytes=64) for f in range(E)]
-        q_first = keep.tile([P, C], F32, name="q_first", tag="first", align_bytes=64)
+        q_first = keep.tile([P, P], F32, name="q_first", tag="first", align_bytes=64)
         a_sb = keep.tile([P, PACK, T], F32, name="a_sb")
         g1 = keep.tile([P, T], F32, name="g1")
         w1_raw = [keep.tile([P, PACK, K], F32, name="w1_raw%d" % e) for e in range(E)]
@@ -77,7 +78,7 @@ def tile_moe_seb_relu_kernel(
                 w2t_scales[:, :, QUAD_ROWS * quad : QUAD_ROWS * (quad + 1), :].rearrange("f s b i -> b (f s) i").bitcast(I32),
             )
         nc.sync.dma_start(w2_w_raw[1][:].bitcast(I32), w2_rows[1])
-        nc.sync.dma_start(q_first[:], gate2[:, :C])
+        nc.sync.dma_start(q_first[:], gate2[:, :P])
         nc.sync.dma_start(q[0][:], gate2[:, :C])
         nc.sync.dma_start(q[1][:], gate2[:, C:])
 
@@ -86,25 +87,26 @@ def tile_moe_seb_relu_kernel(
             for t in range(PACK):
                 nc.sync.dma_start(planes[:, t, :], by_plane[t])
 
-        load_planes(w1_raw[0], w1t[0])
-        load_planes(a_sb, a)
+        for e in range(E):
+            load_planes(w1_raw[e], w1t[e])
         nc.sync.dma_start(g1[:], gate1)
+        load_planes(a_sb, a)
         nc.sync.dma_start(list1[:], offs)
-        load_planes(w1_raw[1], w1t[1])
 
         w2_w = [keep.tile([P, PASSES, PACK, 2 * P], U8, name="w2_w%d" % f, align_bytes=64) for f in range(E)]
         w2_s = [keep.tile([P, PASSES, PACK, P], U8, name="w2_s%d" % f, align_bytes=64) for f in range(E)]
 
-        def sort_by_plane(planes, raw):
+        def sort_by_plane(planes, raw, t0, t1):
             nc.scalar.copy(
-                planes.bitcast(U32).rearrange("p s t (b w) -> p s t b w", b=BLOCKS),
-                raw.bitcast(U32).rearrange("p s (b t w) -> p s t b w", b=BLOCKS, t=PACK),
+                planes.bitcast(U32).rearrange("p s t (b w) -> p s t b w", b=BLOCKS)[:, :, t0:t1, :, :],
+                raw.bitcast(U32).rearrange("p s (b t w) -> p s t b w", b=BLOCKS, t=PACK)[:, :, t0:t1, :, :],
             )
 
         for f in range(E):
             passes = slice(PASSES * f, PASSES * (f + 1))
-            sort_by_plane(w2_w[f][:], w2_w_raw[f][:])
-            sort_by_plane(w2_s[f][:], w2_s_raw[:, passes, :])
+            sort_by_plane(w2_w[f][:], w2_w_raw[f][:], 0, PACK)
+            for t0, t1 in ((0, 2), (2, PACK)) if f == 0 else ((0, PACK),):
+                sort_by_plane(w2_s[f][:], w2_s_raw[:, passes, :], t0, t1)
 
         slot_w = [keep.tile([P, T], U32, name="slot_w%d" % s, align_bytes=64) for s in range(PASSES)]
         slot_s = [
@@ -112,10 +114,7 @@ def tile_moe_seb_relu_kernel(
             keep.tile([P, PASSES, C], U8, name="slot_s1", tag="first", align_bytes=64),
         ]
         dc = [keep.tile([P, T], F32, name="dc%d" % t, align_bytes=64) for t in range(PACK)]
-        dc_slots = [
-            [keep.tile([P, C], F32, name="dc_slots%d%d" % (f, t), tag="dc_slots%d%d" % (f, t), align_bytes=64) for t in range(PACK)]
-            for f in range(E)
-        ]
+        dc_slots = keep.tile([P, PACK, T], F32, name="dc_slots", tag="dc_slots", align_bytes=64)
 
         def gather_words(f, s):
             lo, hi = f * C, (f + 1) * C
@@ -124,19 +123,25 @@ def tile_moe_seb_relu_kernel(
         def gather_scales(f, s):
             nc.vector.tensor_copy(slot_s[f][:, s, :], dy_s[:, s, :].indirect(entries(list2, f * C, (f + 1) * C)))
 
-        def second_layer(f, t):
-            acc = psum.tile([P, C], F32, name="acc", tag="bank")
-            for s in range(PASSES):
-                nc.tensor.matmul_mx(
-                    out=acc[:],
-                    lhsT=w2_w[f][:, s, t, :].bitcast(FP4X4),
-                    lhsT_scale=w2_s[f][:, s, t, :],
-                    rhs=slot_w[s][:, f * C : (f + 1) * C].bitcast(FP8X4),
-                    rhs_scale=slot_s[f][:, s, :],
-                    start=(s == 0),
-                    stop=(s == PASSES - 1),
-                )
-            nc.vector.tensor_tensor(dc_slots[f][t][:], acc[:], (q_first if f == 0 and t == 0 else q[f])[:], ALU.mult)
+        def second_layer(f, t0, t1, lo, hi, gate):
+            acc = psum.tile([P, t1 - t0, hi - lo], F32, name="acc", tag="bank")
+            for t in range(t0, t1):
+                for s in range(PASSES):
+                    nc.tensor.matmul_mx(
+                        out=acc[:, t - t0, :],
+                        lhsT=w2_w[f][:, s, t, :].bitcast(FP4X4),
+                        lhsT_scale=w2_s[f][:, s, t, :],
+                        rhs=slot_w[s][:, f * C + lo : f * C + hi].bitcast(FP8X4),
+                        rhs_scale=slot_s[f][:, s, lo:hi],
+                        start=(s == 0),
+                        stop=(s == PASSES - 1),
+                    )
+            nc.vector.tensor_tensor(
+                dc_slots[:, t0:t1, f * C + lo : f * C + hi],
+                acc[:],
+                gate.unsqueeze(1).to_broadcast([P, t1 - t0, hi - lo]),
+                ALU.mult,
+            )
 
         def scatter(on_vector, window, offsets, values):
             if on_vector:
@@ -150,33 +155,36 @@ def tile_moe_seb_relu_kernel(
             gather_scales(0, s)
         for s in range(PASSES):
             gather_words(1, s)
-        second_layer(0, 0)
+        second_layer(0, 0, 2, 0, P, q_first[:])
         for s in range(PASSES):
             gather_scales(1, s)
-        for t in range(1, PACK):
-            second_layer(0, t)
-        for t in range(PACK):
-            second_layer(1, t)
-        for f in range(E):
-            for t in range(PACK):
-                scatter(t == VECTOR_PLANE, dc[t], entries(list2, f * C, (f + 1) * C), dc_slots[f][t][:])
+        second_layer(0, 0, 2, P, C, q[0][:, P:])
+        for t in (LAST_PLANE, 2):
+            second_layer(0, t, t + 1, 0, C, q[0][:])
+        for t0 in range(0, PACK, 2):
+            second_layer(1, t0, t0 + 2, 0, C, q[1][:])
 
-        slope = [keep.tile([P, PACK, C], F32, name="slope%d" % e, tag="slope") for e in range(E)]
-        da = [keep.tile([P, PACK, C], F32, name="da%d" % e) for e in range(E)]
-        w1_bf = [
-            keep.tile([P, K, PACK], BF16, name="w1_bf0", align_bytes=64),
-            keep.tile([P, K, PACK], BF16, name="w1_bf1", tag="dc_slots1%d" % LAST_PLANE, align_bytes=64),
-        ]
+        def scatter_dc(on_vector, t, lo, hi):
+            scatter(on_vector, dc[t], entries(list2, lo, hi), dc_slots[:, t, lo:hi])
+
+        for lo in range(0, C, P):
+            for t in range(2):
+                scatter_dc(False, t, lo, lo + P)
+        scatter_dc(False, 2, 0, C)
+        scatter_dc(True, LAST_PLANE, 0, C)
+        scatter_dc(True, LAST_PLANE, C, VECTOR_SLOTS)
+        for t in EARLY_PLANES:
+            scatter_dc(False, t, C, T)
+        scatter_dc(False, LAST_PLANE, VECTOR_SLOTS, T)
+
+        slope = keep.tile([P, PACK, T], F32, name="slope")
+        shared = PACK * LAST_PLANE
+        da_rows = keep.tile([P, shared + 1, C], F32, name="da_rows")
+        da = [da_rows[:, shared - LAST_PLANE : shared + 1, :], da_rows[:, 0 : shared + 1 : PACK, :]]
+        w1_bf = [keep.tile([P, K, PACK], BF16, name="w1_bf%d" % e, align_bytes=64) for e in range(E)]
         w1_w = [keep.tile([P, K], U32, name="w1_w%d" % e, align_bytes=64) for e in range(E)]
         w1_s = [keep.tile([P, K], U8, name="w1_s%d" % e, align_bytes=64) for e in range(E)]
-        dx_slots = keep.tile([P, GROUPS, K // P, P], F32, name="dx_slots")
-        dx = [keep.tile([P, T], F32, name="dx%d" % kt) for kt in range(K // P)]
-
-        def make_slope(e):
-            slots = slice(e * C, (e + 1) * C)
-            nc.vector.scalar_tensor_tensor(
-                slope[e][:], a_sb[:, :, slots], 0.0, g1[:, slots].unsqueeze(1).to_broadcast([P, PACK, C]), ALU.is_gt, ALU.mult
-            )
+        dx = []
 
         def interleave(copy, columns, planes):
             copy(columns.rearrange("p (c i) t -> p c t i", i=PACK), planes.rearrange("p t (c i) -> p c t i", i=PACK))
@@ -189,28 +197,23 @@ def tile_moe_seb_relu_kernel(
 
         def gather_dc(e, t, lo, hi):
             nc.vector.tensor_tensor(
-                da[e][:, t, lo:hi], dc[t][:].indirect(entries(list1, e * C + lo, e * C + hi)), slope[e][:, t, lo:hi], ALU.mult
+                da[e][:, t, lo:hi], dc[t][:].indirect(entries(list1, e * C + lo, e * C + hi)), slope[:, t, e * C + lo : e * C + hi], ALU.mult
             )
 
-        def first_layer(c):
+        def first_layer(c, sums):
             e, half = divmod(c, GROUPS_PER_EXPERT)
             lo = half * P
-            gather_dc(e, LAST_PLANE, lo, lo + P)
-            da_bf = keep.tile([P, P, PACK], BF16, name="da_bf%d" % c, align_bytes=64)
+            da_bf = keep.tile([P, P, PACK], BF16, name="da_bf%d" % c, tag="da_bf%d" % c, align_bytes=64)
             da_w = keep.tile([P, P], U32, name="da_w%d" % c, align_bytes=64)
             da_s = keep.tile([P, P], U8, name="da_s%d" % c, align_bytes=64)
-            interleave(nc.vector.tensor_copy, da_bf[:], da[e][:, :, lo : lo + P])
+            interleave(nc.scalar.copy if c in SCALAR_ROUNDS else nc.vector.tensor_copy, da_bf[:], da[e][:, :, lo : lo + P])
+            if e == 0:
+                gather_dc(1, LAST_PLANE, lo, lo + P)
             quantize(da_w[:], da_s[:], da_bf[:])
-            last = c == GROUPS - 1
-            if last:
-                banks = [psum.tile([P, P], F32, name="acc1", tag="bank")[:] for kt in range(K // P)]
-            else:
-                both = psum.tile([P, K // P, P], F32, name="acc1", tag="bank")
-                banks = [both[:, kt, :] for kt in range(K // P)]
             for kt in range(K // P):
                 cols = slice(kt * P, (kt + 1) * P)
                 nc.tensor.matmul_mx(
-                    out=banks[kt],
+                    out=sums[:, kt, :],
                     lhsT=w1_w[e][:, cols].bitcast(FP8X4),
                     lhsT_scale=w1_s[e][:, cols],
                     rhs=da_w[:].bitcast(FP8X4),
@@ -218,29 +221,37 @@ def tile_moe_seb_relu_kernel(
                     start=True,
                     stop=True,
                 )
-            if last:
-                for kt in (1, 0):
-                    nc.vector.tensor_copy(dx_slots[:, c, kt, :], banks[kt])
-            else:
-                nc.scalar.copy(dx_slots[:, c, :, :], both[:])
 
-        def scatter_dx(c, kt):
-            scatter(c == GROUPS - 1, dx[kt], entries(list1, c * P, (c + 1) * P), dx_slots[:, c, kt, :])
+        def scatter_dx(kt, lo, hi):
+            scatter(kt == 1, dx[kt], entries(list1, lo, hi), dx_slots[:, kt, lo:hi])
 
-        round_on_gpsimd(w1_bf[0][:], w1_raw[0][:].rearrange("p t k -> p k t"))
-        interleave(nc.scalar.copy, w1_bf[1][:], w1_raw[1][:])
         for e in range(E):
-            make_slope(e)
-            for t in EARLY_PLANES:
-                gather_dc(e, t, 0, C)
+            round_on_gpsimd(w1_bf[e][:], w1_raw[e][:].rearrange("p t k -> p k t"))
             quantize(w1_w[e][:], w1_s[e][:], w1_bf[e][:])
-            for half in range(GROUPS_PER_EXPERT):
-                first_layer(e * GROUPS_PER_EXPERT + half)
-                if e == 0:
-                    for kt in range(K // P):
-                        scatter_dx(half, kt)
-        for kt in range(K // P):
-            scatter_dx(GROUPS - 2, kt)
-            scatter_dx(GROUPS - 1, 1 - kt)
+        for t0 in range(0, PACK, 2):
+            planes = slice(t0, t0 + 2)
+            nc.vector.scalar_tensor_tensor(
+                slope[:, planes, :], a_sb[:, planes, :], 0.0, g1[:].unsqueeze(1).to_broadcast([P, 2, T]), ALU.is_gt, ALU.mult
+            )
+        for t in EARLY_PLANES:
+            for e in range(E):
+                gather_dc(e, t, 0, C)
+        for lo in range(0, C, P):
+            gather_dc(0, LAST_PLANE, lo, lo + P)
+        dx_slots = keep.tile([P, K // P, T], F32, name="dx_slots")
+        for c in range(GROUPS_PER_EXPERT):
+            bank = psum.tile([P, K // P, P], F32, name="acc1", tag="bank")
+            first_layer(c, bank[:])
+            nc.scalar.copy(dx_slots[:, :, c * P : (c + 1) * P], bank[:])
+        bank = psum.tile([P, K // P, C], F32, name="acc1", tag="bank")
+        for half in range(GROUPS_PER_EXPERT):
+            first_layer(GROUPS_PER_EXPERT + half, bank[:, :, half * P : (half + 1) * P])
+        dx.append(keep.tile([P, T], F32, name="dx0"))
+        dx.append(keep.tile([P, T], F32, name="dx1"))
+        nc.vector.tensor_copy(dx_slots[:, :, C:], bank[:])
+        scatter_dx(1, 0, P)
+        scatter_dx(1, P, T)
+        for lo, hi in ((0, P), (P, C), (C, T)):
+            scatter_dx(0, lo, hi)
         for kt in range(K // P):
             nc.sync.dma_start(out[kt * P : (kt + 1) * P, :], dx[kt][:])

@@ -177,10 +177,11 @@ def tile_moe_seb_relu_kernel(
             scatter_dc(False, t, C, T)
         scatter_dc(False, LAST_PLANE, VECTOR_SLOTS, T)
 
-        slope = keep.tile([P, PACK, T], F32, name="slope")
-        shared = PACK * LAST_PLANE
-        da_rows = keep.tile([P, shared + 1, C], F32, name="da_rows")
-        da = [da_rows[:, shared - LAST_PLANE : shared + 1, :], da_rows[:, 0 : shared + 1 : PACK, :]]
+        step = 2 * LAST_PLANE + 1
+        first = LAST_PLANE * step - 2 * LAST_PLANE
+        rows = keep.tile([P, first + PACK * E, C], F32, name="rows")
+        slope = rows[:, first:, :].rearrange("p (t e) c -> p t (e c)", e=E)
+        da = [rows[:, 1 : 1 + PACK, :], rows[:, 0 : LAST_PLANE * step + 1 : step, :]]
         w1_bf = [keep.tile([P, K, PACK], BF16, name="w1_bf%d" % e, align_bytes=64) for e in range(E)]
         w1_w = [keep.tile([P, K], U32, name="w1_w%d" % e, align_bytes=64) for e in range(E)]
         w1_s = [keep.tile([P, K], U8, name="w1_s%d" % e, align_bytes=64) for e in range(E)]
@@ -207,13 +208,11 @@ def tile_moe_seb_relu_kernel(
             da_w = keep.tile([P, P], U32, name="da_w%d" % c, align_bytes=64)
             da_s = keep.tile([P, P], U8, name="da_s%d" % c, align_bytes=64)
             interleave(nc.scalar.copy if c in SCALAR_ROUNDS else nc.vector.tensor_copy, da_bf[:], da[e][:, :, lo : lo + P])
-            if e == 0:
-                gather_dc(1, LAST_PLANE, lo, lo + P)
             quantize(da_w[:], da_s[:], da_bf[:])
             for kt in range(K // P):
                 cols = slice(kt * P, (kt + 1) * P)
                 nc.tensor.matmul_mx(
-                    out=sums[:, kt, :],
+                    out=sums[kt],
                     lhsT=w1_w[e][:, cols].bitcast(FP8X4),
                     lhsT_scale=w1_s[e][:, cols],
                     rhs=da_w[:].bitcast(FP8X4),
@@ -236,22 +235,21 @@ def tile_moe_seb_relu_kernel(
         for t in EARLY_PLANES:
             for e in range(E):
                 gather_dc(e, t, 0, C)
-        for lo in range(0, C, P):
-            gather_dc(0, LAST_PLANE, lo, lo + P)
+        for e in range(E):
+            for lo in range(0, C, P):
+                gather_dc(e, LAST_PLANE, lo, lo + P)
         dx_slots = keep.tile([P, K // P, T], F32, name="dx_slots")
-        for c in range(GROUPS_PER_EXPERT):
-            bank = psum.tile([P, K // P, P], F32, name="acc1", tag="bank")
-            first_layer(c, bank[:])
-            nc.scalar.copy(dx_slots[:, :, c * P : (c + 1) * P], bank[:])
-        bank = psum.tile([P, K // P, C], F32, name="acc1", tag="bank")
-        for half in range(GROUPS_PER_EXPERT):
-            first_layer(GROUPS_PER_EXPERT + half, bank[:, :, half * P : (half + 1) * P])
-        dx.append(keep.tile([P, T], F32, name="dx0"))
-        dx.append(keep.tile([P, T], F32, name="dx1"))
-        nc.vector.tensor_copy(dx_slots[:, :, C:], bank[:])
-        scatter_dx(1, 0, P)
-        scatter_dx(1, P, T)
-        for lo, hi in ((0, P), (P, C), (C, T)):
-            scatter_dx(0, lo, hi)
-        for kt in range(K // P):
-            nc.sync.dma_start(out[kt * P : (kt + 1) * P, :], dx[kt][:])
+        dx.extend(keep.tile([P, T], F32, name="dx%d" % kt) for kt in range(K // P))
+        for lo, hi in ((0, P), (P, T)):
+            banks = [psum.tile([P, hi - lo], F32, name="acc1", tag="bank") for kt in range(K // P)]
+            for c in range(lo // P, hi // P):
+                first_layer(c, [bank[:, c * P - lo : (c + 1) * P - lo] for bank in banks])
+            nc.scalar.copy(dx_slots[:, 0, lo:hi], banks[0][:])
+            if lo == 0:
+                nc.scalar.copy(dx_slots[:, 1, lo:hi], banks[1][:])
+            else:
+                nc.vector.tensor_copy(dx_slots[:, 1, lo:hi], banks[1][:])
+            for kt in range(K // P):
+                scatter_dx(kt, lo, hi)
+        nc.scalar.dma_start(out[:P, :], dx[0][:])
+        nc.sync.dma_start(out[P:, :], dx[1][:])

@@ -47,8 +47,8 @@ def tile_moe_seb_relu_kernel(
         list1 = keep.tile([P, T // LANES], U16, name="list1")
         dy_w = keep.tile([P, PASSES, T], I32, name="dy_w", align_bytes=64)
         dy_s = keep.tile([P, PASSES, T], U8, name="dy_s", align_bytes=64)
-        w2_w_raw = [keep.tile([P, PASSES, 2 * H], U8, name="w2_w_raw%d" % f, align_bytes=64) for f in range(E)]
-        w2_s_raw = keep.tile([P, E * PASSES, H], U8, name="w2_s_raw", align_bytes=64)
+        w2_w_raw = [keep.tile([P, PASSES, 2 * H], U8, name="w2_w_raw%d" % f, tag="w2_w_raw%d" % f, align_bytes=64) for f in range(E)]
+        w2_s_raw = keep.tile([P, E * PASSES, H], U8, name="w2_s_raw", tag="w2_s_raw", align_bytes=64)
         q = [keep.tile([P, C], F32, name="q%d" % f, tag="q%d" % f, align_bytes=64) for f in range(E)]
         q_first = keep.tile([P, P], F32, name="q_first", tag="first", align_bytes=64)
         a_sb = keep.tile([P, PACK, T], F32, name="a_sb")
@@ -108,38 +108,48 @@ def tile_moe_seb_relu_kernel(
             for t0, t1 in ((0, 2), (2, PACK)) if f == 0 else ((0, PACK),):
                 sort_by_plane(w2_s[f][:], w2_s_raw[:, passes, :], t0, t1)
 
-        slot_w = [keep.tile([P, T], U32, name="slot_w%d" % s, align_bytes=64) for s in range(PASSES)]
+        slot_w = [
+            [keep.tile([P, C], U32, name="slot_w0%d" % s, align_bytes=64) for s in range(PASSES)],
+            [
+                keep.tile([P, C], U32, name="slot_w10", tag="w2_w_raw0", align_bytes=64),
+                keep.tile([P, C], U32, name="slot_w11", align_bytes=64),
+            ],
+        ]
         slot_s = [
-            keep.tile([P, PASSES, C], U8, name="slot_s0", align_bytes=64),
-            keep.tile([P, PASSES, C], U8, name="slot_s1", tag="first", align_bytes=64),
+            [keep.tile([P, C], U8, name="slot_s0%d" % s, align_bytes=64) for s in range(PASSES)],
+            [
+                keep.tile([P, C], U8, name="slot_s10", tag="w2_s_raw", align_bytes=64),
+                keep.tile([P, C], U8, name="slot_s11", tag="first", align_bytes=64),
+            ],
         ]
         dc = [keep.tile([P, T], F32, name="dc%d" % t, align_bytes=64) for t in range(PACK)]
         dc_slots = keep.tile([P, PACK, T], F32, name="dc_slots", tag="dc_slots", align_bytes=64)
 
         def gather_words(f, s):
             lo, hi = f * C, (f + 1) * C
-            nc.vector.tensor_copy(slot_w[s][:, lo:hi], dy_w[:, s, :].bitcast(U32).indirect(entries(list2, lo, hi)))
+            nc.vector.tensor_copy(slot_w[f][s][:], dy_w[:, s, :].bitcast(U32).indirect(entries(list2, lo, hi)))
 
         def gather_scales(f, s):
-            nc.vector.tensor_copy(slot_s[f][:, s, :], dy_s[:, s, :].indirect(entries(list2, f * C, (f + 1) * C)))
+            nc.vector.tensor_copy(slot_s[f][s][:], dy_s[:, s, :].indirect(entries(list2, f * C, (f + 1) * C)))
 
-        def second_layer(f, t0, t1, lo, hi, gate):
-            acc = psum.tile([P, t1 - t0, hi - lo], F32, name="acc", tag="bank")
-            for t in range(t0, t1):
+        def second_layer(f, t0, t1, lo, hi, gate, step=1):
+            planes = range(t0, t1, step)
+            acc = psum.tile([P, len(planes), hi - lo], F32, name="acc", tag="bank")
+            for place, t in enumerate(planes):
                 for s in range(PASSES):
                     nc.tensor.matmul_mx(
-                        out=acc[:, t - t0, :],
+                        out=acc[:, place, :],
                         lhsT=w2_w[f][:, s, t, :].bitcast(FP4X4),
                         lhsT_scale=w2_s[f][:, s, t, :],
-                        rhs=slot_w[s][:, f * C + lo : f * C + hi].bitcast(FP8X4),
-                        rhs_scale=slot_s[f][:, s, lo:hi],
+                        rhs=slot_w[f][s][:, lo:hi].bitcast(FP8X4),
+                        rhs_scale=slot_s[f][s][:, lo:hi],
                         start=(s == 0),
                         stop=(s == PASSES - 1),
                     )
             nc.vector.tensor_tensor(
-                dc_slots[:, t0:t1, f * C + lo : f * C + hi],
+                dc_slots[:, t0:t1:step, f * C + lo : f * C + hi],
                 acc[:],
-                gate.unsqueeze(1).to_broadcast([P, t1 - t0, hi - lo]),
+                gate.unsqueeze(1).to_broadcast([P, len(planes), hi - lo]),
                 ALU.mult,
             )
 
@@ -155,14 +165,14 @@ def tile_moe_seb_relu_kernel(
             gather_scales(0, s)
         for s in range(PASSES):
             gather_words(1, s)
+        gather_scales(1, 0)
         second_layer(0, 0, 2, 0, P, q_first[:])
-        for s in range(PASSES):
-            gather_scales(1, s)
         second_layer(0, 0, 2, P, C, q[0][:, P:])
+        gather_scales(1, 1)
         for t in (LAST_PLANE, 2):
             second_layer(0, t, t + 1, 0, C, q[0][:])
-        for t0 in range(0, PACK, 2):
-            second_layer(1, t0, t0 + 2, 0, C, q[1][:])
+        for t0, t1, step in ((0, PACK, LAST_PLANE), (1, LAST_PLANE, 1)):
+            second_layer(1, t0, t1, 0, C, q[1][:], step)
 
         def scatter_dc(on_vector, t, lo, hi):
             scatter(on_vector, dc[t], entries(list2, lo, hi), dc_slots[:, t, lo:hi])
@@ -177,11 +187,10 @@ def tile_moe_seb_relu_kernel(
             scatter_dc(False, t, C, T)
         scatter_dc(False, LAST_PLANE, VECTOR_SLOTS, T)
 
-        step = 2 * LAST_PLANE + 1
-        first = LAST_PLANE * step - 2 * LAST_PLANE
-        rows = keep.tile([P, first + PACK * E, C], F32, name="rows")
-        slope = rows[:, first:, :].rearrange("p (t e) c -> p t (e c)", e=E)
-        da = [rows[:, 1 : 1 + PACK, :], rows[:, 0 : LAST_PLANE * step + 1 : step, :]]
+        slope = keep.tile([P, PACK, T], F32, name="slope")
+        shared = PACK * LAST_PLANE
+        da_rows = keep.tile([P, shared + 1, C], F32, name="da_rows")
+        da = [da_rows[:, shared - LAST_PLANE : shared + 1, :], da_rows[:, 0 : shared + 1 : PACK, :]]
         w1_bf = [keep.tile([P, K, PACK], BF16, name="w1_bf%d" % e, align_bytes=64) for e in range(E)]
         w1_w = [keep.tile([P, K], U32, name="w1_w%d" % e, align_bytes=64) for e in range(E)]
         w1_s = [keep.tile([P, K], U8, name="w1_s%d" % e, align_bytes=64) for e in range(E)]
@@ -208,11 +217,13 @@ def tile_moe_seb_relu_kernel(
             da_w = keep.tile([P, P], U32, name="da_w%d" % c, align_bytes=64)
             da_s = keep.tile([P, P], U8, name="da_s%d" % c, align_bytes=64)
             interleave(nc.scalar.copy if c in SCALAR_ROUNDS else nc.vector.tensor_copy, da_bf[:], da[e][:, :, lo : lo + P])
+            if e == 0:
+                gather_dc(1, LAST_PLANE, lo, lo + P)
             quantize(da_w[:], da_s[:], da_bf[:])
             for kt in range(K // P):
                 cols = slice(kt * P, (kt + 1) * P)
                 nc.tensor.matmul_mx(
-                    out=sums[kt],
+                    out=sums[:, kt, :],
                     lhsT=w1_w[e][:, cols].bitcast(FP8X4),
                     lhsT_scale=w1_s[e][:, cols],
                     rhs=da_w[:].bitcast(FP8X4),
@@ -235,21 +246,22 @@ def tile_moe_seb_relu_kernel(
         for t in EARLY_PLANES:
             for e in range(E):
                 gather_dc(e, t, 0, C)
-        for e in range(E):
-            for lo in range(0, C, P):
-                gather_dc(e, LAST_PLANE, lo, lo + P)
+        for lo in range(0, C, P):
+            gather_dc(0, LAST_PLANE, lo, lo + P)
         dx_slots = keep.tile([P, K // P, T], F32, name="dx_slots")
-        dx.extend(keep.tile([P, T], F32, name="dx%d" % kt) for kt in range(K // P))
-        for lo, hi in ((0, P), (P, T)):
-            banks = [psum.tile([P, hi - lo], F32, name="acc1", tag="bank") for kt in range(K // P)]
-            for c in range(lo // P, hi // P):
-                first_layer(c, [bank[:, c * P - lo : (c + 1) * P - lo] for bank in banks])
-            nc.scalar.copy(dx_slots[:, 0, lo:hi], banks[0][:])
-            if lo == 0:
-                nc.scalar.copy(dx_slots[:, 1, lo:hi], banks[1][:])
-            else:
-                nc.vector.tensor_copy(dx_slots[:, 1, lo:hi], banks[1][:])
-            for kt in range(K // P):
-                scatter_dx(kt, lo, hi)
-        nc.scalar.dma_start(out[:P, :], dx[0][:])
-        nc.sync.dma_start(out[P:, :], dx[1][:])
+        for c in range(GROUPS_PER_EXPERT):
+            bank = psum.tile([P, K // P, P], F32, name="acc1", tag="bank")
+            first_layer(c, bank[:])
+            nc.scalar.copy(dx_slots[:, :, c * P : (c + 1) * P], bank[:])
+        bank = psum.tile([P, K // P, C], F32, name="acc1", tag="bank")
+        for half in range(GROUPS_PER_EXPERT):
+            first_layer(GROUPS_PER_EXPERT + half, bank[:, :, half * P : (half + 1) * P])
+        dx.append(keep.tile([P, T], F32, name="dx0"))
+        dx.append(keep.tile([P, T], F32, name="dx1"))
+        nc.vector.tensor_copy(dx_slots[:, :, C:], bank[:])
+        scatter_dx(1, 0, P)
+        scatter_dx(1, P, T)
+        for lo, hi in ((0, P), (P, C), (C, T)):
+            scatter_dx(0, lo, hi)
+        for kt in range(K // P):
+            nc.sync.dma_start(out[kt * P : (kt + 1) * P, :], dx[kt][:])

@@ -21,14 +21,14 @@ P = 128
 PACK = 4
 PASSES = N // (P * PACK)
 LANES = 16
-QUADS, QUAD, QUAD_ROWS = 4, 32, 4
+QUAD, QUAD_ROWS = 32, 4
 QUAD_ORDER = (0, 2, 1, 3)
 BLOCKS, RUN = H // 32, 8
-GROUPS = T // P
-GROUPS_PER_EXPERT = C // P
-VECTOR_SLOTS = 320
-SCALAR_ROUNDS = (1, 2)
-EARLY_PLANES, LAST_PLANE = (0, 1, 2), 3
+VECTOR_PLANE = 3
+LAST_PLANE = 2
+EARLY_PLANES = (3, 0, 1)
+HALF_RANGE = 2.0**75
+CEILING = 2.0**-24
 
 
 def tile_moe_seb_relu_kernel(
@@ -38,6 +38,9 @@ def tile_moe_seb_relu_kernel(
 
     def entries(list_tile, lo, hi):
         return list_tile[:, lo // LANES : hi // LANES]
+
+    def place(t):
+        return (t + 1) % PACK
 
     with ExitStack() as ctx:
         keep = ctx.enter_context(tc.tile_pool(name="keep", bufs=1))
@@ -51,7 +54,7 @@ def tile_moe_seb_relu_kernel(
         w2_s_raw = keep.tile([P, E * PASSES, H], U8, name="w2_s_raw", tag="w2_s_raw", align_bytes=64)
         q = [keep.tile([P, C], F32, name="q%d" % f, tag="q%d" % f, align_bytes=64) for f in range(E)]
         q_first = keep.tile([P, P], F32, name="q_first", tag="first", align_bytes=64)
-        a_sb = keep.tile([P, PACK, T], F32, name="a_sb")
+        a_sb = [keep.tile([P, PACK, C], F32, name="a_sb%d" % e, tag="a_sb%d" % e, align_bytes=64) for e in range(E)]
         g1 = keep.tile([P, T], F32, name="g1")
         w1_raw = [keep.tile([P, PACK, K], F32, name="w1_raw%d" % e) for e in range(E)]
 
@@ -85,12 +88,13 @@ def tile_moe_seb_relu_kernel(
         def load_planes(planes, rows):
             by_plane = rows.rearrange("(b t u) c -> t b u c", t=PACK, u=RUN)
             for t in range(PACK):
-                nc.sync.dma_start(planes[:, t, :], by_plane[t])
+                nc.sync.dma_start(planes[:, place(t), :], by_plane[t])
 
+        load_planes(a_sb[1], a[:, C:])
+        nc.sync.dma_start(g1[:], gate1)
         for e in range(E):
             load_planes(w1_raw[e], w1t[e])
-        nc.sync.dma_start(g1[:], gate1)
-        load_planes(a_sb, a)
+        load_planes(a_sb[0], a[:, :C])
         nc.sync.dma_start(list1[:], offs)
 
         w2_w = [keep.tile([P, PASSES, PACK, 2 * P], U8, name="w2_w%d" % f, align_bytes=64) for f in range(E)]
@@ -123,11 +127,10 @@ def tile_moe_seb_relu_kernel(
             ],
         ]
         dc = [keep.tile([P, T], F32, name="dc%d" % t, align_bytes=64) for t in range(PACK)]
-        dc_slots = keep.tile([P, PACK, T], F32, name="dc_slots", tag="dc_slots", align_bytes=64)
+        slots = [keep.tile([P, PACK, C], F32, name="slots%d" % f, align_bytes=64) for f in range(E)]
 
         def gather_words(f, s):
-            lo, hi = f * C, (f + 1) * C
-            nc.vector.tensor_copy(slot_w[f][s][:], dy_w[:, s, :].bitcast(U32).indirect(entries(list2, lo, hi)))
+            nc.vector.tensor_copy(slot_w[f][s][:], dy_w[:, s, :].bitcast(U32).indirect(entries(list2, f * C, (f + 1) * C)))
 
         def gather_scales(f, s):
             nc.vector.tensor_copy(slot_s[f][s][:], dy_s[:, s, :].indirect(entries(list2, f * C, (f + 1) * C)))
@@ -135,10 +138,10 @@ def tile_moe_seb_relu_kernel(
         def second_layer(f, t0, t1, lo, hi, gate, step=1):
             planes = range(t0, t1, step)
             acc = psum.tile([P, len(planes), hi - lo], F32, name="acc", tag="bank")
-            for place, t in enumerate(planes):
+            for j, t in enumerate(planes):
                 for s in range(PASSES):
                     nc.tensor.matmul_mx(
-                        out=acc[:, place, :],
+                        out=acc[:, j, :],
                         lhsT=w2_w[f][:, s, t, :].bitcast(FP4X4),
                         lhsT_scale=w2_s[f][:, s, t, :],
                         rhs=slot_w[f][s][:, lo:hi].bitcast(FP8X4),
@@ -147,7 +150,7 @@ def tile_moe_seb_relu_kernel(
                         stop=(s == PASSES - 1),
                     )
             nc.vector.tensor_tensor(
-                dc_slots[:, t0:t1:step, f * C + lo : f * C + hi],
+                slots[f][:, t0:t1:step, lo:hi],
                 acc[:],
                 gate.unsqueeze(1).to_broadcast([P, len(planes), hi - lo]),
                 ALU.mult,
@@ -169,99 +172,92 @@ def tile_moe_seb_relu_kernel(
         second_layer(0, 0, 2, 0, P, q_first[:])
         second_layer(0, 0, 2, P, C, q[0][:, P:])
         gather_scales(1, 1)
-        for t in (LAST_PLANE, 2):
+        for t in (VECTOR_PLANE, LAST_PLANE):
             second_layer(0, t, t + 1, 0, C, q[0][:])
-        for t0, t1, step in ((0, PACK, LAST_PLANE), (1, LAST_PLANE, 1)):
+        for t0, t1, step in ((0, PACK, VECTOR_PLANE), (1, VECTOR_PLANE, 1)):
             second_layer(1, t0, t1, 0, C, q[1][:], step)
 
-        def scatter_dc(on_vector, t, lo, hi):
-            scatter(on_vector, dc[t], entries(list2, lo, hi), dc_slots[:, t, lo:hi])
+        def scatter_dc(on_vector, t, f, lo, hi):
+            scatter(on_vector, dc[t], entries(list2, f * C + lo, f * C + hi), slots[f][:, t, lo:hi])
 
         for lo in range(0, C, P):
             for t in range(2):
-                scatter_dc(False, t, lo, lo + P)
-        scatter_dc(False, 2, 0, C)
-        scatter_dc(True, LAST_PLANE, 0, C)
-        scatter_dc(True, LAST_PLANE, C, VECTOR_SLOTS)
-        for t in EARLY_PLANES:
-            scatter_dc(False, t, C, T)
-        scatter_dc(False, LAST_PLANE, VECTOR_SLOTS, T)
+                scatter_dc(False, t, 0, lo, lo + P)
+        scatter_dc(False, LAST_PLANE, 0, 0, C)
+        for f in range(E):
+            scatter_dc(True, VECTOR_PLANE, f, 0, C)
+        for t in range(VECTOR_PLANE):
+            scatter_dc(False, t, 1, 0, C)
 
-        slope = keep.tile([P, PACK, T], F32, name="slope")
-        shared = PACK * LAST_PLANE
-        da_rows = keep.tile([P, shared + 1, C], F32, name="da_rows")
-        da = [da_rows[:, shared - LAST_PLANE : shared + 1, :], da_rows[:, 0 : shared + 1 : PACK, :]]
-        w1_bf = [keep.tile([P, K, PACK], BF16, name="w1_bf%d" % e, align_bytes=64) for e in range(E)]
-        w1_w = [keep.tile([P, K], U32, name="w1_w%d" % e, align_bytes=64) for e in range(E)]
+        slope = [keep.tile([P, PACK, C], F32, name="slope%d" % e) for e in range(E)]
+        lifted = keep.tile([P, PACK, C], F32, name="lifted")
+        w1_bf = [keep.tile([P, K, PACK], BF16, name="w1_bf%d" % e, tag="rounded%d" % e, align_bytes=64) for e in range(E)]
         w1_s = [keep.tile([P, K], U8, name="w1_s%d" % e, align_bytes=64) for e in range(E)]
-        dx = []
 
-        def interleave(copy, columns, planes):
-            copy(columns.rearrange("p (c i) t -> p c t i", i=PACK), planes.rearrange("p t (c i) -> p c t i", i=PACK))
+        def by_column(columns):
+            return columns.rearrange("p (c i) t -> p c t i", i=PACK)
 
-        def round_on_gpsimd(rounded, values):
-            nc.gpsimd.tensor_scalar(rounded, values, 1.0, 0.0, ALU.mult, ALU.add)
+        def by_plane(planes):
+            return planes.rearrange("p t (c i) -> p c t i", i=PACK)
 
         def quantize(words, scales, columns):
             nc.vector.quantize_mx(out=words.bitcast(FP8X4), scales=scales, in_=columns.rearrange("p c t -> p (c t)"))
 
-        def gather_dc(e, t, lo, hi):
-            nc.vector.tensor_tensor(
-                da[e][:, t, lo:hi], dc[t][:].indirect(entries(list1, e * C + lo, e * C + hi)), slope[:, t, e * C + lo : e * C + hi], ALU.mult
-            )
+        def gate_rows(e):
+            return g1[:, e * C : (e + 1) * C].unsqueeze(1).to_broadcast([P, PACK, C])
 
-        def first_layer(c, sums):
-            e, half = divmod(c, GROUPS_PER_EXPERT)
-            lo = half * P
-            da_bf = keep.tile([P, P, PACK], BF16, name="da_bf%d" % c, tag="da_bf%d" % c, align_bytes=64)
-            da_w = keep.tile([P, P], U32, name="da_w%d" % c, align_bytes=64)
-            da_s = keep.tile([P, P], U8, name="da_s%d" % c, align_bytes=64)
-            interleave(nc.scalar.copy if c in SCALAR_ROUNDS else nc.vector.tensor_copy, da_bf[:], da[e][:, :, lo : lo + P])
-            if e == 0:
-                gather_dc(1, LAST_PLANE, lo, lo + P)
-            quantize(da_w[:], da_s[:], da_bf[:])
-            for kt in range(K // P):
-                cols = slice(kt * P, (kt + 1) * P)
-                nc.tensor.matmul_mx(
-                    out=sums[:, kt, :],
-                    lhsT=w1_w[e][:, cols].bitcast(FP8X4),
-                    lhsT_scale=w1_s[e][:, cols],
-                    rhs=da_w[:].bitcast(FP8X4),
-                    rhs_scale=da_s[:],
-                    start=True,
-                    stop=True,
-                )
-
-        def scatter_dx(kt, lo, hi):
-            scatter(kt == 1, dx[kt], entries(list1, lo, hi), dx_slots[:, kt, lo:hi])
-
+        nc.gpsimd.tensor_scalar(lifted[:], a_sb[1][:], CEILING, 0.0, ALU.min, ALU.max)
+        nc.gpsimd.tensor_scalar(lifted[:], lifted[:], HALF_RANGE, HALF_RANGE, ALU.mult, ALU.mult)
+        nc.gpsimd.tensor_scalar(lifted[:], lifted[:], 1.0, 0.0, ALU.min, ALU.max)
+        nc.gpsimd.tensor_tensor(slope[1][:], lifted[:], gate_rows(1), ALU.mult)
         for e in range(E):
-            round_on_gpsimd(w1_bf[e][:], w1_raw[e][:].rearrange("p t k -> p k t"))
-            quantize(w1_w[e][:], w1_s[e][:], w1_bf[e][:])
-        for t0 in range(0, PACK, 2):
-            planes = slice(t0, t0 + 2)
-            nc.vector.scalar_tensor_tensor(
-                slope[:, planes, :], a_sb[:, planes, :], 0.0, g1[:].unsqueeze(1).to_broadcast([P, 2, T]), ALU.is_gt, ALU.mult
+            nc.gpsimd.tensor_scalar(w1_bf[e][:], w1_raw[e][:].rearrange("p t k -> p k t"), 1.0, 0.0, ALU.mult, ALU.add)
+        nc.vector.scalar_tensor_tensor(slope[0][:], a_sb[0][:], 0.0, gate_rows(0), ALU.is_gt, ALU.mult)
+
+        def gather_times_slope(t):
+            nc.vector.tensor_tensor(
+                slots[0][:, place(t), :], dc[t][:].indirect(entries(list1, 0, C)), slope[0][:, place(t), :], ALU.mult
             )
+
         for t in EARLY_PLANES:
-            for e in range(E):
-                gather_dc(e, t, 0, C)
-        for lo in range(0, C, P):
-            gather_dc(0, LAST_PLANE, lo, lo + P)
+            gather_times_slope(t)
+        w1_w = keep.tile([P, E, K], U32, name="w1_w", tag="a_sb0", align_bytes=64)
+        for e in range(E):
+            quantize(w1_w[:, e, :], w1_s[e][:], w1_bf[e][:])
+        gather_times_slope(LAST_PLANE)
+        for t in (0, 1, VECTOR_PLANE, LAST_PLANE):
+            nc.scalar.activation(slots[1][:, place(t), :], dc[t][:].indirect(entries(list1, C, T)), ACT.Copy)
+
         dx_slots = keep.tile([P, K // P, T], F32, name="dx_slots")
-        for c in range(GROUPS_PER_EXPERT):
-            bank = psum.tile([P, K // P, P], F32, name="acc1", tag="bank")
-            first_layer(c, bank[:])
-            nc.scalar.copy(dx_slots[:, :, c * P : (c + 1) * P], bank[:])
-        bank = psum.tile([P, K // P, C], F32, name="acc1", tag="bank")
-        for half in range(GROUPS_PER_EXPERT):
-            first_layer(GROUPS_PER_EXPERT + half, bank[:, :, half * P : (half + 1) * P])
-        dx.append(keep.tile([P, T], F32, name="dx0"))
-        dx.append(keep.tile([P, T], F32, name="dx1"))
-        nc.vector.tensor_copy(dx_slots[:, :, C:], bank[:])
-        scatter_dx(1, 0, P)
-        scatter_dx(1, P, T)
-        for lo, hi in ((0, P), (P, C), (C, T)):
-            scatter_dx(0, lo, hi)
+        for e in range(E):
+            bank = psum.tile([P, K // P, C], F32, name="acc1", tag="bank")
+            for half in range(C // P):
+                lo = half * P
+                da_bf = keep.tile([P, P, PACK], BF16, name="da_bf", tag="rounded%d" % half, align_bytes=64)
+                da_w = keep.tile([P, P], U32, name="da_w%d%d" % (e, half), align_bytes=64)
+                da_s = keep.tile([P, P], U8, name="da_s%d%d" % (e, half), align_bytes=64)
+                gathered = by_plane(slots[e][:, :, lo : lo + P])
+                if e == 0:
+                    nc.vector.tensor_copy(by_column(da_bf[:]), gathered)
+                else:
+                    nc.vector.tensor_tensor(by_column(da_bf[:]), gathered, by_plane(slope[e][:, :, lo : lo + P]), ALU.mult)
+                quantize(da_w[:], da_s[:], da_bf[:])
+                for kt in range(K // P):
+                    cols = slice(kt * P, (kt + 1) * P)
+                    nc.tensor.matmul_mx(
+                        out=bank[:, kt, lo : lo + P],
+                        lhsT=w1_w[:, e, cols].bitcast(FP8X4),
+                        lhsT_scale=w1_s[e][:, cols],
+                        rhs=da_w[:].bitcast(FP8X4),
+                        rhs_scale=da_s[:],
+                        start=True,
+                        stop=True,
+                    )
+            nc.scalar.copy(dx_slots[:, :, e * C : (e + 1) * C], bank[:])
+
+        dx = [keep.tile([P, T], F32, name="dx0"), keep.tile([P, T], F32, name="dx1", tag="rounded0", align_bytes=64)]
+        for e in range(E):
+            for kt in range(K // P):
+                scatter(kt == 1, dx[kt], entries(list1, e * C, (e + 1) * C), dx_slots[:, kt, e * C : (e + 1) * C])
         for kt in range(K // P):
             nc.sync.dma_start(out[kt * P : (kt + 1) * P, :], dx[kt][:])

@@ -27,8 +27,7 @@ BLOCKS, RUN = H // 32, 8
 VECTOR_PLANE = 3
 LAST_PLANE = 2
 EARLY_PLANES = (3, 0, 1)
-HALF_RANGE = 2.0**75
-CEILING = 2.0**-24
+SHARE = 64
 
 
 def tile_moe_seb_relu_kernel(
@@ -54,7 +53,7 @@ def tile_moe_seb_relu_kernel(
         w2_s_raw = keep.tile([P, E * PASSES, H], U8, name="w2_s_raw", tag="w2_s_raw", align_bytes=64)
         q = [keep.tile([P, C], F32, name="q%d" % f, tag="q%d" % f, align_bytes=64) for f in range(E)]
         q_first = keep.tile([P, P], F32, name="q_first", tag="first", align_bytes=64)
-        a_sb = [keep.tile([P, PACK, C], F32, name="a_sb%d" % e, tag="a_sb%d" % e, align_bytes=64) for e in range(E)]
+        a_sb = keep.tile([P, PACK, T], F32, name="a_sb")
         g1 = keep.tile([P, T], F32, name="g1")
         w1_raw = [keep.tile([P, PACK, K], F32, name="w1_raw%d" % e) for e in range(E)]
 
@@ -90,11 +89,10 @@ def tile_moe_seb_relu_kernel(
             for t in range(PACK):
                 nc.sync.dma_start(planes[:, place(t), :], by_plane[t])
 
-        load_planes(a_sb[1], a[:, C:])
-        nc.sync.dma_start(g1[:], gate1)
         for e in range(E):
             load_planes(w1_raw[e], w1t[e])
-        load_planes(a_sb[0], a[:, :C])
+        nc.sync.dma_start(g1[:], gate1)
+        load_planes(a_sb, a)
         nc.sync.dma_start(list1[:], offs)
 
         w2_w = [keep.tile([P, PASSES, PACK, 2 * P], U8, name="w2_w%d" % f, align_bytes=64) for f in range(E)]
@@ -186,45 +184,33 @@ def tile_moe_seb_relu_kernel(
         scatter_dc(False, LAST_PLANE, 0, 0, C)
         for f in range(E):
             scatter_dc(True, VECTOR_PLANE, f, 0, C)
-        for t in range(VECTOR_PLANE):
+        scatter_dc(True, LAST_PLANE, 1, C - SHARE, C)
+        for t in range(LAST_PLANE):
             scatter_dc(False, t, 1, 0, C)
+        scatter_dc(False, LAST_PLANE, 1, 0, C - SHARE)
 
-        slope = [keep.tile([P, PACK, C], F32, name="slope%d" % e) for e in range(E)]
-        lifted = keep.tile([P, PACK, C], F32, name="lifted")
         w1_bf = [keep.tile([P, K, PACK], BF16, name="w1_bf%d" % e, tag="rounded%d" % e, align_bytes=64) for e in range(E)]
+        w1_w = [keep.tile([P, K], U32, name="w1_w%d" % e, align_bytes=64) for e in range(E)]
         w1_s = [keep.tile([P, K], U8, name="w1_s%d" % e, align_bytes=64) for e in range(E)]
 
-        def by_column(columns):
-            return columns.rearrange("p (c i) t -> p c t i", i=PACK)
+        def by_column(columns, run):
+            return columns.rearrange("p (c i) t -> p c t i", i=run)
 
-        def by_plane(planes):
-            return planes.rearrange("p t (c i) -> p c t i", i=PACK)
+        def by_plane(planes, run):
+            return planes.rearrange("p t (c i) -> p c t i", i=run)
 
         def quantize(words, scales, columns):
             nc.vector.quantize_mx(out=words.bitcast(FP8X4), scales=scales, in_=columns.rearrange("p c t -> p (c t)"))
 
-        def gate_rows(e):
-            return g1[:, e * C : (e + 1) * C].unsqueeze(1).to_broadcast([P, PACK, C])
-
-        nc.gpsimd.tensor_scalar(lifted[:], a_sb[1][:], CEILING, 0.0, ALU.min, ALU.max)
-        nc.gpsimd.tensor_scalar(lifted[:], lifted[:], HALF_RANGE, HALF_RANGE, ALU.mult, ALU.mult)
-        nc.gpsimd.tensor_scalar(lifted[:], lifted[:], 1.0, 0.0, ALU.min, ALU.max)
-        nc.gpsimd.tensor_tensor(slope[1][:], lifted[:], gate_rows(1), ALU.mult)
         for e in range(E):
             nc.gpsimd.tensor_scalar(w1_bf[e][:], w1_raw[e][:].rearrange("p t k -> p k t"), 1.0, 0.0, ALU.mult, ALU.add)
-        nc.vector.scalar_tensor_tensor(slope[0][:], a_sb[0][:], 0.0, gate_rows(0), ALU.is_gt, ALU.mult)
+            quantize(w1_w[e][:], w1_s[e][:], w1_bf[e][:])
 
-        def gather_times_slope(t):
-            nc.vector.tensor_tensor(
-                slots[0][:, place(t), :], dc[t][:].indirect(entries(list1, 0, C)), slope[0][:, place(t), :], ALU.mult
-            )
-
-        for t in EARLY_PLANES:
-            gather_times_slope(t)
-        w1_w = keep.tile([P, E, K], U32, name="w1_w", tag="a_sb0", align_bytes=64)
-        for e in range(E):
-            quantize(w1_w[:, e, :], w1_s[e][:], w1_bf[e][:])
-        gather_times_slope(LAST_PLANE)
+        slope = keep.tile([P, PACK, C], F32, name="slope")
+        gate_rows = g1[:, C:].unsqueeze(1).to_broadcast([P, PACK, C])
+        nc.vector.scalar_tensor_tensor(slope[:], a_sb[:, :, C:], 0.0, gate_rows, ALU.is_gt, ALU.mult)
+        for t in EARLY_PLANES + (LAST_PLANE,):
+            nc.vector.tensor_tensor(slots[0][:, place(t), :], dc[t][:].indirect(entries(list1, 0, C)), g1[:, :C], ALU.mult)
         for t in (0, 1, VECTOR_PLANE, LAST_PLANE):
             nc.scalar.activation(slots[1][:, place(t), :], dc[t][:].indirect(entries(list1, C, T)), ACT.Copy)
 
@@ -236,17 +222,26 @@ def tile_moe_seb_relu_kernel(
                 da_bf = keep.tile([P, P, PACK], BF16, name="da_bf", tag="rounded%d" % half, align_bytes=64)
                 da_w = keep.tile([P, P], U32, name="da_w%d%d" % (e, half), align_bytes=64)
                 da_s = keep.tile([P, P], U8, name="da_s%d%d" % (e, half), align_bytes=64)
-                gathered = by_plane(slots[e][:, :, lo : lo + P])
+                gathered = slots[e][:, :, lo : lo + P]
                 if e == 0:
-                    nc.vector.tensor_copy(by_column(da_bf[:]), gathered)
+                    nc.vector.scalar_tensor_tensor(
+                        da_bf[:],
+                        a_sb[:, :, lo : lo + P].rearrange("p t c -> p c t"),
+                        0.0,
+                        gathered.rearrange("p t c -> p c t"),
+                        ALU.is_gt,
+                        ALU.mult,
+                    )
                 else:
-                    nc.vector.tensor_tensor(by_column(da_bf[:]), gathered, by_plane(slope[e][:, :, lo : lo + P]), ALU.mult)
+                    nc.vector.tensor_tensor(
+                        by_column(da_bf[:], 2), by_plane(gathered, 2), by_plane(slope[:, :, lo : lo + P], 2), ALU.mult
+                    )
                 quantize(da_w[:], da_s[:], da_bf[:])
                 for kt in range(K // P):
                     cols = slice(kt * P, (kt + 1) * P)
                     nc.tensor.matmul_mx(
                         out=bank[:, kt, lo : lo + P],
-                        lhsT=w1_w[:, e, cols].bitcast(FP8X4),
+                        lhsT=w1_w[e][:, cols].bitcast(FP8X4),
                         lhsT_scale=w1_s[e][:, cols],
                         rhs=da_w[:].bitcast(FP8X4),
                         rhs_scale=da_s[:],
@@ -255,9 +250,15 @@ def tile_moe_seb_relu_kernel(
                     )
             nc.scalar.copy(dx_slots[:, :, e * C : (e + 1) * C], bank[:])
 
-        dx = [keep.tile([P, T], F32, name="dx0"), keep.tile([P, T], F32, name="dx1", tag="rounded0", align_bytes=64)]
-        for e in range(E):
-            for kt in range(K // P):
-                scatter(kt == 1, dx[kt], entries(list1, e * C, (e + 1) * C), dx_slots[:, kt, e * C : (e + 1) * C])
+        dx = [keep.tile([P, T], F32, name="dx%d" % kt) for kt in range(K // P)]
+
+        def scatter_dx(on_vector, kt, lo, hi):
+            scatter(on_vector, dx[kt], entries(list1, lo, hi), dx_slots[:, kt, lo:hi])
+
+        scatter_dx(False, 1, 0, SHARE)
+        scatter_dx(False, 0, 0, C)
+        scatter_dx(True, 1, SHARE, C)
+        for kt in range(K // P):
+            scatter_dx(kt == 1, kt, C, T)
         for kt in range(K // P):
             nc.sync.dma_start(out[kt * P : (kt + 1) * P, :], dx[kt][:])

@@ -216,7 +216,7 @@ def tile_moe_seb_relu_kernel(
 
         dx_slots = keep.tile([P, K // P, T], F32, name="dx_slots")
         for e in range(E):
-            bank = psum.tile([P, K // P, C], F32, name="acc1", tag="bank")
+            banks = [psum.tile([P, C], F32, name="acc1", tag="bank") for kt in range(K // P)]
             for half in range(C // P):
                 lo = half * P
                 da_bf = keep.tile([P, P, PACK], BF16, name="da_bf", tag="rounded%d" % half, align_bytes=64)
@@ -240,7 +240,7 @@ def tile_moe_seb_relu_kernel(
                 for kt in range(K // P):
                     cols = slice(kt * P, (kt + 1) * P)
                     nc.tensor.matmul_mx(
-                        out=bank[:, kt, lo : lo + P],
+                        out=banks[kt][:, lo : lo + P],
                         lhsT=w1_w[e][:, cols].bitcast(FP8X4),
                         lhsT_scale=w1_s[e][:, cols],
                         rhs=da_w[:].bitcast(FP8X4),
@@ -248,17 +248,20 @@ def tile_moe_seb_relu_kernel(
                         start=True,
                         stop=True,
                     )
-            nc.scalar.copy(dx_slots[:, :, e * C : (e + 1) * C], bank[:])
+            if e == 0:
+                for kt in range(K // P):
+                    nc.scalar.copy(dx_slots[:, kt, :C], banks[kt][:])
 
-        dx = [keep.tile([P, T], F32, name="dx%d" % kt) for kt in range(K // P)]
+        dx = [keep.tile([P, T], F32, name="dx0"), keep.tile([P, T], F32, name="dx1", tag="rounded0", align_bytes=64)]
 
         def scatter_dx(on_vector, kt, lo, hi):
             scatter(on_vector, dx[kt], entries(list1, lo, hi), dx_slots[:, kt, lo:hi])
 
-        scatter_dx(False, 1, 0, SHARE)
         scatter_dx(False, 0, 0, C)
-        scatter_dx(True, 1, SHARE, C)
-        for kt in range(K // P):
-            scatter_dx(kt == 1, kt, C, T)
+        scatter_dx(True, 1, 0, P)
+        nc.scalar.copy(dx_slots[:, 0, C:], banks[0][:])
+        nc.vector.tensor_copy(dx_slots[:, 1, C:], banks[1][:])
+        scatter_dx(False, 0, C, T)
+        scatter_dx(True, 1, P, T)
         for kt in range(K // P):
             nc.sync.dma_start(out[kt * P : (kt + 1) * P, :], dx[kt][:])

@@ -27,7 +27,8 @@ BLOCKS, RUN = H // 32, 8
 VECTOR_PLANE = 3
 LAST_PLANE = 2
 EARLY_PLANES = (3, 0, 1)
-SHARE = 64
+SHARE = 96
+STEP = 512
 
 
 def tile_moe_seb_relu_kernel(
@@ -43,6 +44,7 @@ def tile_moe_seb_relu_kernel(
 
     with ExitStack() as ctx:
         keep = ctx.enter_context(tc.tile_pool(name="keep", bufs=1))
+        ring = ctx.enter_context(tc.tile_pool(name="ring", bufs=1))
         psum = ctx.enter_context(tc.psum_pool(name="psum", bufs=8))
 
         list2 = keep.tile([P, T // LANES], U16, name="list2")
@@ -189,8 +191,8 @@ def tile_moe_seb_relu_kernel(
             scatter_dc(False, t, 1, 0, C)
         scatter_dc(False, LAST_PLANE, 1, 0, C - SHARE)
 
-        w1_bf = [keep.tile([P, K, PACK], BF16, name="w1_bf%d" % e, tag="rounded%d" % e, align_bytes=64) for e in range(E)]
-        w1_w = [keep.tile([P, K], U32, name="w1_w%d" % e, align_bytes=64) for e in range(E)]
+        w1_bf = [keep.tile([P, K, PACK], BF16, name="w1_bf%d" % e, align_bytes=64) for e in range(E)]
+        w1_w = [keep.tile([P, K], U32, name="w1_w0", align_bytes=64)]
         w1_s = [keep.tile([P, K], U8, name="w1_s%d" % e, align_bytes=64) for e in range(E)]
 
         def by_column(columns, run):
@@ -204,22 +206,34 @@ def tile_moe_seb_relu_kernel(
 
         for e in range(E):
             nc.gpsimd.tensor_scalar(w1_bf[e][:], w1_raw[e][:].rearrange("p t k -> p k t"), 1.0, 0.0, ALU.mult, ALU.add)
-            quantize(w1_w[e][:], w1_s[e][:], w1_bf[e][:])
+        quantize(w1_w[0][:], w1_s[0][:], w1_bf[0][:])
 
         slope = keep.tile([P, PACK, C], F32, name="slope")
         gate_rows = g1[:, C:].unsqueeze(1).to_broadcast([P, PACK, C])
         nc.vector.scalar_tensor_tensor(slope[:], a_sb[:, :, C:], 0.0, gate_rows, ALU.is_gt, ALU.mult)
-        for t in EARLY_PLANES + (LAST_PLANE,):
-            nc.vector.tensor_tensor(slots[0][:, place(t), :], dc[t][:].indirect(entries(list1, 0, C)), g1[:, :C], ALU.mult)
+
+        def gather_times_gate(t, lo, hi):
+            nc.vector.tensor_tensor(slots[0][:, place(t), lo:hi], dc[t][:].indirect(entries(list1, lo, hi)), g1[:, lo:hi], ALU.mult)
+
+        for t in EARLY_PLANES:
+            gather_times_gate(t, 0, C)
+        for lo in range(0, C, P):
+            gather_times_gate(LAST_PLANE, lo, lo + P)
         for t in (0, 1, VECTOR_PLANE, LAST_PLANE):
             nc.scalar.activation(slots[1][:, place(t), :], dc[t][:].indirect(entries(list1, C, T)), ACT.Copy)
 
         dx_slots = keep.tile([P, K // P, T], F32, name="dx_slots")
         for e in range(E):
             banks = [psum.tile([P, C], F32, name="acc1", tag="bank") for kt in range(K // P)]
+            if e == 1:
+                w1_w.append(ring.tile([P, K], U32, name="w1_w1", offset=0, align_bytes=64))
+                quantize(w1_w[1][:], w1_s[1][:], w1_bf[1][:])
             for half in range(C // P):
                 lo = half * P
-                da_bf = keep.tile([P, P, PACK], BF16, name="da_bf", tag="rounded%d" % half, align_bytes=64)
+                if half == 0:
+                    da_bf = ring.tile([P, P, PACK], BF16, name="da_bf%d" % e, offset=(1 + e) * STEP, align_bytes=64)
+                else:
+                    da_bf = keep.tile([P, P, PACK], BF16, name="da_bf", tag="rounded", align_bytes=64)
                 da_w = keep.tile([P, P], U32, name="da_w%d%d" % (e, half), align_bytes=64)
                 da_s = keep.tile([P, P], U8, name="da_s%d%d" % (e, half), align_bytes=64)
                 gathered = slots[e][:, :, lo : lo + P]
@@ -248,20 +262,16 @@ def tile_moe_seb_relu_kernel(
                         start=True,
                         stop=True,
                     )
-            if e == 0:
-                for kt in range(K // P):
-                    nc.scalar.copy(dx_slots[:, kt, :C], banks[kt][:])
+            for kt in range(K // P):
+                nc.scalar.copy(dx_slots[:, kt, e * C : (e + 1) * C], banks[kt][:])
 
-        dx = [keep.tile([P, T], F32, name="dx0"), keep.tile([P, T], F32, name="dx1", tag="rounded0", align_bytes=64)]
+        dx = [keep.tile([P, T], F32, name="dx0"), ring.tile([P, T], F32, name="dx1", offset=3 * STEP, align_bytes=64)]
 
         def scatter_dx(on_vector, kt, lo, hi):
             scatter(on_vector, dx[kt], entries(list1, lo, hi), dx_slots[:, kt, lo:hi])
 
-        scatter_dx(False, 0, 0, C)
-        scatter_dx(True, 1, 0, P)
-        nc.scalar.copy(dx_slots[:, 0, C:], banks[0][:])
-        nc.vector.tensor_copy(dx_slots[:, 1, C:], banks[1][:])
-        scatter_dx(False, 0, C, T)
-        scatter_dx(True, 1, P, T)
+        for e in range(E):
+            for kt in range(K // P):
+                scatter_dx(kt == 1, kt, e * C, (e + 1) * C)
         for kt in range(K // P):
             nc.sync.dma_start(out[kt * P : (kt + 1) * P, :], dx[kt][:])

@@ -272,6 +272,6 @@ def tile_moe_seb_relu_kernel(
 
         for e in range(E):
             for kt in range(K // P):
-                scatter_dx(kt == 1, kt, e * C, (e + 1) * C)
+                scatter_dx(kt != e, kt, e * C, (e + 1) * C)
         for kt in range(K // P):
             nc.sync.dma_start(out[kt * P : (kt + 1) * P, :], dx[kt][:])

@@ -54,7 +54,7 @@ def tile_moe_seb_relu_kernel(
         w2_w_raw = [keep.tile([P, PASSES, 2 * H], U8, name="w2_w_raw%d" % f, tag="w2_w_raw%d" % f, align_bytes=64) for f in range(E)]
         w2_s_raw = keep.tile([P, E * PASSES, H], U8, name="w2_s_raw", tag="w2_s_raw", align_bytes=64)
         q = [keep.tile([P, C], F32, name="q%d" % f, tag="q%d" % f, align_bytes=64) for f in range(E)]
-        q_first = keep.tile([P, P], F32, name="q_first", tag="first", align_bytes=64)
+        q_first = keep.tile([P, C], F32, name="q_first", tag="first", align_bytes=64)
         a_sb = keep.tile([P, PACK, T], F32, name="a_sb")
         g1 = keep.tile([P, T], F32, name="g1")
         w1_raw = [keep.tile([P, PACK, K], F32, name="w1_raw%d" % e) for e in range(E)]
@@ -82,7 +82,7 @@ def tile_moe_seb_relu_kernel(
                 w2t_scales[:, :, QUAD_ROWS * quad : QUAD_ROWS * (quad + 1), :].rearrange("f s b i -> b (f s) i").bitcast(I32),
             )
         nc.sync.dma_start(w2_w_raw[1][:].bitcast(I32), w2_rows[1])
-        nc.sync.dma_start(q_first[:], gate2[:, :P])
+        nc.sync.dma_start(q_first[:], gate2[:, :C])
         nc.sync.dma_start(q[0][:], gate2[:, :C])
         nc.sync.dma_start(q[1][:], gate2[:, C:])
 
@@ -169,8 +169,8 @@ def tile_moe_seb_relu_kernel(
         for s in range(PASSES):
             gather_words(1, s)
         gather_scales(1, 0)
-        second_layer(0, 0, 2, 0, P, q_first[:])
-        second_layer(0, 0, 2, P, C, q[0][:, P:])
+        second_layer(0, 0, 1, 0, C, q_first[:])
+        second_layer(0, 1, 2, 0, C, q[0][:])
         gather_scales(1, 1)
         for t in (VECTOR_PLANE, LAST_PLANE):
             second_layer(0, t, t + 1, 0, C, q[0][:])
@@ -180,10 +180,8 @@ def tile_moe_seb_relu_kernel(
         def scatter_dc(on_vector, t, f, lo, hi):
             scatter(on_vector, dc[t], entries(list2, f * C + lo, f * C + hi), slots[f][:, t, lo:hi])
 
-        for lo in range(0, C, P):
-            for t in range(2):
-                scatter_dc(False, t, 0, lo, lo + P)
-        scatter_dc(False, LAST_PLANE, 0, 0, C)
+        for t in range(VECTOR_PLANE):
+            scatter_dc(False, t, 0, 0, C)
         for f in range(E):
             scatter_dc(True, VECTOR_PLANE, f, 0, C)
         scatter_dc(True, LAST_PLANE, 1, C - SHARE, C)

from contextlib import ExitStack

import concourse.mybir as mybir

K, T, H, N = 256, 512, 512, 1024
E, C = 2, 256
FLOPS = 2 * T * (N * H + H * K)

F32 = mybir.dt.float32
BF16 = mybir.dt.bfloat16
I32 = mybir.dt.int32
U32 = mybir.dt.uint32
U16 = mybir.dt.uint16
U8 = mybir.dt.uint8
FP8X4 = mybir.dt.float8_e4m3fn_x4
FP4X4 = mybir.dt.float4_e2m1fn_x4
ALU = mybir.AluOpType
ACT = mybir.ActivationFunctionType

P = 128
PACK = 4
PASSES = N // (P * PACK)
LANES = 16
QUAD, QUAD_ROWS = 32, 4
QUAD_ORDER = (0, 2, 1, 3)
BLOCKS, RUN = H // 32, 8
VECTOR_PLANE = 3
LAST_PLANE = 2
EARLY_PLANES = (3, 0, 1)
SHARE = 96
STEP = 512


def tile_moe_seb_relu_kernel(
    tc, dy_words, dy_scales, w2t_words, w2t_scales, w1t, a, gate1, gate2, offs, offs2, out
):
    nc = tc.nc

    def entries(list_tile, lo, hi):
        return list_tile[:, lo // LANES : hi // LANES]

    def place(t):
        return (t + 1) % PACK

    with ExitStack() as ctx:
        keep = ctx.enter_context(tc.tile_pool(name="keep", bufs=1))
        ring = ctx.enter_context(tc.tile_pool(name="ring", bufs=1))
        psum = ctx.enter_context(tc.psum_pool(name="psum", bufs=8))

        list2 = keep.tile([P, T // LANES], U16, name="list2")
        list1 = keep.tile([P, T // LANES], U16, name="list1")
        dy_w = keep.tile([P, PASSES, T], I32, name="dy_w", align_bytes=64)
        dy_s = keep.tile([P, PASSES, T], U8, name="dy_s", align_bytes=64)
        w2_w_raw = [keep.tile([P, PASSES, 2 * H], U8, name="w2_w_raw%d" % f, tag="w2_w_raw%d" % f, align_bytes=64) for f in range(E)]
        w2_s_raw = keep.tile([P, E * PASSES, H], U8, name="w2_s_raw", tag="w2_s_raw", align_bytes=64)
        q = [keep.tile([P, C], F32, name="q%d" % f, tag="q%d" % f, align_bytes=64) for f in range(E)]
        q_first = keep.tile([P, C], F32, name="q_first", tag="first", align_bytes=64)
        a_sb = keep.tile([P, PACK, T], F32, name="a_sb")
        g1 = keep.tile([P, T], F32, name="g1")
        w1_raw = [keep.tile([P, PACK, K], F32, name="w1_raw%d" % e) for e in range(E)]

        nc.gpsimd.memset(dy_s[:].bitcast(I32), 0)
        w2_s_words = w2_s_raw[:].rearrange("p a i -> p (a i)").bitcast(I32)
        odd = w2_s_words.shape[1] // 2 + 1
        nc.vector.memset(w2_s_words[:, :odd], 0)
        nc.vector.memset(w2_s_words[:, odd:], 0)

        dy_rows = dy_words.rearrange("s p t d -> p s (t d)").bitcast(I32)
        nc.sync.dma_start(dy_w[:, 0, :], dy_rows[:, 0, :])
        nc.sync.dma_start(list2[:], offs2)
        for quad in QUAD_ORDER:
            nc.sync.dma_start(
                dy_s[QUAD * quad : QUAD * quad + QUAD_ROWS, :, :].bitcast(I32),
                dy_scales[:, QUAD_ROWS * quad : QUAD_ROWS * (quad + 1), :].rearrange("s b t -> b s t").bitcast(I32),
            )
        nc.sync.dma_start(dy_w[:, 1, :], dy_rows[:, 1, :])
        w2_rows = w2t_words.rearrange("f s p n -> f p s n").bitcast(I32)
        nc.sync.dma_start(w2_w_raw[0][:].bitcast(I32), w2_rows[0])
        for quad in QUAD_ORDER:
            nc.sync.dma_start(
                w2_s_raw[QUAD * quad : QUAD * quad + QUAD_ROWS, :, :].bitcast(I32),
                w2t_scales[:, :, QUAD_ROWS * quad : QUAD_ROWS * (quad + 1), :].rearrange("f s b i -> b (f s) i").bitcast(I32),
            )
        nc.sync.dma_start(w2_w_raw[1][:].bitcast(I32), w2_rows[1])
        nc.sync.dma_start(q_first[:], gate2[:, :C])
        nc.sync.dma_start(q[0][:], gate2[:, :C])
        nc.sync.dma_start(q[1][:], gate2[:, C:])

        def load_planes(planes, rows):
            by_plane = rows.rearrange("(b t u) c -> t b u c", t=PACK, u=RUN)
            for t in range(PACK):
                nc.sync.dma_start(planes[:, place(t), :], by_plane[t])

        for e in range(E):
            load_planes(w1_raw[e], w1t[e])
        nc.sync.dma_start(g1[:], gate1)
        load_planes(a_sb, a)
        nc.sync.dma_start(list1[:], offs)

        w2_w = [keep.tile([P, PASSES, PACK, 2 * P], U8, name="w2_w%d" % f, align_bytes=64) for f in range(E)]
        w2_s = [keep.tile([P, PASSES, PACK, P], U8, name="w2_s%d" % f, align_bytes=64) for f in range(E)]

        def sort_by_plane(planes, raw, t0, t1):
            nc.scalar.copy(
                planes.bitcast(U32).rearrange("p s t (b w) -> p s t b w", b=BLOCKS)[:, :, t0:t1, :, :],
                raw.bitcast(U32).rearrange("p s (b t w) -> p s t b w", b=BLOCKS, t=PACK)[:, :, t0:t1, :, :],
            )

        for f in range(E):
            passes = slice(PASSES * f, PASSES * (f + 1))
            sort_by_plane(w2_w[f][:], w2_w_raw[f][:], 0, PACK)
            for t0, t1 in ((0, 2), (2, PACK)) if f == 0 else ((0, PACK),):
                sort_by_plane(w2_s[f][:], w2_s_raw[:, passes, :], t0, t1)

        slot_w = [
            [keep.tile([P, C], U32, name="slot_w0%d" % s, align_bytes=64) for s in range(PASSES)],
            [
                keep.tile([P, C], U32, name="slot_w10", tag="w2_w_raw0", align_bytes=64),
                keep.tile([P, C], U32, name="slot_w11", align_bytes=64),
            ],
        ]
        slot_s = [
            [keep.tile([P, C], U8, name="slot_s0%d" % s, align_bytes=64) for s in range(PASSES)],
            [
                keep.tile([P, C], U8, name="slot_s10", tag="w2_s_raw", align_bytes=64),
                keep.tile([P, C], U8, name="slot_s11", tag="first", align_bytes=64),
            ],
        ]
        dc = [keep.tile([P, T], F32, name="dc%d" % t, align_bytes=64) for t in range(PACK)]
        slots = [keep.tile([P, PACK, C], F32, name="slots%d" % f, align_bytes=64) for f in range(E)]

        def gather_words(f, s):
            nc.vector.tensor_copy(slot_w[f][s][:], dy_w[:, s, :].bitcast(U32).indirect(entries(list2, f * C, (f + 1) * C)))

        def gather_scales(f, s):
            nc.vector.tensor_copy(slot_s[f][s][:], dy_s[:, s, :].indirect(entries(list2, f * C, (f + 1) * C)))

        def second_layer(f, t0, t1, lo, hi, gate, step=1):
            planes = range(t0, t1, step)
            acc = psum.tile([P, len(planes), hi - lo], F32, name="acc", tag="bank")
            for j, t in enumerate(planes):
                for s in range(PASSES):
                    nc.tensor.matmul_mx(
                        out=acc[:, j, :],
                        lhsT=w2_w[f][:, s, t, :].bitcast(FP4X4),
                        lhsT_scale=w2_s[f][:, s, t, :],
                        rhs=slot_w[f][s][:, lo:hi].bitcast(FP8X4),
                        rhs_scale=slot_s[f][s][:, lo:hi],
                        start=(s == 0),
                        stop=(s == PASSES - 1),
                    )
            nc.vector.tensor_tensor(
                slots[f][:, t0:t1:step, lo:hi],
                acc[:],
                gate.unsqueeze(1).to_broadcast([P, len(planes), hi - lo]),
                ALU.mult,
            )

        def scatter(on_vector, window, offsets, values):
            if on_vector:
                nc.vector.tensor_copy(window[:].indirect(offsets), values)
            else:
                nc.scalar.activation(window[:].indirect(offsets), values, ACT.Copy)

        for s in range(PASSES):
            gather_words(0, s)
        for s in range(PASSES):
            gather_scales(0, s)
        for s in range(PASSES):
            gather_words(1, s)
        gather_scales(1, 0)
        second_layer(0, 0, 1, 0, C, q_first[:])
        second_layer(0, 1, 2, 0, C, q[0][:])
        gather_scales(1, 1)
        for t in (VECTOR_PLANE, LAST_PLANE):
            second_layer(0, t, t + 1, 0, C, q[0][:])
        for t0, t1, step in ((0, PACK, VECTOR_PLANE), (1, VECTOR_PLANE, 1)):
            second_layer(1, t0, t1, 0, C, q[1][:], step)

        def scatter_dc(on_vector, t, f, lo, hi):
            scatter(on_vector, dc[t], entries(list2, f * C + lo, f * C + hi), slots[f][:, t, lo:hi])

        for t in range(VECTOR_PLANE):
            scatter_dc(False, t, 0, 0, C)
        for f in range(E):
            scatter_dc(True, VECTOR_PLANE, f, 0, C)
        scatter_dc(True, LAST_PLANE, 1, C - SHARE, C)
        for t in range(LAST_PLANE):
            scatter_dc(False, t, 1, 0, C)
        scatter_dc(False, LAST_PLANE, 1, 0, C - SHARE)

        w1_bf = [keep.tile([P, K, PACK], BF16, name="w1_bf%d" % e, align_bytes=64) for e in range(E)]
        w1_w = [keep.tile([P, K], U32, name="w1_w0", align_bytes=64)]
        w1_s = [keep.tile([P, K], U8, name="w1_s%d" % e, align_bytes=64) for e in range(E)]

        def by_column(columns, run):
            return columns.rearrange("p (c i) t -> p c t i", i=run)

        def by_plane(planes, run):
            return planes.rearrange("p t (c i) -> p c t i", i=run)

        def quantize(words, scales, columns):
            nc.vector.quantize_mx(out=words.bitcast(FP8X4), scales=scales, in_=columns.rearrange("p c t -> p (c t)"))

        for e in range(E):
            nc.gpsimd.tensor_scalar(w1_bf[e][:], w1_raw[e][:].rearrange("p t k -> p k t"), 1.0, 0.0, ALU.mult, ALU.add)
        quantize(w1_w[0][:], w1_s[0][:], w1_bf[0][:])

        slope = keep.tile([P, PACK, C], F32, name="slope")
        gate_rows = g1[:, C:].unsqueeze(1).to_broadcast([P, PACK, C])
        nc.vector.scalar_tensor_tensor(slope[:], a_sb[:, :, C:], 0.0, gate_rows, ALU.is_gt, ALU.mult)

        def gather_times_gate(t, lo, hi):
            nc.vector.tensor_tensor(slots[0][:, place(t), lo:hi], dc[t][:].indirect(entries(list1, lo, hi)), g1[:, lo:hi], ALU.mult)

        for t in EARLY_PLANES:
            gather_times_gate(t, 0, C)
        for lo in range(0, C, P):
            gather_times_gate(LAST_PLANE, lo, lo + P)
        for t in (0, 1, VECTOR_PLANE, LAST_PLANE):
            nc.scalar.activation(slots[1][:, place(t), :], dc[t][:].indirect(entries(list1, C, T)), ACT.Copy)

        dx_slots = keep.tile([P, K // P, T], F32, name="dx_slots")
        for e in range(E):
            banks = [psum.tile([P, C], F32, name="acc1", tag="bank") for kt in range(K // P)]
            if e == 1:
                w1_w.append(ring.tile([P, K], U32, name="w1_w1", offset=0, align_bytes=64))
                quantize(w1_w[1][:], w1_s[1][:], w1_bf[1][:])
            for half in range(C // P):
                lo = half * P
                if half == 0:
                    da_bf = ring.tile([P, P, PACK], BF16, name="da_bf%d" % e, offset=(1 + e) * STEP, align_bytes=64)
                else:
                    da_bf = keep.tile([P, P, PACK], BF16, name="da_bf", tag="rounded", align_bytes=64)
                da_w = keep.tile([P, P], U32, name="da_w%d%d" % (e, half), align_bytes=64)
                da_s = keep.tile([P, P], U8, name="da_s%d%d" % (e, half), align_bytes=64)
                gathered = slots[e][:, :, lo : lo + P]
                if e == 0:
                    nc.vector.scalar_tensor_tensor(
                        da_bf[:],
                        a_sb[:, :, lo : lo + P].rearrange("p t c -> p c t"),
                        0.0,
                        gathered.rearrange("p t c -> p c t"),
                        ALU.is_gt,
                        ALU.mult,
                    )
                else:
                    nc.vector.tensor_tensor(
                        by_column(da_bf[:], 2), by_plane(gathered, 2), by_plane(slope[:, :, lo : lo + P], 2), ALU.mult
                    )
                quantize(da_w[:], da_s[:], da_bf[:])
                for kt in range(K // P):
                    cols = slice(kt * P, (kt + 1) * P)
                    nc.tensor.matmul_mx(
                        out=banks[kt][:, lo : lo + P],
                        lhsT=w1_w[e][:, cols].bitcast(FP8X4),
                        lhsT_scale=w1_s[e][:, cols],
                        rhs=da_w[:].bitcast(FP8X4),
                        rhs_scale=da_s[:],
                        start=True,
                        stop=True,
                    )
            for kt in range(K // P):
                nc.scalar.copy(dx_slots[:, kt, e * C : (e + 1) * C], banks[kt][:])

        dx = [keep.tile([P, T], F32, name="dx0"), ring.tile([P, T], F32, name="dx1", offset=3 * STEP, align_bytes=64)]

        def scatter_dx(on_vector, kt, lo, hi):
            scatter(on_vector, dx[kt], entries(list1, lo, hi), dx_slots[:, kt, lo:hi])

        for e in range(E):
            for kt in range(K // P):
                scatter_dx(kt != e, kt, e * C, (e + 1) * C)
        for kt in range(K // P):
            nc.sync.dma_start(out[kt * P : (kt + 1) * P, :], dx[kt][:])
